import numpy as np, ml_dtypes
CORES = [48,51,52,55]
N = 4
BF = ml_dtypes.bfloat16
def gentries(a):
    return np.ascontiguousarray(a.reshape(8, 16, -1).transpose(0, 2, 1)).reshape(8, -1)
def gtable(e):
    e = np.asarray(e); return np.ascontiguousarray(e.reshape(8, -1, 16).transpose(0, 2, 1)).reshape(128, -1).astype(np.int32)
V, D, B, C = 2048, 4, 256, 512
NONE = 1 << 24
def ring(n, s, order, step):
    n[order, s] = np.roll(order, -step); n[order, s + 1] = np.roll(order, step)
def mesh(rng, pairs):
    n = np.zeros((N * V, D), np.int64); h = D // 2 - 1
    if pairs:
        q = rng.permutation(N)
        circles = [np.stack([q[i] * V + rng.permutation(B), q[i + 1] * V + rng.permutation(B)], 1).reshape(-1) for i in range(0, N, 2)]
    else:
        circles = [rng.permutation((np.arange(N)[:, None] * V + np.arange(B)).reshape(-1))]
    for o in circles:
        for i in range(h): ring(n, 2 * i, o, 2 * i + 1)
    for r in range(N):
        a = r * V + rng.permutation(B); m = r * V + B + rng.permutation(B); p = r * V + C + rng.permutation(V - C)
        ring(n, 2 * h, np.stack([a, m], 1).reshape(-1), 1)
        at = np.zeros(V - B, bool); at[rng.permutation(V - B)[:B]] = True
        o = np.zeros(V - B, np.int64); o[at] = rng.permutation(m); o[~at] = p
        for i in range(h): ring(n, 2 * i, o, i + 1)
        ring(n, 2 * h, p, h + 1)
    return rng.permuted(n, axis=1)
def planes(rng, *shape):
    p = rng.integers(np.array([-3, -3, -3, -10]), np.array([4, 4, 4, 11]), shape + (3, 4))
    return np.matmul(p.swapaxes(-1, -2), p)
def parts(rng, pairs=False):
    return planes(rng, N, 8, V), rng.integers(-15, 16, (N, 8, V, 3)), np.stack([mesh(rng, pairs) for g in range(8)])
def pack(q, c, n):
    h = np.concatenate([c, np.ones(c.shape[:-1] + (1,), c.dtype)], -1); p = h[..., :, None] * h[..., None, :]
    e = n.reshape(8, N, V, D).transpose(1, 0, 3, 2).reshape(N, 8, D * V)
    return {"qu": np.ascontiguousarray(q.transpose(0, 1, 3, 4, 2)).reshape(N, 128, V).astype(np.float32),
            "po": np.ascontiguousarray(p.transpose(0, 1, 3, 4, 2)).reshape(N, 128, V).astype(np.float32).astype(BF),
            "nb": np.stack([gtable(e[r]) for r in range(N)])}
def setup_inputs(rng):
    return pack(*parts(rng))
def setup_inputs_ties(rng):
    n = parts(rng)[2]; G = np.arange(8)[None, :, None]
    a = planes(rng, 8, 2) + np.array([1, 2])[:, None, None] * np.eye(4, dtype=np.int64); b = rng.integers(-15, 16, (8, 2, 3))
    return pack(a[G, rng.integers(0, 2, (N, 8, V))], b[G, rng.integers(0, 2, (N, 8, V))], n)
def setup_inputs_stars(rng):
    q, c, n = parts(rng); c[..., 0] = np.minimum(c[..., 0], 14)
    for g in range(8):
        m = n[g]; v = rng.permutation((np.arange(N)[:, None] * V + np.arange(B)).reshape(-1)); k = m[v]
        meet = (m[k][:, :, :, None] == k[:, None, None, :]).any((1, 2, 3)); used = np.zeros(N * V, bool); done = 0
        for w in v[~meet]:
            leaf = m[w]; near = np.concatenate([leaf, m[leaf].reshape(-1)])
            if used[near].any(): continue
            used[near] = True; done += 1
            for u in np.append(leaf, w):
                q[u // V, g, u % V] = 0; q[u // V, g, u % V, 0, 3] = q[u // V, g, u % V, 3, 0] = -499; c[u // V, g, u % V, 0] = 15 if u == w else -15
            if done == 4: break
        assert done == 4
    return pack(q, c, n)
def setup_inputs_pairs(rng):
    return pack(*parts(rng, True))
def setup_inputs_heavy(rng):
    n = np.stack([mesh(rng, False) for g in range(8)]); G = np.arange(8)[None, :, None]
    x = rng.integers(0, 9, (N, 8, V, 4, 4)); k = np.tril(x) + np.tril(x, -1).swapaxes(-1, -2)
    s = np.where(G < 4, -1, np.where(G < 6, 1, 1 - 2 * rng.integers(0, 2, (N, 8, V))))
    d = pack(s[..., None, None] * (500 - k), rng.integers(12, 16, (N, 8, V, 3)), n)
    n_all = lists_of(d["nb"]); q_all = whole_meshes(d["qu"]); p_all = whole_meshes(d["po"]); own = np.arange(N * V); large = 0
    for g in range(4):
        m1 = collapse(costs(q_all[g], p_all[g], n_all[g]), n_all[g]); q1 = q_all[g].copy()
        for i in range(D): q1 += np.where(m1[n_all[g, i]] == own, q_all[g][:, n_all[g, i]], 0)
        n2 = m1[n_all[g]]; c2 = np.where(n2 == own, NONE, costs(q1, p_all[g], n2)); m2 = collapse(c2, n2)
        large += np.count_nonzero((m1 == own) & (m2 != own) & (np.min(c2, axis=0) < -(1 << 22)))
    assert large > 0
    return d
def setup_inputs_spread(rng):
    q, c, n = parts(rng); a = (500 >> rng.integers(0, 9, (N, 8, V)))[..., None, None]
    x = rng.integers(-a, a + 1, (N, 8, V, 4, 4)); x = np.where(rng.random((N, 8, V, 1, 1)) < 0.0625, 500 - 1000 * rng.integers(0, 2, x.shape), x)
    q = np.tril(x) + np.tril(x, -1).swapaxes(-1, -2); k = rng.integers(0, 8, c.shape)
    c = np.where(k == 0, 0, np.where(k == 1, 15, np.where(k == 2, -15, c)))
    return pack(q, c, n)
def lists_of(nb):
    return np.stack([gentries(nb[r]).reshape(8, D, V) for r in range(N)], axis=2).reshape(8, D, N * V).astype(np.int64)
def whole_meshes(x):
    return x.astype(np.float64).reshape(N, 8, 16, V).transpose(1, 2, 0, 3).reshape(8, 16, N * V).astype(np.int64)
def check_inputs(d):
    bad = []; q = d["qu"].astype(np.float64).reshape(N, 8, 4, 4, V); p = d["po"].astype(np.float64).reshape(N, 8, 4, 4, V); h = p[:, :, :, 3]
    if not np.isfinite(q).all() or (q != np.rint(q)).any() or (np.abs(q) > 500).any(): bad.append("quadrics: whole numbers of size at most 500")
    if (q != q.transpose(0, 1, 3, 2, 4)).any(): bad.append("quadrics: symmetric")
    if not np.isfinite(p).all() or (h != np.rint(h)).any() or (np.abs(h) > 15).any() or (h[:, :, 3] != 1).any() or (p != h[:, :, :, None] * h[:, :, None]).any(): bad.append("points: products of whole coordinates of size at most 15 and 1")
    n = lists_of(d["nb"]).transpose(0, 2, 1); own = np.arange(N * V)[None, :, None]
    if (n < 0).any() or (n >= N * V).any(): return bad + ["neighbours: in range"]
    s = np.sort(n, axis=2)
    if (n == own).any() or (s[:, :, 1:] == s[:, :, :-1]).any(): bad.append("neighbours: different, not the vertex itself")
    if (np.sort((own * (N * V) + n).reshape(8, -1), axis=1) != np.sort((n * (N * V) + own).reshape(8, -1), axis=1)).any(): bad.append("neighbours: symmetric")
    if ((own // V != n // V) & ((own % V >= B) | (n % V >= B))).any(): bad.append("edges between ranks: columns under B")
    if ((own % V < B) & (n % V >= C)).any(): bad.append("neighbours of columns under B: columns under C")
    return bad
def costs(q, p, n):
    return np.stack([np.sum((q + q[:, n[s]]) * p[:, n[s]], axis=0) for s in range(D)])
def collapse(cost, n):
    own = np.arange(N * V); s = np.argmin(cost, axis=0)
    best = cost[s, own]; first = (best < best[n]) | ((best == best[n]) & (own < n)) | (n == own)
    return np.where(np.all(first, axis=0) & (best < NONE), n[s, own], own)
def reference(qu, po, nb):
    n_all = lists_of(nb); q_all = whole_meshes(qu); p_all = whole_meshes(po); own = np.arange(N * V)
    q1 = q_all.copy(); goal = np.zeros((8, N * V), np.int64)
    for g in range(8):
        n = n_all[g]; q = q_all[g]; p = p_all[g]
        m1 = collapse(costs(q, p, n), n)
        for s in range(D): q1[g] += np.where(m1[n[s]] == own, q[:, n[s]], 0)
        n2 = m1[n]
        m2 = collapse(np.where(n2 == own, NONE, costs(q1[g], p, n2)), n2)
        goal[g] = m2[m1]
    q1 = np.ascontiguousarray(q1.reshape(8, 16, N, V).transpose(2, 0, 1, 3)).reshape(N, 128, V)
    goal = np.ascontiguousarray(goal.reshape(8, N, V).transpose(1, 0, 2))
    return {"q1": q1.astype(np.float32), "goal": goal.astype(np.float32)}

@@ -1,0 +1,696 @@
+from concourse.bass import DstId, RemoteDMATransfer
+from concourse.mybir import AluOpType as A, ActivationFunctionType as F
+
+N, V, NB, NC = 4, 2048, 256, 512
+C0, CW, GB = [0, 256, 512, 1024], [256, 256, 512, 1024], [0, 1024, 2048, 4096]
+HALO1, HALO2 = V + 3 * NB, 16 + V + 3 * NC
+BIG = 65536.0
+NONE = float(1 << 24)
+
+SCRATCH = {}
+for _n, _w, _t in (
+        ("Qw", 16 + HALO1, "float32"), ("Pb", V, "bfloat16"), ("nbi", 512, "int32"), ("W", HALO1, "bfloat16"),
+        ("W1", HALO2, "bfloat16"), ("Bw", HALO1, "bfloat16"), ("Mw", HALO1, "bfloat16"), ("B2w", HALO2, "bfloat16"),
+        ("M2w", HALO1, "bfloat16"), ("L1", 512, "uint16"), ("LQ", 512, "uint16"), ("L2", 512, "uint16"), ("LG", 128, "uint16"),
+        ("posq", 512, "float32"), ("VT", 512, "float32"), ("EQ", 512, "float32"), ("NF", 128, "float32"), ("mA", 128, "float32"),
+        ("mB", 384, "float32"), ("GA", 8192, "bfloat16"), ("GB", 8192, "bfloat16"), ("GH", 8192, "float16"),
+        ("PR", 8192, "float32"), ("PRS", V, "float32"), ("C1f", V, "float32"), ("DS", V, "bfloat16"), ("DB", V, "bfloat16"),
+        ("DM", V, "bfloat16"), ("TB", V, "bfloat16"), ("ON", 512, "bfloat16"), ("Id", 128, "bfloat16"), ("PM", 128, "bfloat16"),
+        ("PMh", 128, "float16"), ("PMf", 128, "float32"), ("PI", 128, "bfloat16"), ("E8", 8, "bfloat16"), ("wC", 8, "float32"),
+        ("wS", 8, "float32"), ("wK", 32, "bfloat16"), ("wKf", 32, "float32"), ("ci", 8, "int32"), ("cf", 32, "float32"),
+        ("VC", 128, "float32"), ("VK1", 512, "float32"), ("VK2", 512, "float32"), ("t1", 256, "float32"), ("t2", 256, "float32"),
+        ("best", 128, "float32"), ("rem", 128, "float32"), ("E", 512, "float32"), ("X", 512, "float32"), ("X2", 256, "float32"),
+        ("XI", 128, "int32"), ("CI", 128, "int32"), ("DD", 128, "float32"), ("Dh", 128, "bfloat16"), ("Dl", 128, "float32"),
+        ("LT", 512, "float32"), ("tt", 512, "float32"), ("tm", 256, "float32"), ("tn", 128, "float32"), ("cl", 128, "float32"),
+        ("GO", 128, "float32")):
+    SCRATCH[_n] = ("sbuf", [128, _w], _t)
+for _i in range(8):
+    SCRATCH["b%d" % _i] = ("psum", [128, 512], "float32")
+EX = ["xQ", "xW", "xB", "xM", "xW1", "xB2", "xM2"]
+SEMAPHORES = ["v", "s", "p", "g", "rl", "dq1", "dgo"] + ["d%d" % i for i in range(9)] + EX
+
+
+def make(g, T):
+    QO = {"v": g.vector, "s": g.scalar, "p": g.tensor, "y": g.sync, "g": g}
+    cnt = {"v": 0, "s": 0, "p": 0, "g": 0}
+    known = {q: {} for q in QO}
+    clk, acc = {}, {}
+
+    def waits(q, toks):
+        k = known[q]
+        todo = {}
+        for ch, n in toks:
+            if k.get(ch, 0) < n:
+                todo[ch] = max(n, todo.get(ch, 0))
+        items = sorted(todo.items())
+        for ch, n in items:
+            if any(c2 != ch and clk[(c2, n2)].get(ch, 0) >= n for c2, n2 in items):
+                continue
+            QO[q].wait_ge(T.sem[ch], n)
+            k[ch] = max(n, k.get(ch, 0))
+            for c3, n3 in clk[(ch, n)].items():
+                k[c3] = max(n3, k.get(c3, 0))
+
+    def is_bank(key):
+        return len(key) == 2 and key[0] == "b" and key[1].isdigit()
+
+    def deps(q, r, w, isdma):
+        toks = set()
+        for lst, wr in ((r, False), (w, True)):
+            for key, lo, hi in lst:
+                bank = is_bank(key)
+                for lo2, hi2, tok, q2, w2 in acc.get(key, []):
+                    same = q2 == q and not isdma
+                    if same and q == "p":
+                        continue
+                    if bank and not same:
+                        toks.add(tok)
+                        continue
+                    if lo2 >= hi or lo >= hi2:
+                        continue
+                    if w2 or (wr and not same):
+                        toks.add(tok)
+        return toks
+
+    def record(q, r, w, tok):
+        for key, lo, hi in w:
+            bank = is_bank(key)
+            acc[key] = [a for a in acc.get(key, []) if not ((lo <= a[0] and a[1] <= hi) or (bank and a[3] != q))]
+            acc[key].append((lo, hi, tok, q, True))
+        for key, lo, hi in r:
+            bank = is_bank(key)
+            acc[key] = [a for a in acc.get(key, [])
+                        if not ((not a[4] and a[3] == q and q in cnt and lo <= a[0] and a[1] <= hi) or (bank and a[3] != q))]
+            acc[key].append((lo, hi, tok, q, False))
+
+    def op(q, fn, r, w):
+        waits(q, deps(q, r, w, False))
+        cnt[q] += 1
+        fn(QO[q]).then_inc(T.sem[q], 1)
+        tok = (q, cnt[q])
+        c = dict(known[q])
+        c[q] = cnt[q]
+        clk[tok] = c
+        record(q, r, w, tok)
+
+    def dma(q, out, in_, r, w, sem, total=16):
+        waits(q, deps(q, r, w, True))
+        QO[q].dma_start(out, in_).then_inc(T.sem[sem], 16)
+        tok = (sem, total)
+        c = dict(known[q])
+        c[sem] = total
+        clk[tok] = c
+        record("d", r, w, tok)
+
+    def arrives(sem, total, w):
+        tok = (sem, total)
+        clk[tok] = {sem: total}
+        record("d", [], w, tok)
+
+    def reads(q, r):
+        waits(q, deps(q, r, [], True))
+
+    def finish(q, toks):
+        for ch in ("v", "s", "p", "g"):
+            if cnt[ch]:
+                toks.append((ch, cnt[ch]))
+        for ch, n in toks:
+            if known[q].get(ch, 0) < n or ch not in cnt:
+                QO[q].wait_ge(T.sem[ch], n)
+                known[q][ch] = n
+
+    return op, dma, arrives, reads, finish
+
+
+def run(*gens):
+    gens = list(gens)
+    while gens:
+        left = []
+        for x in gens:
+            try:
+                next(x)
+                left.append(x)
+            except StopIteration:
+                pass
+        gens = left
+
+
+def rank_program(g, core, T, topo):
+    rank = T.rank_of(core)
+    if rank is None:
+        return
+    op, dma, arrives, reads, finish = make(g, T)
+    own = V * rank
+    others = [c for c in T.cores if c != core]
+    R = range(4)
+
+    def ap(b, lo, hi):
+        return T[b][:, lo:hi]
+
+    def tt(o, a, b, f):
+        op("v", lambda e: e.tensor_tensor(ap(*o), ap(*a), ap(*b), f), [a, b], [o])
+
+    def ts(o, a, s1, s2, f1, f2=None):
+        rd = [a] + [x for x in (s1, s2) if isinstance(x, tuple)]
+        x1 = ap(*s1) if isinstance(s1, tuple) else s1
+        x2 = ap(*s2) if isinstance(s2, tuple) else s2
+        if f2 is None:
+            op("v", lambda e: e.tensor_scalar(ap(*o), ap(*a), x1, x2, f1), rd, [o])
+        else:
+            op("v", lambda e: e.tensor_scalar(ap(*o), ap(*a), x1, x2, f1, f2), rd, [o])
+
+    def cp(q, o, a):
+        if q == "v":
+            op("v", lambda e: e.tensor_copy(ap(*o), ap(*a)), [a], [o])
+        else:
+            op("s", lambda e: e.activation(ap(*o), ap(*a), F.Copy), [a], [o])
+
+    def scaled(o, a, col, bias=None):
+        rd = [a, col] + ([bias] if bias else [])
+        if bias:
+            op("s", lambda e: e.activation(ap(*o), ap(*a), F.Identity, bias=ap(*bias), scale=ap(*col)), rd, [o])
+        else:
+            op("s", lambda e: e.activation(ap(*o), ap(*a), F.Identity, scale=ap(*col)), rd, [o])
+
+    def dcol(d, k, b0, b1):
+        return (d + "#%d" % k, 128 * b0, 128 * b1), T[d][:, 128 * b0 + k:128 * b1:16]
+
+    def mm(o, lt, rh, start, stop, r):
+        op("p", lambda e: e.matmul(ap(*o), lt, rh, start, stop), r, [o])
+
+    def fill(b, lo, hi, x):
+        op("v", lambda e: e.memset(ap(b, lo, hi), x), [], [(b, lo, hi)])
+
+    for i in R:
+        a = 512 * i
+        dma("y", T.Qw[:, 16 + a:16 + a + 512], T.qu[:, a:a + 512], [], [("Qw", 16 + a, 16 + a + 512)], "d%d" % i)
+        dma("s", T.Pb[:, a:a + 512], T.po[:, a:a + 512], [], [("Pb", a, a + 512)], "d%d" % (4 + i))
+        if i == 0:
+            dma("s", T.nbi[:], T.nb[:], [], [("nbi", 0, 512)], "d8")
+
+    msk = topo.mask(core, others[0])
+    for c in others[1:]:
+        msk &= topo.mask(core, c)
+    ne = bin(msk).count("1")
+    sent = [0]
+    arrives("xQ", 3 * ne, [("Qw", 16 + V, 16 + HALO1)])
+    for b, x in (("W", "xW"), ("Bw", "xB"), ("Mw", "xM"), ("M2w", "xM2")):
+        arrives(x, 3 * ne, [(b, V, HALO1)])
+    for b, x in (("W1", "xW1"), ("B2w", "xB2")):
+        arrives(x, 3 * ne, [(b, 16 + V, HALO2)])
+
+    def share(b, sem, lo, w, base):
+        reads("g", [(b, lo, lo + w)])
+        ids, dst = [], []
+        for c in others:
+            q = T.rank_of(c)
+            at = base + w * (rank if rank < q else rank - 1)
+            rid, pid = topo.addr(c)[0], topo.addr(c)[1]
+            ids.append(DstId(rid=rid, pnc=pid))
+            dst.append(T[b][:, at:at + w])
+        g.remote_dma_fused([RemoteDMATransfer(dst_ids=ids, dma_engine_mask=msk, remote_sem=T.sem[sem],
+                                              srcs=[T[b][:, lo:lo + w]], dsts=dst)], local_sem=T.sem.rl)
+        sent[0] += ne
+
+    def g_sel(o, i, pat, c, base, cm):
+        op("g", lambda e: e.affine_select(ap(*o), ap(*i), pat, c, 0.0, base, cm), [i], [o])
+
+    def g_iota(o, pat, base, cm, fl=True, w=None):
+        if fl:
+            op("g", lambda e: e.iota(ap(*o), pat, base, cm, allow_small_or_imprecise_dtypes=True), [], w or [o])
+        else:
+            op("g", lambda e: e.iota(ap(*o), pat, base, cm), [], [o])
+
+    def classes(d):
+        return [(d + "#%d" % k, 0, V) for k in range(16)]
+
+    def ci(k):
+        return ("ci", k, k + 1)
+
+    def cf(k):
+        return ("cf", k, k + 1)
+
+    fill("ON", 0, 512, 1.0)
+    fill("Qw", 0, 16, 0.0)
+    g_iota(ci(0), [[0, 1]], 0, 1, False)
+    g_sel(("Id", 0, 128), ("ON", 0, 128), [[-1, 128]], A.is_equal, 0, 1)
+    g_sel(("E8", 0, 8), ("ON", 0, 8), [[-16, 8]], A.is_ge, 0, 1)
+    g_sel(("E8", 0, 8), ("E8", 0, 8), [[16, 8]], A.is_ge, 15, -1)
+    g_iota(("VC", 0, 128), [[128, 16], [0, 8]], own, 1)
+    for x in range(4):
+        n = CW[x] // 16
+        g_iota(("VT", GB[x] // 16, GB[x] // 16 + 4 * n), [[0, 4], [16, n]], own + C0[x], 0)
+    share("Qw", "xQ", 16, NB, 16 + V)
+    K1 = {"A": (0, 2, 0), "L": (2, 8, 64), "H": (8, 16, 256)}
+    K2 = {"A": (0, 4, 0), "L": (4, 8, 128), "H": (8, 16, 256)}
+    ts(ci(1), ci(0), 15, None, A.bitwise_and)
+    op("v", lambda e: e.memset(T.DS[:], 0.0), [], classes("DS"))
+    ts(ci(2), ci(1), 2, None, A.logical_shift_right)
+    ts(ci(3), ci(1), 3, None, A.bitwise_and)
+    cp("v", cf(0), ci(1))
+    tt(cf(1), ci(3), ci(2), A.is_lt)
+    tt(cf(3), ci(3), ci(2), A.is_gt)
+    tt(cf(2), ci(3), ci(2), A.is_equal)
+    ts(cf(4), cf(1), -1.0, 1.0, A.mult, A.add)
+    ts(cf(5), ci(3), 0.0, cf(1), A.is_equal, A.mult)
+    ts(cf(6), cf(3), 2.0, cf(2), A.mult, A.add)
+    ts(cf(8), ci(1), 9.0, None, A.is_equal)
+    tt(cf(7), cf(6), cf(5), A.add)
+    ts(cf(9), ci(1), 13.0, cf(8), A.is_equal, A.add)
+    for s in R:
+        ts(cf(10 + s), ci(1), 14.0, 8192.0 * (3 - s), A.is_equal, A.mult)
+    for s in R:
+        tt(cf(10 + s), cf(10 + s), cf(9), A.add)
+    ts(cf(20), ci(1), 4.0, NONE, A.is_equal, A.mult)
+    ts(cf(21), ci(1), 0.0, NONE, A.is_equal, A.mult)
+    scaled(("PM", 0, 128), ("Id", 0, 128), cf(4))
+    scaled(("wS", 0, 8), ("E8", 0, 8), cf(6))
+    scaled(("wC", 0, 8), ("E8", 0, 8), cf(7))
+    for s in R:
+        scaled(("wKf", 8 * s, 8 * s + 8), ("E8", 0, 8), cf(10 + s))
+    cp("s", ("wK", 0, 32), ("wKf", 0, 32))
+    scaled(("PMf", 0, 128), ("Id", 0, 128), cf(4))
+    scaled(("PMh", 0, 128), ("Id", 0, 128), cf(4))
+    scaled(("PI", 0, 128), ("Id", 0, 128), cf(1))
+    scaled(("W1", 0, 16), ("ON", 0, 16), cf(20))
+    scaled(("B2w", 0, 16), ("ON", 0, 16), cf(21))
+    vt = ("VT", 0, 512)
+    op("s", lambda e: e.activation(ap(*vt), ap(*vt), F.Identity, bias=ap(*cf(0))), [vt, cf(0)], [vt])
+    vc = ("VC", 0, 128)
+    k9, a9 = dcol("DS", 9, 0, 16)
+    k13, a13 = dcol("DS", 13, 0, 16)
+    k14, a14 = dcol("DS", 14, 0, 16)
+    op("v", lambda e: e.tensor_copy(a9, ap(*vc)), [vc], [k9])
+    op("v", lambda e: e.tensor_scalar(a14, ap(*vc), 0.0, 1.0, A.mult, A.add), [vc], [k14])
+    op("v", lambda e: e.tensor_tensor(a13, ap(*vc), a9, A.subtract), [vc, k9], [k13])
+
+    def number_to_place(src, n, base0, halo, h):
+        off = [(base0 if k == rank else halo + h * (k if k < rank else k - 1)) - V * k for k in range(N)]
+        st = [k for k in range(1, N) if off[k] != off[k - 1]]
+        ts(("mA", 0, n), src, float(off[0]), None, A.add)
+        for k in st:
+            ts(("mB", 128 * (k - 1), 128 * (k - 1) + n), src, float(V * k), float(off[k] - off[k - 1]), A.is_ge, A.mult)
+        for k in st:
+            tt(("mA", 0, n), ("mA", 0, n), ("mB", 128 * (k - 1), 128 * (k - 1) + n), A.add)
+
+    def own_place(x, s):
+        t0, w, lo = 128 * s + C0[x] // 16, CW[x] // 16, GB[x] // 16
+        a, o = ("EQ", t0, t0 + w), ("posq", lo + s * w, lo + (s + 1) * w)
+        op("s", lambda e: e.activation(ap(*o), ap(*a), F.Identity, bias=float(16 - own)), [a], [o])
+
+    def s_sum(bank, blks):
+        for b in blks:
+            src = ("PRS", 128 * b, 128 * b + 128)
+            mm((bank, 8 * b, 8 * b + 8), ap(*src), T.wS[:], True, True, [src, ("wS", 0, 8)])
+
+    def pieces(d, ks, src, b0, b1):
+        rem = ("rem", 8 * b0, 8 * b1)
+        for i, k in enumerate(ks):
+            kk, aa = dcol(d, k, b0, b1)
+            if i == len(ks) - 1:
+                kp, pv = dcol(d, ks[i - 1], b0, b1)
+                op("v", lambda e: e.tensor_tensor(aa, ap(*src), pv, A.subtract), [src, kp], [kk])
+            else:
+                op("v", lambda e: e.tensor_copy(aa, ap(*src)), [src], [kk])
+                yield
+                if i < len(ks) - 2:
+                    op("v", lambda e: e.tensor_tensor(ap(*rem), ap(*src), aa, A.subtract), [src, kk], [rem])
+                    src = rem
+            yield
+
+    def points(b0, b1, bank):
+        src = ("Pb", 128 * b0, 128 * b1)
+        mm((bank, 0, 128 * (b1 - b0)), T.PM[:], ap(*src), True, False, [src, ("PM", 0, 128)])
+
+    def spread(d, ks, win, base, b0, b1, bank, q, with_p=False):
+        o = (bank, 0, 128 * (b1 - b0))
+        for b in range(b0, b1):
+            mm((bank, 128 * (b - b0), 128 * (b - b0) + 128), T[d][:, 128 * b:128 * b + 128], T.Id[:], not with_p,
+               (b == b1 - 1) or not with_p, [(d + "#%d" % k, 128 * b, 128 * b + 128) for k in ks] + [("Id", 0, 128)])
+        cp(q, (win, base + 128 * b0, base + 128 * b1), o)
+
+    DSK, SK = [4, 8, 12, 9, 13, 14], [4, 8, 12]
+    for i in R:
+        q = ("Qw", 16 + 512 * i, 528 + 512 * i)
+        c = ("C1f", 512, 1024) if i == 1 else ("b%d" % i, 0, 512)
+        scaled(c, q, cf(4), cf(1))
+        tt(("PRS", 512 * i, 512 * i + 512), ("Pb", 512 * i, 512 * i + 512), c, A.mult)
+        s_sum(("b4", "b4", "b5", "b5")[i], range(4 * i, 4 * i + 4))
+        if i == 0:
+            cp("v", ("EQ", 0, 512), ("nbi", 0, 512))
+        if i == 1:
+            for x in (1, 2, 3):
+                for s in R:
+                    own_place(x, s)
+            for s in R:
+                cp("s", ("NF", 16 * s, 16 * s + 16), ("EQ", 128 * s, 128 * s + 16))
+            points(0, 4, "b6")
+            points(4, 8, "b7")
+            run(pieces("DS", SK, ("b4", 0, 64), 0, 8))
+            spread("DS", DSK, "W", 0, 0, 4, "b6", "s", True)
+            spread("DS", DSK, "W", 0, 4, 8, "b7", "v", True)
+            share("W", "xW", 0, NB, V)
+    points(8, 12, "b4")
+    points(12, 16, "b6")
+    number_to_place(("NF", 0, 64), 64, 0, V, NB)
+    run(pieces("DS", SK, ("b5", 64, 128), 8, 16))
+    ts(("L1", 128, 512), ("posq", 128, 512), float(-16 - NB), None, A.add)
+    ts(("L1", 64, 128), ("posq", 64, 128), -16.0, None, A.add)
+    cp("v", ("L1", 0, 64), ("mA", 0, 64))
+    spread("DS", DSK, "W", 0, 8, 12, "b4", "s", True)
+    spread("DS", DSK, "W", 0, 12, 16, "b6", "v", True)
+    ts(("posq", 0, 64), ("mA", 0, 64), 16.0, None, A.add)
+
+    g_iota(("DB", 0, V), [[0, V]], 0, 0, True, classes("DB"))
+    for nm, K in (("VK1", K1), ("VK2", K2)):
+        for ch in "HLA":
+            b0, b1, o = K[ch]
+            g_iota((nm, o, o + 32 * (b1 - b0)), [[-8192, 4], [128, b1 - b0], [0, 8]], own + 3 * 8192 + 128 * b0, 1)
+        if nm == "VK1":
+            g_iota(("TB", 0, V), [[0, V]], 0, 0)
+            g_iota(("DM", 0, V), [[0, V]], 0, 0, True, classes("DM"))
+
+    def gather(q, out, lo, hi, win, w0, w1, offs):
+        o, wn, of = (out, lo, hi), (win, w0, w1), (offs, lo // 16, hi // 16)
+        if q == "v":
+            op("v", lambda e: e.tensor_copy(ap(*o), ap(*wn).indirect(ap(*of))), [wn, of], [o])
+        else:
+            op("s", lambda e: e.activation(ap(*o), ap(*wn).indirect(ap(*of)), F.Copy), [wn, of], [o])
+
+    def fused(lo, hi, win, w0, w1, offs, c0, c1):
+        o, wn, of, c = ("PR", lo, hi), (win, w0, w1), (offs, lo // 16, hi // 16), ("C1f", c0, c1)
+        op("v", lambda e: e.tensor_tensor(ap(*o), ap(*wn).indirect(ap(*of)), ap(*c), A.mult), [wn, of, c], [o])
+
+    def sums(src, w, x, s, c0, c1, bank, col, n, b0):
+        for b in range(c0 // 128, c1 // 128):
+            lo = GB[x] + s * CW[x] + 128 * b - C0[x]
+            at = col + s * n + 8 * (b - b0)
+            sr = (src, lo, lo + 128)
+            mm((bank, at, at + 8), ap(*sr), ap(*w), True, True, [sr, w])
+
+    def costs(K, ch, x, banks, slots=R):
+        b0, b1, _ = K[ch]
+        for s in slots:
+            for c0 in range(C0[x], C0[x] + CW[x], 512):
+                k, w = c0 // 512, min(512, CW[x])
+                lo = GB[x] + s * CW[x] + c0 - C0[x]
+                tt(("PR", lo, lo + w), ("GA", lo, lo + w), ("b%d" % k, c0 - 512 * k, c0 - 512 * k + w), A.mult)
+                sums("PR", wC, x, s, c0, c0 + w, banks[s // 2], 0, 8 * (b1 - b0), b0)
+                yield
+
+    def fused_costs(K, ch, x, win, w0, w1, offs, banks):
+        b0, b1, _ = K[ch]
+        for s in R:
+            lo = GB[x] + s * CW[x]
+            fused(lo, lo + CW[x], win, w0, w1, offs, C0[x], C0[x] + CW[x])
+            sums("PR", wC, x, s, C0[x], C0[x] + CW[x], banks[s // 2], 0, 8 * (b1 - b0), b0)
+            sums("PR", ("wKf", 8 * s, 8 * s + 8), x, s, C0[x], C0[x] + CW[x], banks[0], 256, 8 * (b1 - b0), b0)
+
+    def numbers(K, ch, x, banks):
+        b0, b1, _ = K[ch]
+        for s in R:
+            sums("GA", ("wK", 8 * s, 8 * s + 8), x, s, C0[x], C0[x] + CW[x], banks[0], 256, 8 * (b1 - b0), b0)
+
+    def bests(K, ch, x, bank):
+        b0, b1, _ = K[ch]
+        for s in R:
+            sums("GB", E8, x, s, C0[x], C0[x] + CW[x], bank, 0, 8 * (b1 - b0), b0)
+
+    def first_half(K, ch, banks):
+        b0, b1, o = K[ch]
+        n, h = 8 * (b1 - b0), o // 2
+        cp("v", ("t1", h, h + 2 * n), (banks[0], 0, 2 * n))
+
+    def best_of(K, ch, banks, half_done=False):
+        b0, b1, o = K[ch]
+        n, h = 8 * (b1 - b0), o // 2
+        be = ("best", 8 * b0, 8 * b1)
+        if not half_done:
+            first_half(K, ch, banks)
+            yield
+        tt(("t2", h, h + 2 * n), (banks[1], 2 * n, 4 * n), ("t1", h, h + 2 * n), A.min)
+        yield
+        tt(be, ("t2", h, h + n), ("t2", h + n, h + 2 * n), A.min)
+        yield
+        yield from pieces("DB", BK, be, b0, b1)
+
+    def choice(K, ch, banks, vk):
+        b0, b1, o = K[ch]
+        n, h = 8 * (b1 - b0), o // 2
+        c = (8 * b0, 8 * b1)
+        be = ("best",) + c
+        kk = (banks[0], 256, 256 + 4 * n)
+        for s in R:
+            tt(("E", o + s * n, o + (s + 1) * n), (banks[s // 2], s * n, (s + 1) * n), be, A.is_equal)
+            yield
+        tt(("LT", o, o + 4 * n), kk, (vk, o, o + 4 * n), A.is_gt)
+        yield
+        tt(("X", o, o + 4 * n), kk, ("E", o, o + 4 * n), A.mult)
+        yield
+        tt(("X2", h, h + 2 * n), ("X", o, o + 2 * n), ("X", o + 2 * n, o + 4 * n), A.max)
+        yield
+        tt(("XI",) + c, ("X2", h, h + n), ("X2", h + n, h + 2 * n), A.max)
+        yield
+        ts(("CI",) + c, ("XI",) + c, 8191, None, A.bitwise_and)
+        yield
+        tt(("DD",) + c, ("CI",) + c, ("VC",) + c, A.subtract)
+        yield
+        cp("v", ("Dh",) + c, ("DD",) + c)
+        yield
+        tt(("Dl",) + c, ("DD",) + c, ("Dh",) + c, A.subtract)
+        yield
+
+    def move_of(K, ch, bank):
+        b0, b1, o = K[ch]
+        n, h = 8 * (b1 - b0), o // 2
+        c = (8 * b0, 8 * b1)
+        tt(("tt", o, o + 4 * n), (bank, 0, 4 * n), ("LT", o, o + 4 * n), A.add)
+        yield
+        tt(("tm", h, h + 2 * n), ("tt", o, o + 2 * n), ("tt", o + 2 * n, o + 4 * n), A.min)
+        yield
+        tt(("tn",) + c, ("tm", h, h + n), ("tm", h + n, h + 2 * n), A.min)
+        yield
+        tt(("cl",) + c, ("tn",) + c, ("best",) + c, A.is_gt)
+        yield
+        for k, d in ((0, "Dh"), (1, "Dl")):
+            kk, aa = dcol("DM", k, b0, b1)
+            op("v", lambda e: e.tensor_tensor(aa, ap(*(("cl",) + c)), ap(*((d,) + c)), A.mult), [("cl",) + c, (d,) + c], [kk])
+            yield
+
+    def start_q1(i):
+        o, a = ("b%d" % i, 0, 512), ("Qw", 16 + 512 * i, 528 + 512 * i)
+        mm(o, T.PMf[:], ap(*a), True, False, [a, ("PMf", 0, 128)])
+        mm(o, T.PI[:], T.ON[:], False, False, [("PI", 0, 128), ("ON", 0, 512)])
+
+    def weights_of_tables():
+        for b in range(16):
+            o, a = T.TB[:, 129 * b:128 * b + 128:16], T.E8[:]
+            op("s", lambda e: e.activation(o, a, F.Copy), [E8], [("TB", 128 * b, 128 * b + 128)])
+
+    wC, E8 = ("wC", 0, 8), ("E8", 0, 8)
+    BK, MK = [0, 1, 2], [0, 1, 2, 3]
+
+    bH, bL, bA = ("b4", "b1"), ("b5", "b5"), ("b3", "b3")
+    gather("s", "GA", GB[3], GB[3] + 2048, "W", NB, V, "L1")
+    gather("s", "GA", GB[1], GB[2], "W", 0, V, "L1")
+    gather("s", "GA", GB[3] + 2048, 8192, "W", NB, V, "L1")
+    gather("s", "GA", 0, GB[1], "W", 0, HALO1, "L1")
+    weights_of_tables()
+    fused_costs(K1, "L", 2, "W", NB, V, "L1", bL)
+    run(costs(K1, "H", 3, bH, (0, 1)))
+    run(costs(K1, "L", 1, bL))
+    first_half(K1, "H", bH)
+    run(costs(K1, "H", 3, bH, (2, 3)), best_of(K1, "L", bL))
+    spread("DB", BK, "Bw", 0, 4, 8, "b6", "s")
+    spread("DB", BK, "Bw", 0, 2, 4, "b7", "s")
+    numbers(K1, "L", 1, bL)
+    run(best_of(K1, "H", bH, True))
+    spread("DB", BK, "Bw", 0, 8, 12, "b6", "s")
+    spread("DB", BK, "Bw", 0, 12, 16, "b7", "v")
+    run(costs(K1, "A", 0, bA))
+
+    gather("s", "GB", GB[3], GB[3] + 2048, "Bw", NB, V, "L1")
+    gather("s", "GB", GB[3] + 2048, 8192, "Bw", NB, V, "L1")
+    gather("s", "GB", GB[2], GB[3], "Bw", NB, V, "L1")
+    run(best_of(K1, "A", bA))
+    numbers(K1, "H", 3, bH)
+    numbers(K1, "A", 0, bA)
+    spread("DB", BK, "Bw", 0, 0, 2, "b6", "v")
+    share("Bw", "xB", 0, NB, V)
+    for k, j in ((2, 9), (3, 13)):
+        kk, aa = dcol("DM", k, 0, 16)
+        ks, sv = dcol("DS", j, 0, 16)
+        op("v", lambda e: e.tensor_copy(aa, sv), [ks], [kk])
+    gather("s", "GB", GB[1], GB[2], "Bw", 0, V, "L1")
+    run(choice(K1, "H", bH, "VK1"), choice(K1, "L", bL, "VK1"))
+    bests(K1, "H", 3, "b2")
+    bests(K1, "L", 2, "b0")
+    run(move_of(K1, "H", "b2"), choice(K1, "A", bA, "VK1"))
+    spread("DM", MK, "Mw", 0, 8, 12, "b6", "v")
+    spread("DM", MK, "Mw", 0, 12, 16, "b7", "v")
+    start_q1(2)
+    bests(K1, "L", 1, "b0")
+    gather("s", "GB", 0, GB[1], "Bw", 0, HALO1, "L1")
+    bests(K1, "A", 0, "b1")
+    run(move_of(K1, "L", "b0"))
+    spread("DM", MK, "Mw", 0, 4, 8, "b6", "s")
+    spread("DM", MK, "Mw", 0, 2, 4, "b7", "v")
+    run(move_of(K1, "A", "b1"))
+    spread("DM", MK, "Mw", 0, 0, 2, "b6", "v")
+    for i in (3, 0, 1):
+        start_q1(i)
+    share("Mw", "xM", 0, NB, V)
+
+    def tables(lo, hi, bank):
+        o = (bank, lo // 16, hi // 16)
+        for b in range(16):
+            l = ("TB", 128 * b, 128 * b + 128)
+            mm(o, ap(*l), T.GA[:, lo + b:hi:16], b == 0, b == 15, [l, ("GA", lo, hi)])
+
+    def pull_list(lo, hi, bank):
+        tt(("EQ", lo, hi), (bank, lo, hi), ("VT", lo, hi), A.is_equal)
+        yield
+        tt(("LQ", lo, hi), ("EQ", lo, hi), ("posq", lo, hi), A.mult)
+        yield
+
+    def next_list(lo, hi, bank):
+        ts(("EQ", lo, hi), ("EQ", lo, hi), -BIG, float(16 - own), A.mult, A.add)
+        yield
+        tt(("L2", lo, hi), (bank, lo, hi), ("EQ", lo, hi), A.add)
+        yield
+
+    def pull(x, s, c0, c1, stop):
+        k, lo = c0 // 512, GB[x] + s * CW[x] + c0 - C0[x]
+        a = ("GH", lo, lo + c1 - c0)
+        mm(("b%d" % k, c0 - 512 * k, c1 - 512 * k), T.PMh[:], ap(*a), False, stop, [a, ("PMh", 0, 128)])
+
+    def q1_out(i):
+        cp("s", ("C1f", 512 * i, 512 * i + 512), ("b%d" % i, 0, 512))
+
+    def own_sum(i, bank):
+        tt(("PRS", 512 * i, 512 * i + 512), ("Pb", 512 * i, 512 * i + 512), ("b%d" % i, 0, 512), A.mult)
+        s_sum(bank, range(4 * i, 4 * i + 4))
+
+    OWN2 = 16 + V
+    gather("s", "GA", GB[3], GB[3] + 2048, "Mw", NB, V, "L1")
+    gather("s", "GA", GB[3] + 2048, 8192, "Mw", NB, V, "L1")
+    gather("s", "GA", 0, GB[1], "Mw", 0, HALO1, "L1")
+    gather("v", "GA", GB[2], GB[3], "Mw", NB, V, "L1")
+    gather("v", "GA", GB[1], GB[2], "Mw", 0, V, "L1")
+    tables(GB[2], GB[3], "b5")
+    tables(GB[3], GB[3] + 2048, "b4")
+    tables(GB[1], GB[2], "b7")
+    tables(GB[3] + 2048, 8192, "b6")
+    run(pull_list(128, 256, "b5"))
+    run(pull_list(256, 384, "b4"))
+    run(pull_list(64, 128, "b7"))
+    gather("s", "GH", GB[2], GB[3], "Qw", 0, OWN2, "LQ")
+    gather("v", "GH", GB[3], GB[3] + 2048, "Qw", 0, OWN2, "LQ")
+    tables(0, GB[1], "b7")
+    run(pull_list(384, 512, "b6"), pull_list(0, 64, "b7"))
+    gather("s", "GH", GB[1], GB[2], "Qw", 0, OWN2, "LQ")
+    gather("v", "GH", 0, GB[1], "Qw", 0, 16 + HALO1, "LQ")
+    run(next_list(384, 512, "b6"), next_list(128, 256, "b5"))
+    run(next_list(256, 384, "b4"))
+    cp("v", ("NF", 0, 128), ("b7", 0, 128))
+    for c in (0, 512):
+        for s in (2, 3):
+            lo = GB[3] + 1024 * s + c
+            gather("s", "GH", lo, lo + 512, "Qw", 0, OWN2, "LQ")
+    for s in R:
+        pull(2, s, 512, 1024, s == 3)
+    for s in (0, 1):
+        for c in (1024, 1536):
+            pull(3, s, c, c + 512, False)
+    for s in R:
+        pull(1, s, 256, 512, False)
+    for s in R:
+        pull(0, s, 0, 256, s == 3)
+
+    for s in (2, 3):
+        pull(3, s, 1024, 1536, s == 3)
+    own_sum(1, "b7")
+    own_sum(0, "b7")
+    q1_out(1)
+    for s in (2, 3):
+        pull(3, s, 1536, 2048, s == 3)
+    own_sum(2, "b7")
+    own_sum(3, "b7")
+    q1_out(2)
+    for i, b in enumerate(("b4", "b5", "b6")):
+        points(4 * i, 4 * i + 4, b)
+    number_to_place(("NF", 0, 128), 128, 16, 16 + V, NC)
+    run(pieces("DS", SK, ("b7", 0, 128), 0, 16))
+    ts(("EQ", 0, 128), ("EQ", 0, 128), -BIG, None, A.mult)
+    tt(("L2", 0, 128), ("mA", 0, 128), ("EQ", 0, 128), A.add)
+    spread("DS", DSK, "W1", 16, 0, 4, "b4", "s", True)
+    spread("DS", DSK, "W1", 16, 4, 8, "b5", "v", True)
+    share("W1", "xW1", 16, NC, 16 + V)
+    spread("DS", DSK, "W1", 16, 8, 12, "b6", "s", True)
+    points(12, 16, "b7")
+    spread("DS", DSK, "W1", 16, 12, 16, "b7", "v", True)
+
+    bH, bL, bA = ("b4", "b1"), ("b6", "b6"), ("b5", "b5")
+    gather("s", "GA", GB[3], GB[3] + 2048, "W1", 0, OWN2, "L2")
+    gather("s", "GA", GB[3] + 2048, 8192, "W1", 0, OWN2, "L2")
+    gather("s", "GA", 0, GB[2], "W1", 0, HALO2, "L2")
+    fused_costs(K2, "L", 2, "W1", 0, OWN2, "L2", bL)
+    run(costs(K2, "H", 3, bH, (0, 1)))
+    first_half(K2, "H", bH)
+    run(costs(K2, "H", 3, bH, (2, 3)), best_of(K2, "L", bL))
+    spread("DB", BK, "B2w", 16, 4, 8, "b7", "s")
+    run(best_of(K2, "H", bH, True), costs(K2, "A", 0, bA))
+    spread("DB", BK, "B2w", 16, 8, 12, "b2", "s")
+    run(costs(K2, "A", 1, bA))
+    q1_out(0)
+    spread("DB", BK, "B2w", 16, 12, 16, "b7", "s")
+    q1_out(3)
+    for r in range(16):
+        i, j = r // 4, r % 4
+        k = 4 * min(i, j) + max(i, j)
+        dma("y", T.q1[r::16, :], T.C1f[k::16, :], [("C1f", 0, V)], [("q1#%d" % r, 0, V)], "dq1", 16 * (r + 1))
+    run(best_of(K2, "A", bA))
+    spread("DB", BK, "B2w", 16, 0, 4, "b7", "v")
+    share("B2w", "xB2", 16, NC, 16 + V)
+    numbers(K2, "H", 3, bH)
+    numbers(K2, "A", 0, bA)
+    numbers(K2, "A", 1, bA)
+    for b in range(16):
+        l = ("TB", 128 * b, 128 * b + 128)
+        mm(("b0", 0, 128), ap(*l), T.Mw[:, b:V:16], b == 0, b == 15, [l, ("Mw", 0, V)])
+
+    gather("s", "GB", GB[3], GB[3] + 2048, "B2w", 0, OWN2, "L2")
+    gather("s", "GB", GB[3] + 2048, 8192, "B2w", 0, OWN2, "L2")
+    gather("s", "GB", 0, GB[1], "B2w", 0, HALO2, "L2")
+    gather("s", "GB", GB[2], GB[3], "B2w", 0, OWN2, "L2")
+    run(choice(K2, "H", bH, "VK2"), choice(K2, "L", bL, "VK2"))
+    number_to_place(("b0", 0, 16), 16, 0, V, NB)
+    cp("v", ("LG", 0, 16), ("mA", 0, 16))
+    ts(("LG", 16, 128), ("b0", 16, 128), float(-own), None, A.add)
+    bests(K2, "H", 3, "b2")
+    run(choice(K2, "A", bA, "VK2"))
+    run(move_of(K2, "H", "b2"))
+    gather("v", "GB", GB[1], GB[2], "B2w", 0, HALO2, "L2")
+    bests(K2, "A", 0, "b0")
+    bests(K2, "A", 1, "b0")
+    run(move_of(K2, "A", "b0"))
+    spread("DM", MK, "M2w", 0, 0, 4, "b5", "v")
+    share("M2w", "xM2", 0, NB, V)
+    spread("DM", MK, "M2w", 0, 8, 12, "b7", "s")
+    spread("DM", MK, "M2w", 0, 12, 16, "b3", "s")
+    bests(K2, "L", 2, "b1")
+    run(move_of(K2, "L", "b1"))
+    spread("DM", MK, "M2w", 0, 4, 8, "b4", "v")
+
+    gather("s", "GA", 1024, 2048, "M2w", 0, V, "LG")
+    gather("v", "GA", 256, 1024, "M2w", 0, V, "LG")
+    gather("v", "GA", 0, 256, "M2w", 0, HALO1, "LG")
+    order = [8, 9, 10, 11, 12, 13, 14, 15, 2, 3, 4, 5, 6, 7, 0, 1]
+    for b in order:
+        l, a = ("TB", 128 * b, 128 * b + 128), ("GA", 128 * b, 128 * b + 128)
+        mm(("b6", 0, 128), ap(*l), ap(*a), b == order[0], b == order[-1], [l, a])
+    cp("v", ("GO", 0, 128), ("b6", 0, 128))
+    dma("y", T.goal[:], T.GO[:], [("GO", 0, 128)], [("goal", 0, V)], "dgo")
+
+    finish("y", [("dq1", 256), ("dgo", 16)])
+    finish("g", [("rl", sent[0])] + [("d%d" % i, 16) for i in range(9)] + [(x, 3 * ne) for x in EX])

@@ -2,695 +2,703 @@ from concourse.bass import DstId, RemoteDMATransfer
 from concourse.mybir import AluOpType as A, ActivationFunctionType as F
 
 N, V, NB, NC = 4, 2048, 256, 512
-C0, CW, GB = [0, 256, 512, 1024], [256, 256, 512, 1024], [0, 1024, 2048, 4096]
-HALO1, HALO2 = V + 3 * NB, 16 + V + 3 * NC
-BIG = 65536.0
+H1, H2 = 3 * NB, 3 * NC
+CH = [(0, 2), (2, 4), (4, 8), (8, 12), (12, 14), (14, 16)]
+LOADS = [(0, 2), (2, 4), (4, 8), (8, 12), (12, 14), (14, 16)]
+STORES = [(0, 1024), (1024, 2048)]
+PLAN = dict(
+    fused1={0: (0, 1, 2, 3), 1: (0, 1, 2, 3), 5: (3,)}, fused2={0: (0, 1, 2, 3), 1: (0, 1, 2, 3), 5: (3,)},
+    cost1=[("b4", (1, 0), ("b6",)), ("b5", (2, 3), ("b7", "b6")), ("b0", (4, 5), ("b4", "b1"))],
+    cost2=[("b4", (1, 0), ("b6",)), ("b5", (2, 3), ("b7", "b6")), ("b0", (4, 5), ("b4", "b1"))],
+    test1=[("b2", (1, 0), ("b5",), "b4"), ("b3", (2, 3), ("b6", "b7"), "b0"), ("b2", (4, 5), ("b5", "b4"), "b7")],
+    halo=("b5", "b5", "b6", "b6"),
+    pull=[((1,), "b4", ("b6",), "b5"), ((0,), "b4", ("b6",), "b7"), ((2,), "b4", ("b6",), "b5"), ((3,), "b4", ("b6",), "b7"),
+          ((4, 5), "b4", ("b6", "b7"), "b5")],
+    test2=[("b2", (0,), ("b7",)), ("b3", (1, 2), ("b5", "b0", "b7")), ("b2", (3, 4), ("b1", "b7", "b5")), ("b3", (5,), ("b0",))],
+    margin=1000.0, q1="sentW1", turns=4, far=2500.0, rate=100.0, once=3000.0, firstx="W", lrate=250.0, gl="s", plain=(), soon=(), cross=350.0, ago=1e9, xw=128, fix="s",
+    grain=(1, 1, 1, 1, 1, 1), cgrain=(1, 1, 1, 1, 1, 1), sgrain=(1, 1, 1, 1, 1, 1),
+)
 NONE = float(1 << 24)
+FAR = 32768.0
+R16, R8 = 1.5 * 2.0 ** 39, 1.5 * 2.0 ** 31
+EPS = 2.0 ** -14
+CYC, PE, PICK, HOP = 0.83, 0.42, 1.56, 130.0
 
 SCRATCH = {}
 for _n, _w, _t in (
-        ("Qw", 16 + HALO1, "float32"), ("Pb", V, "bfloat16"), ("nbi", 512, "int32"), ("W", HALO1, "bfloat16"),
-        ("W1", HALO2, "bfloat16"), ("Bw", HALO1, "bfloat16"), ("Mw", HALO1, "bfloat16"), ("B2w", HALO2, "bfloat16"),
-        ("M2w", HALO1, "bfloat16"), ("L1", 512, "uint16"), ("LQ", 512, "uint16"), ("L2", 512, "uint16"), ("LG", 128, "uint16"),
-        ("posq", 512, "float32"), ("VT", 512, "float32"), ("EQ", 512, "float32"), ("NF", 128, "float32"), ("mA", 128, "float32"),
-        ("mB", 384, "float32"), ("GA", 8192, "bfloat16"), ("GB", 8192, "bfloat16"), ("GH", 8192, "float16"),
-        ("PR", 8192, "float32"), ("PRS", V, "float32"), ("C1f", V, "float32"), ("DS", V, "bfloat16"), ("DB", V, "bfloat16"),
-        ("DM", V, "bfloat16"), ("TB", V, "bfloat16"), ("ON", 512, "bfloat16"), ("Id", 128, "bfloat16"), ("PM", 128, "bfloat16"),
-        ("PMh", 128, "float16"), ("PMf", 128, "float32"), ("PI", 128, "bfloat16"), ("E8", 8, "bfloat16"), ("wC", 8, "float32"),
-        ("wS", 8, "float32"), ("wK", 32, "bfloat16"), ("wKf", 32, "float32"), ("ci", 8, "int32"), ("cf", 32, "float32"),
-        ("VC", 128, "float32"), ("VK1", 512, "float32"), ("VK2", 512, "float32"), ("t1", 256, "float32"), ("t2", 256, "float32"),
-        ("best", 128, "float32"), ("rem", 128, "float32"), ("E", 512, "float32"), ("X", 512, "float32"), ("X2", 256, "float32"),
-        ("XI", 128, "int32"), ("CI", 128, "int32"), ("DD", 128, "float32"), ("Dh", 128, "bfloat16"), ("Dl", 128, "float32"),
-        ("LT", 512, "float32"), ("tt", 512, "float32"), ("tm", 256, "float32"), ("tn", 128, "float32"), ("cl", 128, "float32"),
-        ("GO", 128, "float32")):
+        ("Qw", V, "float32"), ("Pb", V, "bfloat16"), ("nbi", 512, "int32"), ("Cf", V, "float32"), ("Ch", H1 + V, "float16"),
+        ("W", H1 + V, "bfloat16"), ("W1", H2 + V + 16, "bfloat16"), ("Bw", H1 + V, "bfloat16"), ("B2w", H2 + V + 16, "bfloat16"),
+        ("M2w", H2 + V, "bfloat16"), ("X", 2 * (H1 + V), "float32"),
+        ("L1", 512, "uint16"), ("LC", 512, "uint16"), ("L2", 512, "uint16"), ("LG", 128, "uint16"),
+        ("GL", 512, "float32"), ("GLh", 512, "float16"), ("P2", 512, "float16"), ("FL", 128, "float16"), ("CT", 512, "float32"),
+        ("CO", 128, "float32"), ("NI", 64, "int32"), ("IX", 64, "int32"), ("CA", 64, "int32"), ("ma", 128, "float32"),
+        ("mb", 128, "float32"), ("GA", 8192, "bfloat16"), ("GB", 8192, "bfloat16"), ("GH", 8192, "float16"), ("PR", 8192, "float32"),
+        ("PRS", V, "float32"), ("DS", V, "bfloat16"), ("DB", V, "bfloat16"), ("DM", V, "bfloat16"), ("ON", 128, "bfloat16"),
+        ("ZZ", 128, "bfloat16"), ("Id", 128, "bfloat16"), ("Idh", 128, "float16"), ("PM", 128, "bfloat16"), ("PMh", 128, "float16"),
+        ("E8", 8, "bfloat16"), ("E32", 32, "bfloat16"), ("wA", 8, "float32"), ("wS", 8, "float32"), ("WC0", 64, "float32"),
+        ("WC", 72, "float32"), ("WO", 64, "bfloat16"), ("WB", 40, "bfloat16"), ("WE", 40, "bfloat16"), ("WN", 32, "bfloat16"),
+        ("ZB", 144, "bfloat16"), ("ZX", 144, "float16"), ("ZG", 144, "float32"), ("ZM", 144, "bfloat16"), ("RZ", 240, "float16"),
+        ("Rep", 1024, "float16"), ("RS", 256, "bfloat16"), ("ci", 8, "int32"), ("cf", 32, "float32"), ("VC", 128, "float32"),
+        ("GC", 128, "float32"), ("EV", 128, "float32"), ("MS", 512, "float32"), ("NF", 512, "bfloat16"), ("WD", 512, "float32"),
+        ("MV", 512, "float32"), ("r8", 128, "float32"), ("cl", 128, "bfloat16"), ("XD", 256, "float16"), ("XT", 768, "float16"),
+        ("XH", 768, "float16"), ("GO", 128, "float32"), ("Dh", 128, "bfloat16"), ("Dl", 128, "bfloat16")):
     SCRATCH[_n] = ("sbuf", [128, _w], _t)
 for _i in range(8):
     SCRATCH["b%d" % _i] = ("psum", [128, 512], "float32")
-EX = ["xQ", "xW", "xB", "xM", "xW1", "xB2", "xM2"]
-SEMAPHORES = ["v", "s", "p", "g", "rl", "dq1", "dgo"] + ["d%d" % i for i in range(9)] + EX
+EX = ["C", "W", "B", "X", "W1", "Wl", "B2", "Bl", "M2"]
+SEMAPHORES = ["v", "s", "p", "g", "dq1", "dgo"] + ["d%d" % i for i in range(1 + 2 * len(LOADS))] + ["x" + e for e in EX] + ["l" + e for e in EX]
 
 
 def make(g, T):
     QO = {"v": g.vector, "s": g.scalar, "p": g.tensor, "y": g.sync, "g": g}
-    cnt = {"v": 0, "s": 0, "p": 0, "g": 0}
-    known = {q: {} for q in QO}
-    clk, acc = {}, {}
+    calls, acc = [], {}
 
-    def waits(q, toks):
-        k = known[q]
-        todo = {}
-        for ch, n in toks:
-            if k.get(ch, 0) < n:
-                todo[ch] = max(n, todo.get(ch, 0))
-        items = sorted(todo.items())
-        for ch, n in items:
-            if any(c2 != ch and clk[(c2, n2)].get(ch, 0) >= n for c2, n2 in items):
-                continue
-            QO[q].wait_ge(T.sem[ch], n)
-            k[ch] = max(n, k.get(ch, 0))
-            for c3, n3 in clk[(ch, n)].items():
-                k[c3] = max(n3, k.get(c3, 0))
-
-    def is_bank(key):
-        return len(key) == 2 and key[0] == "b" and key[1].isdigit()
-
-    def deps(q, r, w, isdma):
-        toks = set()
+    def call(ways, r, w, tok=None, late=0.0, behind=None, first=0.0, group=None, stop=None):
+        before = {}
         for lst, wr in ((r, False), (w, True)):
-            for key, lo, hi in lst:
-                bank = is_bank(key)
-                for lo2, hi2, tok, q2, w2 in acc.get(key, []):
-                    same = q2 == q and not isdma
-                    if same and q == "p":
+            for key, lo, hi in [x[:3] for x in lst]:
+                b, part = (key.split("#") + [None])[:2]
+                bank = b in SCRATCH and SCRATCH[b][0] == "psum"
+                for j, p2, lo2, hi2, w2 in acc.get(b, []):
+                    if bank and group and calls[j]["group"] == group:
                         continue
-                    if bank and not same:
-                        toks.add(tok)
-                        continue
-                    if lo2 >= hi or lo >= hi2:
-                        continue
-                    if w2 or (wr and not same):
-                        toks.add(tok)
-        return toks
+                    meet = (part is None or p2 is None or part == p2) and lo2 < hi and lo < hi2
+                    if meet and (w2 or wr):
+                        before[j] = 2
+                    elif bank and (list(ways) != ["v"] or list(calls[j]["ways"]) != ["v"]):
+                        before[j] = max(1, before.get(j, 0))
+        i = len(calls)
+        for lst, wr in ((w, True), (r, False)):
+            for key, lo, hi in [x[:3] for x in lst]:
+                b, part = (key.split("#") + [None])[:2]
+                if wr and not group:
+                    acc[b] = [a for a in acc.get(b, []) if not ((part is None or part == a[1]) and lo <= a[2] and a[3] <= hi)]
+                acc.setdefault(b, []).append((i, part, lo, hi, wr))
+        calls.append(dict(ways=ways, before=before, tok=tok, late=late, behind=behind, first=first, group=group, stop=stop))
+        return i
 
-    def record(q, r, w, tok):
-        for key, lo, hi in w:
-            bank = is_bank(key)
-            acc[key] = [a for a in acc.get(key, []) if not ((lo <= a[0] and a[1] <= hi) or (bank and a[3] != q))]
-            acc[key].append((lo, hi, tok, q, True))
-        for key, lo, hi in r:
-            bank = is_bank(key)
-            acc[key] = [a for a in acc.get(key, [])
-                        if not ((not a[4] and a[3] == q and q in cnt and lo <= a[0] and a[1] <= hi) or (bank and a[3] != q))]
-            acc[key].append((lo, hi, tok, q, False))
+    def must_wait(a, qa, c, qc, k):
+        return a["tok"] is not None or c["tok"] is not None or qa != qc or (k == 2 and qc != "p")
 
-    def op(q, fn, r, w):
-        waits(q, deps(q, r, w, False))
-        cnt[q] += 1
-        fn(QO[q]).then_inc(T.sem[q], 1)
-        tok = (q, cnt[q])
-        c = dict(known[q])
-        c[q] = cnt[q]
-        clk[tok] = c
-        record(q, r, w, tok)
+    def sweep(order, links, back):
+        busy = {q: [] for q in QO}
+        for i in order:
+            c = calls[i]
+            best = None
+            for q, (fn, ns) in (c["ways"] or {None: (None, 0.0)}).items():
+                t = 0.0
+                for j, k in links[i]:
+                    a = calls[j]
+                    if must_wait(c, q, a, a["q"], k) if back else must_wait(a, a["q"], c, q, k):
+                        t = max(t, a["end"] + (HOP if q == a["q"] else PLAN["cross"]))
+                    else:
+                        t = max(t, a["end"])
+                t += c["late"] if back else 0.0
+                for a, e in busy.get(q, []):
+                    if t + ns <= a:
+                        break
+                    t = max(t, e)
+                if best is None or t + ns < best[0]:
+                    best = (t + ns, q, t)
+            c["q"], c["at"], c["end"] = best[1], best[2], best[0] + (0.0 if back else c["late"])
+            if best[1]:
+                busy[best[1]].append((best[2], best[0]))
+                busy[best[1]].sort()
+        return max(c["end"] for c in calls)
 
-    def dma(q, out, in_, r, w, sem, total=16):
-        waits(q, deps(q, r, w, True))
-        QO[q].dma_start(out, in_).then_inc(T.sem[sem], 16)
-        tok = (sem, total)
-        c = dict(known[q])
-        c[sem] = total
-        clk[tok] = c
-        record("d", r, w, tok)
+    def place():
+        n = len(calls)
+        before = [list(c["before"].items()) + ([(c["behind"], 1)] if c["behind"] is not None else []) for c in calls]
+        after = [[] for c in calls]
+        way = [0.0] * n
+        for i in range(n - 1, -1, -1):
+            c = calls[i]
+            way[i] += c["late"] + min([x[1] for x in c["ways"].values()] or [0.0])
+            for j, k in before[i]:
+                after[j].append((i, k))
+                calls[j]["first"] = max(calls[j]["first"], c["first"])
+                one = k == 1 and list(calls[j]["ways"]) == list(c["ways"]) or list(calls[j]["ways"]) == list(c["ways"]) == ["p"]
+                way[j] = max(way[j], way[i] + (1.0 if one else HOP))
+        best = None
+        for turn in range(PLAN["turns"]):
+            order = sorted(range(n), key=lambda x: (-way[x] - calls[x]["first"], x))
+            t = sweep(order, before, False)
+            if best is None or t < best[0]:
+                best = (t, order)
+            sweep(sorted(range(n), key=lambda x: (-calls[x]["end"], -x)), after, True)
+            way = [c["end"] for c in calls]
+        sweep(best[1], before, False)
 
-    def arrives(sem, total, w):
-        tok = (sem, total)
-        clk[tok] = {sem: total}
-        record("d", [], w, tok)
+    def issue(ends):
+        place()
+        last = {}
+        for c in calls:
+            if c["group"] and (c["group"] not in last or c["at"] > last[c["group"]]["at"]):
+                last[c["group"]] = c
+        for c in last.values():
+            c["stop"][0] = True
+        cnt = {"v": 0, "s": 0, "p": 0, "g": 0}
+        known = {q: {} for q in QO}
+        clk, ends_of = {}, {q: [] for q in "vsp"}
+        for i in sorted(range(len(calls)), key=lambda x: (calls[x]["at"], x)):
+            c = calls[i]
+            q = c["q"]
+            if q is None:
+                c["done"] = c["tok"]
+                clk[c["tok"]] = {c["tok"][0]: c["tok"][1]}
+                continue
+            k, todo = known[q], {}
+            for j, kind in c["before"].items():
+                ch, m = calls[j]["done"]
+                if must_wait(calls[j], calls[j]["q"], c, q, kind) and k.get(ch, 0) < m:
+                    while ch in ends_of and ch != q and m < cnt[ch] and ends_of[ch][m] + PLAN["ago"] <= c["at"]:
+                        m += 1
+                    todo[ch] = max(m, todo.get(ch, 0))
+            items = sorted(todo.items())
+            for ch, m in items:
+                if any(c2 != ch and clk[(c2, m2)].get(ch, 0) >= m for c2, m2 in items):
+                    continue
+                QO[q].wait_ge(T.sem[ch], m)
+                for c3, m3 in clk[(ch, m)].items():
+                    k[c3] = max(m3, k.get(c3, 0))
+            x = c["ways"][q][0](QO[q])
+            if c["tok"] is None:
+                cnt[q] += 1
+                ends_of.get(q, []).append(c["end"])
+                c["done"] = (q, cnt[q])
+                x.then_inc(T.sem[q], 1)
+            else:
+                c["done"] = c["tok"]
+            clk[c["done"]] = dict(k)
+            clk[c["done"]][c["done"][0]] = c["done"][1]
+        for q, toks in ends:
+            for ch, m in toks + ([x for x in cnt.items()] if q == "g" else []):
+                QO[q].wait_ge(T.sem[ch], m)
 
-    def reads(q, r):
-        waits(q, deps(q, r, [], True))
-
-    def finish(q, toks):
-        for ch in ("v", "s", "p", "g"):
-            if cnt[ch]:
-                toks.append((ch, cnt[ch]))
-        for ch, n in toks:
-            if known[q].get(ch, 0) < n or ch not in cnt:
-                QO[q].wait_ge(T.sem[ch], n)
-                known[q][ch] = n
-
-    return op, dma, arrives, reads, finish
-
-
-def run(*gens):
-    gens = list(gens)
-    while gens:
-        left = []
-        for x in gens:
-            try:
-                next(x)
-                left.append(x)
-            except StopIteration:
-                pass
-        gens = left
+    return call, issue
 
 
 def rank_program(g, core, T, topo):
     rank = T.rank_of(core)
     if rank is None:
         return
-    op, dma, arrives, reads, finish = make(g, T)
+    call, issue = make(g, T)
     own = V * rank
     others = [c for c in T.cores if c != core]
-    R = range(4)
+    R, ALL = range(4), range(16)
 
-    def ap(b, lo, hi):
-        return T[b][:, lo:hi]
+    def at(b, lo, hi, step=1, part=None, rows=128):
+        return (b if part is None else "%s#%d" % (b, part), lo, hi, T[b][0:rows, lo:hi:step], b, len(range(lo, hi, step)))
+
+    def kind(x):
+        return SCRATCH[x[4]][2] if SCRATCH[x[4]][0] == "sbuf" else "psum"
+
+    def vec(n, *xs):
+        return CYC * max(64, n / 2 if all(kind(x) in ("bfloat16", "float16", "uint16") for x in xs) else n)
+
+    def act(n):
+        return CYC * (100 + n)
+
+    def pick(ways, q):
+        return {k: x for k, x in ways.items() if k in q}
 
     def tt(o, a, b, f):
-        op("v", lambda e: e.tensor_tensor(ap(*o), ap(*a), ap(*b), f), [a, b], [o])
+        ns = CYC * max(64, o[5] * (1 if "psum" in (kind(a), kind(b)) else 2))
+        call({"v": (lambda e: e.tensor_tensor(o[3], a[3], b[3], f), ns)}, [a, b], [o])
 
     def ts(o, a, s1, s2, f1, f2=None):
         rd = [a] + [x for x in (s1, s2) if isinstance(x, tuple)]
-        x1 = ap(*s1) if isinstance(s1, tuple) else s1
-        x2 = ap(*s2) if isinstance(s2, tuple) else s2
+        x1 = s1[3] if isinstance(s1, tuple) else s1
+        x2 = s2[3] if isinstance(s2, tuple) else s2
         if f2 is None:
-            op("v", lambda e: e.tensor_scalar(ap(*o), ap(*a), x1, x2, f1), rd, [o])
+            call({"v": (lambda e: e.tensor_scalar(o[3], a[3], x1, x2, f1), vec(o[5], o, a))}, rd, [o])
         else:
-            op("v", lambda e: e.tensor_scalar(ap(*o), ap(*a), x1, x2, f1, f2), rd, [o])
+            call({"v": (lambda e: e.tensor_scalar(o[3], a[3], x1, x2, f1, f2), vec(o[5], o, a))}, rd, [o])
+
+    def scan(o, a, b, f1, f2):
+        call({"v": (lambda e: e.tensor_tensor_scan(o[3], a[3], b[3], 0.0, f1, f2), vec(o[5], o, a, b))}, [a, b], [o])
 
     def cp(q, o, a):
-        if q == "v":
-            op("v", lambda e: e.tensor_copy(ap(*o), ap(*a)), [a], [o])
-        else:
-            op("s", lambda e: e.activation(ap(*o), ap(*a), F.Copy), [a], [o])
+        call(pick({"v": (lambda e: e.tensor_copy(o[3], a[3]), vec(o[5], o, a)),
+                   "s": (lambda e: e.activation(o[3], a[3], F.Copy), act(o[5]))}, q), [a], [o])
 
-    def scaled(o, a, col, bias=None):
-        rd = [a, col] + ([bias] if bias else [])
+    def scaled(q, o, a, col, bias=None):
         if bias:
-            op("s", lambda e: e.activation(ap(*o), ap(*a), F.Identity, bias=ap(*bias), scale=ap(*col)), rd, [o])
+            ways = {"v": (lambda e: e.tensor_scalar(o[3], a[3], col[3], bias[3], A.mult, A.add), vec(o[5], o, a)),
+                    "s": (lambda e: e.activation(o[3], a[3], F.Identity, bias=bias[3], scale=col[3]), act(o[5]))}
         else:
-            op("s", lambda e: e.activation(ap(*o), ap(*a), F.Identity, scale=ap(*col)), rd, [o])
+            ways = {"v": (lambda e: e.tensor_scalar(o[3], a[3], col[3], None, A.mult), vec(o[5], o, a)),
+                    "s": (lambda e: e.activation(o[3], a[3], F.Identity, scale=col[3]), act(o[5]))}
+        call(pick(ways, q), [a, col] + ([bias] if bias else []), [o])
 
-    def dcol(d, k, b0, b1):
-        return (d + "#%d" % k, 128 * b0, 128 * b1), T[d][:, 128 * b0 + k:128 * b1:16]
+    opened = {}
 
-    def mm(o, lt, rh, start, stop, r):
-        op("p", lambda e: e.matmul(ap(*o), lt, rh, start, stop), r, [o])
+    def mm(o, lt, rh, start, stop=None, r=(), w=()):
+        ns = PE * max(min(64, lt[5]), rh[5]) * (4 if kind(lt) == "float32" else 1)
+        if start:
+            opened[o[4]] = opened.get(o[4], 0) + 1
+        flag = [bool(stop)]
+        call({"p": (lambda e: e.matmul(o[3], lt[3], rh[3], start, flag[0]), ns)}, [lt, rh] + list(r), [o] + list(w),
+             group=None if start or stop is not None else (o[4], opened[o[4]]), stop=flag)
 
-    def fill(b, lo, hi, x):
-        op("v", lambda e: e.memset(ap(b, lo, hi), x), [], [(b, lo, hi)])
+    def fill(o, x):
+        call({"v": (lambda e: e.memset(o[3], x), vec(o[5], o))}, [], [o])
 
-    for i in R:
-        a = 512 * i
-        dma("y", T.Qw[:, 16 + a:16 + a + 512], T.qu[:, a:a + 512], [], [("Qw", 16 + a, 16 + a + 512)], "d%d" % i)
-        dma("s", T.Pb[:, a:a + 512], T.po[:, a:a + 512], [], [("Pb", a, a + 512)], "d%d" % (4 + i))
+    def dma(q, out, in_, r, w, sem, late, total=16):
+        call({q: (lambda e: e.dma_start(out, in_).then_inc(T.sem[sem], 16), 60.0)}, r, w, (sem, total), late, None,
+             0.0 if r else 1e9 - 1e3 * late)
+
+    def gather(q, out, lo, hi, win, w0, w1, offs):
+        o, wn, of = at(out, lo, hi), at(win, w0, w1), at(offs, lo // 16, hi // 16)
+        ns = CYC * PICK * (hi - lo)
+        call(pick({"v": (lambda e: e.tensor_copy(o[3], wn[3].indirect(of[3])), 50 + ns),
+                   "s": (lambda e: e.activation(o[3], wn[3].indirect(of[3]), F.Copy), 65 + ns)}, q), [wn, of], [o])
+
+    def gather_times(o, wn, of, c):
+        call({"v": (lambda e: e.tensor_tensor(o[3], wn[3].indirect(of[3]), c[3], A.mult), 50 + CYC * PICK * o[5])}, [wn, of, c], [o])
+
+    def g_sel(o, i, pat, c, base, cm):
+        call({"g": (lambda e: e.affine_select(o[3], i[3], pat, c, 0.0, base, cm), 170 + 2 * CYC * o[5])}, [i], [o])
+
+    def g_iota(o, pat, base, cm, late=0.0):
+        call({"g": (lambda e: e.iota(o[3], pat, base, cm, allow_small_or_imprecise_dtypes=True), 130 + 2 * CYC * o[5])}, [], [o], None, late)
+
+    def g_zero(b, lo, hi):
+        for a in range(lo, hi, 512):
+            g_iota(at(b, a, min(hi, a + 512)), [[0, min(hi, a + 512) - a]], 0, 0, PLAN["margin"])
+
+    def cls(d, k, b0, b1):
+        return ("%s#%d" % (d, k), 128 * b0, 128 * b1, T[d][:, 128 * b0 + k:128 * b1:16], d, 8 * (b1 - b0))
+
+    def gcol(b, s):
+        b0, b1 = [c for c in CH if c[0] <= b < c[1]][0]
+        return 512 * b0 + 128 * (s * (b1 - b0) + b - b0)
+
+    Id, Idh, E8 = at("Id", 0, 128), at("Idh", 0, 128), at("E8", 0, 8)
+
+    col = 128 / PLAN["lrate"]
+    for i, (b0, b1) in enumerate(LOADS):
+        a, e, n = 128 * b0, 128 * b1, 2048 if i else 0
+        dma("y", T.Qw[:, a:e], T.qu[:, a:e], [], [("Qw", a, e)], "d%d" % (2 + 2 * i), 1900.0 + (n + 2 * a + 4 * e) * col)
+        dma("s", T.Pb[:, a:e], T.po[:, a:e], [], [("Pb", a, e)], "d%d" % (1 + 2 * i), 1900.0 + (n + 6 * e) * col)
         if i == 0:
-            dma("s", T.nbi[:], T.nb[:], [], [("nbi", 0, 512)], "d8")
+            dma("s", T.nbi[:], T.nb[:], [], [("nbi", 0, 512)], "d0", 1900.0 + (2048 + 6 * e) * col)
 
     msk = topo.mask(core, others[0])
     for c in others[1:]:
         msk &= topo.mask(core, c)
     ne = bin(msk).count("1")
-    sent = [0]
-    arrives("xQ", 3 * ne, [("Qw", 16 + V, 16 + HALO1)])
-    for b, x in (("W", "xW"), ("Bw", "xB"), ("Mw", "xM"), ("M2w", "xM2")):
-        arrives(x, 3 * ne, [(b, V, HALO1)])
-    for b, x in (("W1", "xW1"), ("B2w", "xB2")):
-        arrives(x, 3 * ne, [(b, 16 + V, HALO2)])
 
-    def share(b, sem, lo, w, base):
-        reads("g", [(b, lo, lo + w)])
-        ids, dst = [], []
-        for c in others:
-            q = T.rank_of(c)
-            at = base + w * (rank if rank < q else rank - 1)
-            rid, pid = topo.addr(c)[0], topo.addr(c)[1]
-            ids.append(DstId(rid=rid, pnc=pid))
-            dst.append(T[b][:, at:at + w])
-        g.remote_dma_fused([RemoteDMATransfer(dst_ids=ids, dma_engine_mask=msk, remote_sem=T.sem[sem],
-                                              srcs=[T[b][:, lo:lo + w]], dsts=dst)], local_sem=T.sem.rl)
-        sent[0] += ne
+    sent = []
 
-    def g_sel(o, i, pat, c, base, cm):
-        op("g", lambda e: e.affine_select(ap(*o), ap(*i), pat, c, 0.0, base, cm), [i], [o])
-
-    def g_iota(o, pat, base, cm, fl=True, w=None):
-        if fl:
-            op("g", lambda e: e.iota(ap(*o), pat, base, cm, allow_small_or_imprecise_dtypes=True), [], w or [o])
-        else:
-            op("g", lambda e: e.iota(ap(*o), pat, base, cm), [], [o])
-
-    def classes(d):
-        return [(d + "#%d" % k, 0, V) for k in range(16)]
+    def share(b, name, lo, w, to=None, pitch=None, after=(), off=0):
+        to, pitch = to or b, pitch or w
+        sent.append(name)
+        ids = [DstId(rid=topo.addr(c)[0], pnc=topo.addr(c)[1]) for c in others]
+        dst = [T[to][:, pitch * k + off:pitch * k + off + w] for k in [(rank - T.rank_of(c) - 1) % N for c in others]]
+        tr = RemoteDMATransfer(dst_ids=ids, dma_engine_mask=msk, remote_sem=T.sem["x" + name], srcs=[T[b][:, lo:lo + w]], dsts=dst)
+        late = PLAN["far"] + 3 * 128 * w * 2 / PLAN["rate"] + (PLAN["once"] if name == "W" else 0.0)
+        i = call({"g": (lambda e: e.remote_dma_fused([tr], local_sem=T.sem["l" + name]), 300.0)}, [(b, lo, lo + w)] + list(after),
+                 [("sent" + name, 0, 1)], ("l" + name, ne), late, None, 1e6 if name in PLAN["soon"] else 0.0)
+        call({}, [], [(to, pitch * k + off, pitch * k + off + w) for k in range(3)], ("x" + name, 3 * ne), 0.0, i)
 
     def ci(k):
-        return ("ci", k, k + 1)
+        return at("ci", k, k + 1)
 
     def cf(k):
-        return ("cf", k, k + 1)
+        return at("cf", k, k + 1)
 
-    fill("ON", 0, 512, 1.0)
-    fill("Qw", 0, 16, 0.0)
-    g_iota(ci(0), [[0, 1]], 0, 1, False)
-    g_sel(("Id", 0, 128), ("ON", 0, 128), [[-1, 128]], A.is_equal, 0, 1)
-    g_sel(("E8", 0, 8), ("ON", 0, 8), [[-16, 8]], A.is_ge, 0, 1)
-    g_sel(("E8", 0, 8), ("E8", 0, 8), [[16, 8]], A.is_ge, 15, -1)
-    g_iota(("VC", 0, 128), [[128, 16], [0, 8]], own, 1)
-    for x in range(4):
-        n = CW[x] // 16
-        g_iota(("VT", GB[x] // 16, GB[x] // 16 + 4 * n), [[0, 4], [16, n]], own + C0[x], 0)
-    share("Qw", "xQ", 16, NB, 16 + V)
-    K1 = {"A": (0, 2, 0), "L": (2, 8, 64), "H": (8, 16, 256)}
-    K2 = {"A": (0, 4, 0), "L": (4, 8, 128), "H": (8, 16, 256)}
+    ROW, LOW, UP, W6, WCOST, CODE, NCODE, RA, RX, RQ, B012, NB012, B34, B56, SW, SB = [cf(k) for k in range(16)]
+    fill(at("ON", 0, 128), 1.0)
+    call({"g": (lambda e: e.iota(ci(0)[3], [[0, 1]], 0, 1), 130.0)}, [], [ci(0)])
+    g_sel(E8, at("ON", 0, 8), [[-16, 8]], A.is_ge, 0, 1)
+    g_sel(E8, E8, [[16, 8]], A.is_ge, 15, -1)
+    g_sel(Id, at("ON", 0, 128), [[-1, 128]], A.is_equal, 0, 1)
+    g_iota(at("VC", 0, 128), [[128, 16], [0, 8]], own, 1)
+    g_sel(at("E32", 0, 32), at("ON", 0, 32), [[-16, 8], [0, 4]], A.is_ge, 0, 1)
+    g_sel(at("E32", 0, 32), at("E32", 0, 32), [[16, 8], [0, 4]], A.is_ge, 15, -1)
+    for b0, b1 in CH:
+        g_iota(at("CT", 32 * b0, 32 * b1), [[0, 4], [16, 8 * (b1 - b0)]], 128 * b0, 0)
+    g_iota(at("CO", 0, 128), [[16, 128]], 0, 0)
+    fill(at("DS", 0, 512), 0.0)
+    g_zero("DS", 512, V)
+    g_zero("DB", 0, V)
+    g_zero("XT", 0, 512)
+    g_zero("DM", 0, V)
+    for k in range(3):
+        g_zero("M2w", NC * k + NB, NC * k + NC)
+    for b in ("WC0", "WC", "WO", "WB", "WE", "ZZ", "ZB", "ZX", "ZG", "ZM", "RZ", "RS"):
+        fill(at(b, 0, T[b].shape[1]), 0.0)
+    fill(at("NF", 0, 512, 4, 0), 0.0)
+    fill(at("RS", 0, 256, 4), 1e9)
     ts(ci(1), ci(0), 15, None, A.bitwise_and)
-    op("v", lambda e: e.memset(T.DS[:], 0.0), [], classes("DS"))
     ts(ci(2), ci(1), 2, None, A.logical_shift_right)
     ts(ci(3), ci(1), 3, None, A.bitwise_and)
-    cp("v", cf(0), ci(1))
-    tt(cf(1), ci(3), ci(2), A.is_lt)
-    tt(cf(3), ci(3), ci(2), A.is_gt)
-    tt(cf(2), ci(3), ci(2), A.is_equal)
-    ts(cf(4), cf(1), -1.0, 1.0, A.mult, A.add)
-    ts(cf(5), ci(3), 0.0, cf(1), A.is_equal, A.mult)
-    ts(cf(6), cf(3), 2.0, cf(2), A.mult, A.add)
-    ts(cf(8), ci(1), 9.0, None, A.is_equal)
-    tt(cf(7), cf(6), cf(5), A.add)
-    ts(cf(9), ci(1), 13.0, cf(8), A.is_equal, A.add)
-    for s in R:
-        ts(cf(10 + s), ci(1), 14.0, 8192.0 * (3 - s), A.is_equal, A.mult)
-    for s in R:
-        tt(cf(10 + s), cf(10 + s), cf(9), A.add)
-    ts(cf(20), ci(1), 4.0, NONE, A.is_equal, A.mult)
-    ts(cf(21), ci(1), 0.0, NONE, A.is_equal, A.mult)
-    scaled(("PM", 0, 128), ("Id", 0, 128), cf(4))
-    scaled(("wS", 0, 8), ("E8", 0, 8), cf(6))
-    scaled(("wC", 0, 8), ("E8", 0, 8), cf(7))
-    for s in R:
-        scaled(("wKf", 8 * s, 8 * s + 8), ("E8", 0, 8), cf(10 + s))
-    cp("s", ("wK", 0, 32), ("wKf", 0, 32))
-    scaled(("PMf", 0, 128), ("Id", 0, 128), cf(4))
-    scaled(("PMh", 0, 128), ("Id", 0, 128), cf(4))
-    scaled(("PI", 0, 128), ("Id", 0, 128), cf(1))
-    scaled(("W1", 0, 16), ("ON", 0, 16), cf(20))
-    scaled(("B2w", 0, 16), ("ON", 0, 16), cf(21))
-    vt = ("VT", 0, 512)
-    op("s", lambda e: e.activation(ap(*vt), ap(*vt), F.Identity, bias=ap(*cf(0))), [vt, cf(0)], [vt])
-    vc = ("VC", 0, 128)
-    k9, a9 = dcol("DS", 9, 0, 16)
-    k13, a13 = dcol("DS", 13, 0, 16)
-    k14, a14 = dcol("DS", 14, 0, 16)
-    op("v", lambda e: e.tensor_copy(a9, ap(*vc)), [vc], [k9])
-    op("v", lambda e: e.tensor_scalar(a14, ap(*vc), 0.0, 1.0, A.mult, A.add), [vc], [k14])
-    op("v", lambda e: e.tensor_tensor(a13, ap(*vc), a9, A.subtract), [vc, k9], [k13])
+    cp("v", ROW, ci(1))
+    tt(LOW, ci(3), ci(2), A.is_lt)
+    tt(cf(16), ci(3), ci(2), A.is_gt)
+    tt(cf(17), ci(3), ci(2), A.is_equal)
+    ts(cf(18), ROW, 9.0, None, A.is_equal)
+    ts(RA, ROW, 4.0, None, A.is_equal)
+    ts(cf(19), ROW, 8.0, None, A.is_equal)
+    ts(B012, ROW, 3.0, None, A.is_lt)
+    ts(NB012, ROW, 3.0, -1.0, A.is_lt, A.mult)
+    ts(cf(20), ROW, 5.0, None, A.is_lt)
+    ts(cf(21), ROW, 7.0, None, A.is_lt)
+    ts(SW, ROW, 4.0, NONE, A.is_equal, A.mult)
+    ts(SB, ROW, 0.0, NONE, A.is_equal, A.mult)
+    ts(UP, LOW, -1.0, 1.0, A.mult, A.add)
+    ts(cf(22), ci(3), 0.0, LOW, A.is_equal, A.mult)
+    ts(W6, cf(16), 2.0, cf(17), A.mult, A.add)
+    ts(CODE, ROW, 13.0, cf(18), A.is_equal, A.add)
+    ts(RX, cf(19), FAR, RA, A.mult, A.add)
+    tt(B34, cf(20), B012, A.subtract)
+    ts(B56, cf(21), cf(20), EPS, A.subtract, A.mult)
+    tt(RQ, UP, cf(19), A.add)
+    tt(WCOST, W6, cf(22), A.add)
+    ts(NCODE, CODE, -1.0, None, A.mult)
+    cp("s", at("wA", 0, 8), E8)
+    cp("s", Idh, Id)
+    cp("s", at("ZM", 15, 143, 16), E8)
+    for o, col in ((at("WC0", 0, 64, 8, 0), WCOST), (at("WC0", 1, 64, 8, 1), CODE), (at("WC", 6, 70, 8, 0), WCOST),
+                   (at("WC", 7, 71, 8, 1), CODE), (at("WC", 5, 69, 8, 2), NCODE), (at("WO", 7, 64, 8), NCODE),
+                   (at("WB", 3, 35, 4), B012), (at("WE", 3, 35, 4), B56), (at("ZB", 15, 143, 16), B34), (at("ZX", 15, 143, 16), RX),
+                   (at("ZG", 15, 143, 16), RA), (at("RZ", 112, 128, 2, 0), RQ), (at("RZ", 113, 128, 2, 1), RA), (at("wS", 0, 8), W6)):
+        scaled("s", o, E8, col)
+    scaled("s", at("PM", 0, 128), Id, UP)
+    g_iota(at("GO", 0, 128), [[1, 128]], 0, -1)
+    tt(cf(23), ci(3), ci(2), A.subtract)
+    ts(cf(24), cf(23), 3.0, None, A.mult)
+    ts(at("r8", 0, 128), at("GO", 0, 128), cf(24), cf(16), A.is_equal, A.mult)
+    scaled("s", at("PMh", 0, 128), Id, UP)
+    tt(at("PMh", 0, 128), at("PMh", 0, 128), at("r8", 0, 128), A.add)
+    scaled("s", at("WN", 0, 32), at("E32", 0, 32), NB012)
+    scaled("s", at("W1", H2 + V, H2 + V + 16), at("ON", 0, 16), SW)
+    scaled("s", at("B2w", H2 + V, H2 + V + 16), at("ON", 0, 16), SB)
+    for k in range(8):
+        mm(at("b%d" % (k // 4), 128 * (k % 4), 128 * (k % 4) + 128), at("RZ", 112 - 16 * k, 240 - 16 * k), Idh, True, True)
+    for k in (0, 1):
+        cp("s", at("Rep", 512 * k, 512 * k + 512), at("b%d" % k, 0, 512))
 
-    def number_to_place(src, n, base0, halo, h):
-        off = [(base0 if k == rank else halo + h * (k if k < rank else k - 1)) - V * k for k in range(N)]
-        st = [k for k in range(1, N) if off[k] != off[k - 1]]
-        ts(("mA", 0, n), src, float(off[0]), None, A.add)
-        for k in st:
-            ts(("mB", 128 * (k - 1), 128 * (k - 1) + n), src, float(V * k), float(off[k] - off[k - 1]), A.is_ge, A.mult)
-        for k in st:
-            tt(("mA", 0, n), ("mA", 0, n), ("mB", 128 * (k - 1), 128 * (k - 1) + n), A.add)
+    vc, gc = at("VC", 0, 128), at("GC", 0, 128)
+    ts(gc, vc, float(-1536 * rank), None, A.add)
+    cp("s", cls("DS", 9, 0, 16), gc)
+    tt(cls("DS", 13, 0, 16), gc, cls("DS", 9, 0, 16), A.subtract)
+    cp("s", cls("DB", 5, 0, 16), vc)
+    tt(cls("DB", 6, 0, 16), vc, cls("DB", 5, 0, 16), A.subtract)
+    ts(at("EV", 0, 128), vc, EPS, None, A.mult)
+    cp("s", cls("DM", 2, 0, 16), cls("DB", 5, 0, 16))
+    cp("s", cls("DM", 3, 0, 16), cls("DB", 6, 0, 16))
 
-    def own_place(x, s):
-        t0, w, lo = 128 * s + C0[x] // 16, CW[x] // 16, GB[x] // 16
-        a, o = ("EQ", t0, t0 + w), ("posq", lo + s * w, lo + (s + 1) * w)
-        op("s", lambda e: e.activation(ap(*o), ap(*a), F.Identity, bias=float(16 - own)), [a], [o])
+    for s in R:
+        ts(at("NI", 16 * s, 16 * s + 16), at("nbi", 128 * s, 128 * s + 16), float(V * (3 - rank)), None, A.add)
+    ts(at("MV", 0, 512), at("nbi", 0, 512), float(-own), None, A.add)
+    for b0, b1 in CH[1:]:
+        for s in R:
+            lo, n = gcol(b0, s) // 16, 8 * (b1 - b0)
+            cp(PLAN["gl"], at("GL", lo, lo + n), at("MV", 128 * s + 8 * b0, 128 * s + 8 * b1))
+    ts(at("IX", 0, 64), at("NI", 0, 64), 11, 3, A.logical_shift_right, A.bitwise_and)
+    ts(at("CA", 0, 64), at("NI", 0, 64), V - 1, None, A.bitwise_and)
+    ts(at("ma", 0, 64), at("IX", 0, 64), 256.0, None, A.mult)
+    ts(at("ma", 64, 128), at("IX", 0, 64), 512.0, 512.0, A.mult, A.add)
+    ts(at("mb", 64, 128), at("IX", 0, 64), float(3 - rank), float(-V), A.is_ge, A.mult)
+    tt(at("mb", 0, 64), at("ma", 0, 64), at("CA", 0, 64), A.add)
+    tt(at("ma", 64, 128), at("ma", 64, 128), at("mb", 64, 128), A.add)
+    cp("v", at("L1", 64, 128), at("GL", 64, 128))
+    ts(at("L1", 128, 512), at("GL", 128, 512), float(-NB), None, A.add)
+    cp("v", at("L1", 0, 64), at("mb", 0, 64))
+    tt(at("GL", 0, 64), at("ma", 64, 128), at("CA", 0, 64), A.add)
+    ts(at("P2", 0, 64), at("mb", 0, 64), 2.0, None, A.mult)
+    ts(at("P2", 64, 128), at("GL", 64, 128), 2.0, None, A.mult)
+    ts(at("P2", 128, 512), at("GL", 128, 512), float(-NB), 2.0, A.add, A.mult)
+    cp("s", at("GLh", 0, 512), at("GL", 0, 512))
+    ts(at("FL", 0, 64), at("CA", 0, 64), float(NB), float(V), A.is_ge, A.mult)
+    ts(at("FL", 64, 128), at("GL", 64, 128), float(NB), float(V), A.is_ge, A.mult)
+    ts(at("CT", 0, 512), at("CT", 0, 512), ROW, None, A.add)
+    ts(at("CO", 0, 128), at("CO", 0, 128), ROW, None, A.add)
 
-    def s_sum(bank, blks):
-        for b in blks:
-            src = ("PRS", 128 * b, 128 * b + 128)
-            mm((bank, 8 * b, 8 * b + 8), ap(*src), T.wS[:], True, True, [src, ("wS", 0, 8)])
+    def s_sum(bank, w, b0, b1):
+        for b in range(b0, b1):
+            mm(at(bank, 8 * b, 8 * b + 8), at("PRS", 128 * b, 128 * b + 128), at(w, 0, 8), True, True)
 
     def pieces(d, ks, src, b0, b1):
-        rem = ("rem", 8 * b0, 8 * b1)
-        for i, k in enumerate(ks):
-            kk, aa = dcol(d, k, b0, b1)
-            if i == len(ks) - 1:
-                kp, pv = dcol(d, ks[i - 1], b0, b1)
-                op("v", lambda e: e.tensor_tensor(aa, ap(*src), pv, A.subtract), [src, kp], [kk])
-            else:
-                op("v", lambda e: e.tensor_copy(aa, ap(*src)), [src], [kk])
-                yield
-                if i < len(ks) - 2:
-                    op("v", lambda e: e.tensor_tensor(ap(*rem), ap(*src), aa, A.subtract), [src, kk], [rem])
-                    src = rem
-            yield
+        hi, mid, lo = [cls(d, k, b0, b1) for k in ks]
+        r8 = at("r8", 8 * b0, 8 * b1)
+        ts(r8, src, R8, -R8, A.add, A.add)
+        ts(hi, src, R16, -R16, A.add, A.add)
+        tt(lo, src, r8, A.subtract)
+        tt(mid, r8, hi, A.subtract)
 
-    def points(b0, b1, bank):
-        src = ("Pb", 128 * b0, 128 * b1)
-        mm((bank, 0, 128 * (b1 - b0)), T.PM[:], ap(*src), True, False, [src, ("PM", 0, 128)])
-
-    def spread(d, ks, win, base, b0, b1, bank, q, with_p=False):
-        o = (bank, 0, 128 * (b1 - b0))
+    def spread(d, win, base, b0, b1, bank, with_p=False, q="vs"):
+        if with_p:
+            mm(at(bank, 0, 128 * (b1 - b0)), at("PM", 0, 128), at("Pb", 128 * b0, 128 * b1), True, False)
         for b in range(b0, b1):
-            mm((bank, 128 * (b - b0), 128 * (b - b0) + 128), T[d][:, 128 * b:128 * b + 128], T.Id[:], not with_p,
-               (b == b1 - 1) or not with_p, [(d + "#%d" % k, 128 * b, 128 * b + 128) for k in ks] + [("Id", 0, 128)])
-        cp(q, (win, base + 128 * b0, base + 128 * b1), o)
+            mm(at(bank, 128 * (b - b0), 128 * (b - b0) + 128), at(d, 128 * b, 128 * b + 128), Id, not with_p, None if with_p else True)
+        cp(q, at(win, base + 128 * b0, base + 128 * b1), at(bank, 0, 128 * (b1 - b0)))
 
-    DSK, SK = [4, 8, 12, 9, 13, 14], [4, 8, 12]
-    for i in R:
-        q = ("Qw", 16 + 512 * i, 528 + 512 * i)
-        c = ("C1f", 512, 1024) if i == 1 else ("b%d" % i, 0, 512)
-        scaled(c, q, cf(4), cf(1))
-        tt(("PRS", 512 * i, 512 * i + 512), ("Pb", 512 * i, 512 * i + 512), c, A.mult)
-        s_sum(("b4", "b4", "b5", "b5")[i], range(4 * i, 4 * i + 4))
-        if i == 0:
-            cp("v", ("EQ", 0, 512), ("nbi", 0, 512))
-        if i == 1:
-            for x in (1, 2, 3):
-                for s in R:
-                    own_place(x, s)
-            for s in R:
-                cp("s", ("NF", 16 * s, 16 * s + 16), ("EQ", 128 * s, 128 * s + 16))
-            points(0, 4, "b6")
-            points(4, 8, "b7")
-            run(pieces("DS", SK, ("b4", 0, 64), 0, 8))
-            spread("DS", DSK, "W", 0, 0, 4, "b6", "s", True)
-            spread("DS", DSK, "W", 0, 4, 8, "b7", "v", True)
-            share("W", "xW", 0, NB, V)
-    points(8, 12, "b4")
-    points(12, 16, "b6")
-    number_to_place(("NF", 0, 64), 64, 0, V, NB)
-    run(pieces("DS", SK, ("b5", 64, 128), 8, 16))
-    ts(("L1", 128, 512), ("posq", 128, 512), float(-16 - NB), None, A.add)
-    ts(("L1", 64, 128), ("posq", 64, 128), -16.0, None, A.add)
-    cp("v", ("L1", 0, 64), ("mA", 0, 64))
-    spread("DS", DSK, "W", 0, 8, 12, "b4", "s", True)
-    spread("DS", DSK, "W", 0, 12, 16, "b6", "v", True)
-    ts(("posq", 0, 64), ("mA", 0, 64), 16.0, None, A.add)
+    def c_bank(b0, b1):
+        return at("b%d" % (b0 // 4), 128 * (b0 % 4), 128 * (b0 % 4 + b1 - b0))
 
-    g_iota(("DB", 0, V), [[0, V]], 0, 0, True, classes("DB"))
-    for nm, K in (("VK1", K1), ("VK2", K2)):
-        for ch in "HLA":
-            b0, b1, o = K[ch]
-            g_iota((nm, o, o + 32 * (b1 - b0)), [[-8192, 4], [128, b1 - b0], [0, 8]], own + 3 * 8192 + 128 * b0, 1)
-        if nm == "VK1":
-            g_iota(("TB", 0, V), [[0, V]], 0, 0)
-            g_iota(("DM", 0, V), [[0, V]], 0, 0, True, classes("DM"))
+    def start_c(b0, b1, stop):
+        mm(c_bank(b0, b1), Idh if stop else at("PMh", 0, 128), at("Ch", H1 + 128 * b0, H1 + 128 * b1), True, stop)
 
-    def gather(q, out, lo, hi, win, w0, w1, offs):
-        o, wn, of = (out, lo, hi), (win, w0, w1), (offs, lo // 16, hi // 16)
-        if q == "v":
-            op("v", lambda e: e.tensor_copy(ap(*o), ap(*wn).indirect(ap(*of))), [wn, of], [o])
+    SK = [4, 8, 12]
+    for i, (b0, b1) in enumerate(LOADS):
+        a, e = 128 * b0, 128 * b1
+        q, bank = at("Qw", a, e), "b4" if i % 2 else "b5"
+        scaled("s", at("Ch", H1 + a, H1 + e), q, UP, LOW)
+        start_c(b0, b1, True)
+        if i in PLAN["plain"]:
+            tt(at("PRS", a, e), at("Pb", a, e), q, A.mult)
+            s_sum(bank, "wA", b0, b1)
         else:
-            op("s", lambda e: e.activation(ap(*o), ap(*wn).indirect(ap(*of)), F.Copy), [wn, of], [o])
+            tt(at("PRS", a, e), at("Pb", a, e), c_bank(b0, b1), A.mult)
+            s_sum(bank, "wS", b0, b1)
+        pieces("DS", SK, at(bank, 8 * b0, 8 * b1), b0, b1)
+        spread("DS", "W", H1, b0, b1, "b6" if i % 2 else "b7", True)
+        if i == 0:
+            if PLAN["firstx"] == "C":
+                share("Ch", "C", H1, NB)
+            share("W", "W", H1, NB)
+    if PLAN["firstx"] == "W":
+        share("Ch", "C", H1, NB, after=[("Qw", 0, V), ("Pb", 0, V), ("sentW", 0, 1)])
 
-    def fused(lo, hi, win, w0, w1, offs, c0, c1):
-        o, wn, of, c = ("PR", lo, hi), (win, w0, w1), (offs, lo // 16, hi // 16), ("C1f", c0, c1)
-        op("v", lambda e: e.tensor_tensor(ap(*o), ap(*wn).indirect(ap(*of)), ap(*c), A.mult), [wn, of, c], [o])
+    def clear(bank, n):
+        mm(at(bank, 0, n), at("ZZ", 0, 128), at("Pb", 0, n), True, False)
 
-    def sums(src, w, x, s, c0, c1, bank, col, n, b0):
-        for b in range(c0 // 128, c1 // 128):
-            lo = GB[x] + s * CW[x] + 128 * b - C0[x]
-            at = col + s * n + 8 * (b - b0)
-            sr = (src, lo, lo + 128)
-            mm((bank, at, at + 8), ap(*sr), ap(*w), True, True, [sr, w])
+    def cost_start(bank, b0, b1, win, base):
+        clear(bank, 64 * (b1 - b0))
+        for b in range(b0, b1):
+            mm(at(bank, 64 * (b - b0), 64 * (b - b0) + 64), at(win, base + 128 * b, base + 128 * b + 128), at("WO", 0, 64), False)
 
-    def costs(K, ch, x, banks, slots=R):
-        b0, b1, _ = K[ch]
-        for s in slots:
-            for c0 in range(C0[x], C0[x] + CW[x], 512):
-                k, w = c0 // 512, min(512, CW[x])
-                lo = GB[x] + s * CW[x] + c0 - C0[x]
-                tt(("PR", lo, lo + w), ("GA", lo, lo + w), ("b%d" % k, c0 - 512 * k, c0 - 512 * k + w), A.mult)
-                sums("PR", wC, x, s, c0, c0 + w, banks[s // 2], 0, 8 * (b1 - b0), b0)
-                yield
+    def cost_sums(bank, b0, x, s):
+        w = at("WC0", 0, 64) if s == 0 else at("WC", 6 - 2 * s, 70 - 2 * s)
+        k = PLAN["sgrain"][x]
+        lo = gcol(CH[x][0], s - s % k)
+        for b in range(*CH[x]):
+            mm(at(bank, 64 * (b - b0), 64 * (b - b0) + 64), at("PR", gcol(b, s), gcol(b, s) + 128), w, False,
+               r=[("PR", lo, lo + 128 * k * (CH[x][1] - CH[x][0]))])
 
-    def fused_costs(K, ch, x, win, w0, w1, offs, banks):
-        b0, b1, _ = K[ch]
+    def costs(x, win, w0, w1, offs, bank, b0, fused, c, base):
+        c0, c1 = CH[x]
         for s in R:
-            lo = GB[x] + s * CW[x]
-            fused(lo, lo + CW[x], win, w0, w1, offs, C0[x], C0[x] + CW[x])
-            sums("PR", wC, x, s, C0[x], C0[x] + CW[x], banks[s // 2], 0, 8 * (b1 - b0), b0)
-            sums("PR", ("wKf", 8 * s, 8 * s + 8), x, s, C0[x], C0[x] + CW[x], banks[0], 256, 8 * (b1 - b0), b0)
-
-    def numbers(K, ch, x, banks):
-        b0, b1, _ = K[ch]
+            lo, n, k = gcol(c0, s), 128 * (c1 - c0), c0 // 4
+            if s in fused:
+                gather_times(at("PR", lo, lo + n), at(win, w0, w1), at(offs, lo // 16, (lo + n) // 16), at(c, base + 128 * c0, base + 128 * c1))
+            else:
+                m = min(PLAN["cgrain"][x], 4 - s - len([f for f in fused if f > s]))
+                if s % PLAN["cgrain"][x] == 0:
+                    gather("s", "GA", lo, lo + m * n, win, w0, w1, offs)
+                tt(at("PR", lo, lo + n), at("GA", lo, lo + n), at("b%d" % k, 128 * c0 - 512 * k, 128 * c1 - 512 * k), A.mult)
         for s in R:
-            sums("GA", ("wK", 8 * s, 8 * s + 8), x, s, C0[x], C0[x] + CW[x], banks[0], 256, 8 * (b1 - b0), b0)
+            cost_sums(bank, b0, x, s)
 
-    def bests(K, ch, x, bank):
-        b0, b1, _ = K[ch]
+    def slots_of(out, x, win, w0, w1, offs, q="vs"):
+        n, k = 128 * (CH[x][1] - CH[x][0]), PLAN["grain"][x]
+        for s in range(0, 4, k):
+            gather(q, out, gcol(CH[x][0], s), gcol(CH[x][0], s) + k * n, win, w0, w1, offs)
+
+    def best_of(bank, b0, b1):
+        n = b1 - b0
+        scan(at("MS", 32 * b0, 32 * b1), at("RS", 0, 32 * n), at(bank, 0, 64 * n, 2), A.add, A.min)
+        pieces("DB", [0, 1, 2], at("MS", 32 * b0 + 3, 32 * b1, 4), b0, b1)
+
+    def choice_of(bank, b0, b1, hi, lo):
+        n = b1 - b0
+        for s in (1, 2, 3):
+            tt(at("NF", 32 * b0 + s, 32 * b1, 4, s), at(bank, 2 * s, 64 * n, 8), at("MS", 32 * b0 + s - 1, 32 * b1, 4), A.is_ge)
+        scan(at("WD", 32 * b0, 32 * b1), at("NF", 32 * b0, 32 * b1), at(bank, 1, 64 * n, 2), A.mult, A.add)
+        dd = at("WD", 32 * b0 + 3, 32 * b1, 4)
+        cp("v", hi, dd)
+        tt(lo, dd, hi, A.subtract)
+
+    def test_start(bank, b0, b1, win, base):
+        clear(bank, 32 * (b1 - b0))
+        for b in range(b0, b1):
+            mm(at(bank, 32 * (b - b0), 32 * (b - b0) + 32), at(win, base + 128 * b, base + 128 * b + 128), at("WN", 0, 32), False,
+               w=[("less", 5 * b + 4, 5 * b + 5)])
+
+    def test_sums(bank, b0, x):
         for s in R:
-            sums("GB", E8, x, s, C0[x], C0[x] + CW[x], bank, 0, 8 * (b1 - b0), b0)
+            for b in range(*CH[x]):
+                o, l, whole = at(bank, 32 * (b - b0), 32 * (b - b0) + 32), at("GB", gcol(b, s), gcol(b, s) + 128), ("less", 5 * b + s, 5 * b + s + 1)
+                mm(o, l, at("WB", 3 - s, 35 - s), False, w=[whole])
+                mm(o, l, at("WE", 3 - s, 35 - s), False, r=[whole, ("less", 5 * b + 4, 5 * b + 5)])
 
-    def first_half(K, ch, banks):
-        b0, b1, o = K[ch]
-        n, h = 8 * (b1 - b0), o // 2
-        cp("v", ("t1", h, h + 2 * n), (banks[0], 0, 2 * n))
+    def collapses(o, bank, b0, b1):
+        n = b1 - b0
+        scan(at("MV", 32 * b0, 32 * b1), at("RS", 0, 32 * n), at(bank, 0, 32 * n), A.add, A.min)
+        tt(o, at("MV", 32 * b0 + 3, 32 * b1, 4), at("EV", 8 * b0, 8 * b1), A.is_gt)
 
-    def best_of(K, ch, banks, half_done=False):
-        b0, b1, o = K[ch]
-        n, h = 8 * (b1 - b0), o // 2
-        be = ("best", 8 * b0, 8 * b1)
-        if not half_done:
-            first_half(K, ch, banks)
-            yield
-        tt(("t2", h, h + 2 * n), (banks[1], 2 * n, 4 * n), ("t1", h, h + 2 * n), A.min)
-        yield
-        tt(be, ("t2", h, h + n), ("t2", h + n, h + 2 * n), A.min)
-        yield
-        yield from pieces("DB", BK, be, b0, b1)
+    def tables(z, src, lo, hi, bank, firsts):
+        o = at(bank, lo // 16, hi // 16)
+        for i, c in enumerate(firsts):
+            mm(o, Idh, at(c, lo // 16, hi // 16), i == 0)
+        for b in ALL:
+            mm(o, at(z, 15 - b, 143 - b), at(src, lo + b, hi, 16), False)
 
-    def choice(K, ch, banks, vk):
-        b0, b1, o = K[ch]
-        n, h = 8 * (b1 - b0), o // 2
-        c = (8 * b0, 8 * b1)
-        be = ("best",) + c
-        kk = (banks[0], 256, 256 + 4 * n)
+    OWN2, ALL2 = (H2, H2 + V + 16), (0, H2 + V + 16)
+
+    def window1(x):
+        return ((0, H1, H1 + NB)[min(x, 2)], H1 + V)
+
+    def blocks(xs):
+        return min(CH[x][0] for x in xs), max(CH[x][1] for x in xs)
+
+    def shares(b0, b1, banks):
+        n = (b1 - b0) // len(banks)
+        return [(b0 + n * i, b0 + n * i + n, bank) for i, bank in enumerate(banks)]
+
+    for bank, xs, back in PLAN["cost1"]:
+        b0, b1 = blocks(xs)
+        cost_start(bank, b0, b1, "W", H1)
+        for x in xs:
+            costs(x, "W", *window1(x), "L1", bank, b0, PLAN["fused1"].get(x, ()), "Ch", H1)
+        best_of(bank, b0, b1)
+        choice_of(bank, b0, b1, cls("DB", 3, b0, b1), cls("DB", 4, b0, b1))
+        for c0, c1, k in shares(b0, b1, back):
+            spread("DB", "Bw", H1, c0, c1, k)
+        if b0 == 0:
+            share("Bw", "B", H1, NB)
+
+    def move1(bank, b0, b1, k, tb):
+        c, n = at("XD", 16 * b0, 16 * b1, 2, 0), 16 * (b1 - b0)
+        collapses(c, bank, b0, b1)
+        tt(at("XD", 16 * b0 + 1, 16 * b1, 2, 1), at("WD", 32 * b0 + 3, 32 * b1, 4), c, A.mult)
+        mm(at(tb, 0, 128, 1, None, n), at("XD", 16 * b0, 16 * b1), Idh, True, True)
+        cp("vs", at("XT", 128 * k, 128 * k + 128, 1, None, n), at(tb, 0, 128, 1, None, n))
+
+    def planes(srcs, c0, bv, bs):
+        n = 128 * len(srcs)
+        for p, bank in ((1, bv), (0, bs)):
+            if p or bs != bv:
+                for i, (b, lo, k, rows) in enumerate(srcs):
+                    mm(at(bank, 128 * i, 128 * i + 128), at("Rep", 128 * k, 128 * k + 128, 1, None, rows), at(b, lo, lo + 128, 1, None, rows), True, True)
+            o = at("X", 2 * c0 + p, 2 * (c0 + n), 2, p)
+            if p:
+                tt(o, at(bank, 0, n), at("Ch", c0, c0 + n), A.mult)
+            else:
+                scaled("vs", o, at(bank, 0, n), RA)
+
+    def own_rows(k, b0, b1, c0, c1):
+        return [("XT", 128 * k, b - b0, 16 * (b1 - b0)) for b in range(c0, c1)]
+
+    def chose(lo, hi, bank):
+        tables("ZB", "GB", lo, hi, bank, ["GLh"])
+        t = at(bank, lo // 16, hi // 16)
+        tt(t, t, at("CT", lo // 16, hi // 16), A.is_equal)
+        tt(at("LC", lo // 16, hi // 16), t, at("P2", lo // 16, hi // 16), A.add)
+
+    for k, (bank, xs, back, lists) in enumerate(PLAN["test1"]):
+        b0, b1 = blocks(xs)
+        test_start(bank, b0, b1, "Bw", H1)
+        for x in xs:
+            slots_of("GB", x, "Bw", *window1(x), "L1")
+            test_sums(bank, b0, x)
+        k *= 2
+        move1(bank, b0, b1, k, "b1")
+        if b0 == 0:
+            share("XT", "X", 128 * k, PLAN["xw"], "XH")
+        if b1 - b0 > 4:
+            for c0, c1, j in shares(b0, b1, back):
+                planes(own_rows(k, b0, b1, c0, c1), H1 + 128 * c0, j, j)
+        else:
+            planes(own_rows(k, b0, b1, b0, b1), H1 + 128 * b0, back[0], back[-1])
+        chose(512 * b0, 512 * b1, lists)
+    ha, hb, hc, hd = PLAN["halo"]
+    planes([("XH", PLAN["xw"] * (i // 2), i % 2, 32) for i in range(4)], 0, ha, hb)
+    planes([("XH", 2 * PLAN["xw"], i, 32) for i in range(2)], 512, hc, hd)
+
+    def pulls(x):
+        c0, c1 = CH[x]
+        k = c0 // 4
         for s in R:
-            tt(("E", o + s * n, o + (s + 1) * n), (banks[s // 2], s * n, (s + 1) * n), be, A.is_equal)
-            yield
-        tt(("LT", o, o + 4 * n), kk, (vk, o, o + 4 * n), A.is_gt)
-        yield
-        tt(("X", o, o + 4 * n), kk, ("E", o, o + 4 * n), A.mult)
-        yield
-        tt(("X2", h, h + 2 * n), ("X", o, o + 2 * n), ("X", o + 2 * n, o + 4 * n), A.max)
-        yield
-        tt(("XI",) + c, ("X2", h, h + n), ("X2", h + n, h + 2 * n), A.max)
-        yield
-        ts(("CI",) + c, ("XI",) + c, 8191, None, A.bitwise_and)
-        yield
-        tt(("DD",) + c, ("CI",) + c, ("VC",) + c, A.subtract)
-        yield
-        cp("v", ("Dh",) + c, ("DD",) + c)
-        yield
-        tt(("Dl",) + c, ("DD",) + c, ("Dh",) + c, A.subtract)
-        yield
+            lo = gcol(c0, s)
+            mm(at("b%d" % k, 128 * c0 - 512 * k, 128 * c1 - 512 * k), at("PMh", 0, 128), at("GH", lo, lo + 128 * (c1 - c0)), False)
 
-    def move_of(K, ch, bank):
-        b0, b1, o = K[ch]
-        n, h = 8 * (b1 - b0), o // 2
-        c = (8 * b0, 8 * b1)
-        tt(("tt", o, o + 4 * n), (bank, 0, 4 * n), ("LT", o, o + 4 * n), A.add)
-        yield
-        tt(("tm", h, h + 2 * n), ("tt", o, o + 2 * n), ("tt", o + 2 * n, o + 4 * n), A.min)
-        yield
-        tt(("tn",) + c, ("tm", h, h + n), ("tm", h + n, h + 2 * n), A.min)
-        yield
-        tt(("cl",) + c, ("tn",) + c, ("best",) + c, A.is_gt)
-        yield
-        for k, d in ((0, "Dh"), (1, "Dl")):
-            kk, aa = dcol("DM", k, b0, b1)
-            op("v", lambda e: e.tensor_tensor(aa, ap(*(("cl",) + c)), ap(*((d,) + c)), A.mult), [("cl",) + c, (d,) + c], [kk])
-            yield
+    def own_sum(b0, b1, bank):
+        tt(at("PRS", 128 * b0, 128 * b1), at("Pb", 128 * b0, 128 * b1), c_bank(b0, b1), A.mult)
+        s_sum(bank, "wA", b0, b1)
+        cp("s", at("Qw", 128 * b0, 128 * b1), c_bank(b0, b1))
+        for x, (c0, c1) in enumerate(CH):
+            n = len(PLAN["fused2"].get(x, ()))
+            if b0 <= c0 < b1 and n:
+                scaled("s", at("Cf", 128 * c0, 128 * c1), c_bank(c0, c1), UP, LOW)
+        if any(b0 <= c0 < b1 and len(PLAN["fused2"].get(x, ())) < 4 for x, (c0, c1) in enumerate(CH)):
+            scaled(PLAN["fix"], c_bank(b0, b1), c_bank(b0, b1), UP, LOW)
 
-    def start_q1(i):
-        o, a = ("b%d" % i, 0, 512), ("Qw", 16 + 512 * i, 528 + 512 * i)
-        mm(o, T.PMf[:], ap(*a), True, False, [a, ("PMf", 0, 128)])
-        mm(o, T.PI[:], T.ON[:], False, False, [("PI", 0, 128), ("ON", 0, 512)])
-
-    def weights_of_tables():
-        for b in range(16):
-            o, a = T.TB[:, 129 * b:128 * b + 128:16], T.E8[:]
-            op("s", lambda e: e.activation(o, a, F.Copy), [E8], [("TB", 128 * b, 128 * b + 128)])
-
-    wC, E8 = ("wC", 0, 8), ("E8", 0, 8)
-    BK, MK = [0, 1, 2], [0, 1, 2, 3]
-
-    bH, bL, bA = ("b4", "b1"), ("b5", "b5"), ("b3", "b3")
-    gather("s", "GA", GB[3], GB[3] + 2048, "W", NB, V, "L1")
-    gather("s", "GA", GB[1], GB[2], "W", 0, V, "L1")
-    gather("s", "GA", GB[3] + 2048, 8192, "W", NB, V, "L1")
-    gather("s", "GA", 0, GB[1], "W", 0, HALO1, "L1")
-    weights_of_tables()
-    fused_costs(K1, "L", 2, "W", NB, V, "L1", bL)
-    run(costs(K1, "H", 3, bH, (0, 1)))
-    run(costs(K1, "L", 1, bL))
-    first_half(K1, "H", bH)
-    run(costs(K1, "H", 3, bH, (2, 3)), best_of(K1, "L", bL))
-    spread("DB", BK, "Bw", 0, 4, 8, "b6", "s")
-    spread("DB", BK, "Bw", 0, 2, 4, "b7", "s")
-    numbers(K1, "L", 1, bL)
-    run(best_of(K1, "H", bH, True))
-    spread("DB", BK, "Bw", 0, 8, 12, "b6", "s")
-    spread("DB", BK, "Bw", 0, 12, 16, "b7", "v")
-    run(costs(K1, "A", 0, bA))
-
-    gather("s", "GB", GB[3], GB[3] + 2048, "Bw", NB, V, "L1")
-    gather("s", "GB", GB[3] + 2048, 8192, "Bw", NB, V, "L1")
-    gather("s", "GB", GB[2], GB[3], "Bw", NB, V, "L1")
-    run(best_of(K1, "A", bA))
-    numbers(K1, "H", 3, bH)
-    numbers(K1, "A", 0, bA)
-    spread("DB", BK, "Bw", 0, 0, 2, "b6", "v")
-    share("Bw", "xB", 0, NB, V)
-    for k, j in ((2, 9), (3, 13)):
-        kk, aa = dcol("DM", k, 0, 16)
-        ks, sv = dcol("DS", j, 0, 16)
-        op("v", lambda e: e.tensor_copy(aa, sv), [ks], [kk])
-    gather("s", "GB", GB[1], GB[2], "Bw", 0, V, "L1")
-    run(choice(K1, "H", bH, "VK1"), choice(K1, "L", bL, "VK1"))
-    bests(K1, "H", 3, "b2")
-    bests(K1, "L", 2, "b0")
-    run(move_of(K1, "H", "b2"), choice(K1, "A", bA, "VK1"))
-    spread("DM", MK, "Mw", 0, 8, 12, "b6", "v")
-    spread("DM", MK, "Mw", 0, 12, 16, "b7", "v")
-    start_q1(2)
-    bests(K1, "L", 1, "b0")
-    gather("s", "GB", 0, GB[1], "Bw", 0, HALO1, "L1")
-    bests(K1, "A", 0, "b1")
-    run(move_of(K1, "L", "b0"))
-    spread("DM", MK, "Mw", 0, 4, 8, "b6", "s")
-    spread("DM", MK, "Mw", 0, 2, 4, "b7", "v")
-    run(move_of(K1, "A", "b1"))
-    spread("DM", MK, "Mw", 0, 0, 2, "b6", "v")
-    for i in (3, 0, 1):
-        start_q1(i)
-    share("Mw", "xM", 0, NB, V)
-
-    def tables(lo, hi, bank):
-        o = (bank, lo // 16, hi // 16)
-        for b in range(16):
-            l = ("TB", 128 * b, 128 * b + 128)
-            mm(o, ap(*l), T.GA[:, lo + b:hi:16], b == 0, b == 15, [l, ("GA", lo, hi)])
-
-    def pull_list(lo, hi, bank):
-        tt(("EQ", lo, hi), (bank, lo, hi), ("VT", lo, hi), A.is_equal)
-        yield
-        tt(("LQ", lo, hi), ("EQ", lo, hi), ("posq", lo, hi), A.mult)
-        yield
+    def around(o, x, n, cap):
+        ts(at("ma", 0, n), x, float(NC), float(V), A.is_lt, A.mult)
+        tt(at("mb", 0, n), x, at("ma", 0, n), A.add)
+        ts(o, at("mb", 0, n), float(-NC), cap, A.add, A.min)
 
     def next_list(lo, hi, bank):
-        ts(("EQ", lo, hi), ("EQ", lo, hi), -BIG, float(16 - own), A.mult, A.add)
-        yield
-        tt(("L2", lo, hi), (bank, lo, hi), ("EQ", lo, hi), A.add)
-        yield
+        tables("ZX", "GH", lo, hi, bank, ["GLh"])
+        ts(at("L2", lo // 16, hi // 16), at(bank, lo // 16, hi // 16), float(V), None, A.min)
 
-    def pull(x, s, c0, c1, stop):
-        k, lo = c0 // 512, GB[x] + s * CW[x] + c0 - C0[x]
-        a = ("GH", lo, lo + c1 - c0)
-        mm(("b%d" % k, c0 - 512 * k, c1 - 512 * k), T.PMh[:], ap(*a), False, stop, [a, ("PMh", 0, 128)])
+    cp("vs", cls("DS", 9, 0, 16), cls("DB", 5, 0, 16))
+    cp("vs", cls("DS", 13, 0, 16), cls("DB", 6, 0, 16))
+    for xs, sums, back, lists in PLAN["pull"]:
+        b0, b1 = blocks(xs)
+        start_c(b0, b1, False)
+        for x in xs:
+            slots_of("GH", x, "X", 2 * window1(x)[0], 2 * (H1 + V), "LC")
+            pulls(x)
+        own_sum(b0, b1, sums)
+        pieces("DS", SK, at(sums, 8 * b0, 8 * b1), b0, b1)
+        for c0, c1, k in shares(b0, b1, back):
+            spread("DS", "W1", H2, c0, c1, k, True)
+        if b0 >= 4:
+            next_list(512 * b0, 512 * b1, lists)
+        else:
+            share("W1", "W1" if b0 == 0 else "Wl", H2 + 128 * b0, 128 * (b1 - b0), None, NC, (), 128 * b0)
+            tables("ZX", "GH", 512 * b0, 512 * b1, lists, ["GLh", "FL"])
+            around(at("L2", 32 * b0, 32 * b1), at(lists, 32 * b0, 32 * b1), 32 * (b1 - b0), float(H2 + V))
+    for i, (a, e) in enumerate(STORES):
+        dma("y", T.q1[:, a:e], T.Qw[:, a:e], [("Qw", a, e), (PLAN["q1"], 0, 1)], [], "dq1", 12000.0 + 400 * i, 16 * (i + 1))
 
-    def q1_out(i):
-        cp("s", ("C1f", 512 * i, 512 * i + 512), ("b%d" % i, 0, 512))
+    for bank, xs, back in PLAN["cost2"]:
+        b0, b1 = blocks(xs)
+        cost_start(bank, b0, b1, "W1", H2)
+        for x in xs:
+            costs(x, "W1", *(ALL2 if x < 2 else OWN2), "L2", bank, b0, PLAN["fused2"].get(x, ()), "Cf", 0)
+        best_of(bank, b0, b1)
+        choice_of(bank, b0, b1, at("Dh", 8 * b0, 8 * b1), at("Dl", 8 * b0, 8 * b1))
+        for c0, c1, k in shares(b0, b1, back):
+            spread("DB", "B2w", H2, c0, c1, k)
+        if b0 < 4:
+            share("B2w", "B2" if b0 == 0 else "Bl", H2 + 128 * b0, 128 * (min(b1, 4) - b0), None, NC, (), 128 * b0)
 
-    def own_sum(i, bank):
-        tt(("PRS", 512 * i, 512 * i + 512), ("Pb", 512 * i, 512 * i + 512), ("b%d" % i, 0, 512), A.mult)
-        s_sum(bank, range(4 * i, 4 * i + 4))
+    def move2(bank, b0, b1):
+        c = at("cl", 8 * b0, 8 * b1)
+        collapses(c, bank, b0, b1)
+        for k, d in ((0, "Dh"), (1, "Dl")):
+            tt(cls("DM", k, b0, b1), c, at(d, 8 * b0, 8 * b1), A.mult)
 
-    OWN2 = 16 + V
-    gather("s", "GA", GB[3], GB[3] + 2048, "Mw", NB, V, "L1")
-    gather("s", "GA", GB[3] + 2048, 8192, "Mw", NB, V, "L1")
-    gather("s", "GA", 0, GB[1], "Mw", 0, HALO1, "L1")
-    gather("v", "GA", GB[2], GB[3], "Mw", NB, V, "L1")
-    gather("v", "GA", GB[1], GB[2], "Mw", 0, V, "L1")
-    tables(GB[2], GB[3], "b5")
-    tables(GB[3], GB[3] + 2048, "b4")
-    tables(GB[1], GB[2], "b7")
-    tables(GB[3] + 2048, 8192, "b6")
-    run(pull_list(128, 256, "b5"))
-    run(pull_list(256, 384, "b4"))
-    run(pull_list(64, 128, "b7"))
-    gather("s", "GH", GB[2], GB[3], "Qw", 0, OWN2, "LQ")
-    gather("v", "GH", GB[3], GB[3] + 2048, "Qw", 0, OWN2, "LQ")
-    tables(0, GB[1], "b7")
-    run(pull_list(384, 512, "b6"), pull_list(0, 64, "b7"))
-    gather("s", "GH", GB[1], GB[2], "Qw", 0, OWN2, "LQ")
-    gather("v", "GH", 0, GB[1], "Qw", 0, 16 + HALO1, "LQ")
-    run(next_list(384, 512, "b6"), next_list(128, 256, "b5"))
-    run(next_list(256, 384, "b4"))
-    cp("v", ("NF", 0, 128), ("b7", 0, 128))
-    for c in (0, 512):
-        for s in (2, 3):
-            lo = GB[3] + 1024 * s + c
-            gather("s", "GH", lo, lo + 512, "Qw", 0, OWN2, "LQ")
-    for s in R:
-        pull(2, s, 512, 1024, s == 3)
-    for s in (0, 1):
-        for c in (1024, 1536):
-            pull(3, s, c, c + 512, False)
-    for s in R:
-        pull(1, s, 256, 512, False)
-    for s in R:
-        pull(0, s, 0, 256, s == 3)
+    for b in ALL:
+        mm(at("b6", 0, 128), at("ZG", 15 - b, 143 - b), at("X", 2 * (H1 + b), 2 * (H1 + V), 32, 0), b == 0)
+    tt(at("GO", 0, 128), at("b6", 0, 128), at("CO", 0, 128), A.add)
+    around(at("LG", 0, 16), at("GO", 0, 16), 16, float(H2 + V))
+    cp("v", at("LG", 16, 128), at("GO", 16, 128))
+    for bank, xs, back in PLAN["test2"]:
+        b0, b1 = blocks(xs)
+        test_start(bank, b0, b1, "B2w", H2)
+        for x in xs:
+            slots_of("GB", x, "B2w", *(ALL2 if x < 2 else OWN2), "L2")
+            test_sums(bank, b0, x)
+        move2(bank, b0, b1)
+        for c0, c1, k in shares(b0, b1, back):
+            spread("DM", "M2w", H2, c0, c1, k)
+        if b0 == 0:
+            share("M2w", "M2", H2, NB, None, NC)
 
-    for s in (2, 3):
-        pull(3, s, 1024, 1536, s == 3)
-    own_sum(1, "b7")
-    own_sum(0, "b7")
-    q1_out(1)
-    for s in (2, 3):
-        pull(3, s, 1536, 2048, s == 3)
-    own_sum(2, "b7")
-    own_sum(3, "b7")
-    q1_out(2)
-    for i, b in enumerate(("b4", "b5", "b6")):
-        points(4 * i, 4 * i + 4, b)
-    number_to_place(("NF", 0, 128), 128, 16, 16 + V, NC)
-    run(pieces("DS", SK, ("b7", 0, 128), 0, 16))
-    ts(("EQ", 0, 128), ("EQ", 0, 128), -BIG, None, A.mult)
-    tt(("L2", 0, 128), ("mA", 0, 128), ("EQ", 0, 128), A.add)
-    spread("DS", DSK, "W1", 16, 0, 4, "b4", "s", True)
-    spread("DS", DSK, "W1", 16, 4, 8, "b5", "v", True)
-    share("W1", "xW1", 16, NC, 16 + V)
-    spread("DS", DSK, "W1", 16, 8, 12, "b6", "s", True)
-    points(12, 16, "b7")
-    spread("DS", DSK, "W1", 16, 12, 16, "b7", "v", True)
+    for lo, hi in ((256, 1024), (1024, 1536), (1536, 2048), (0, 256)):
+        gather("vs", "GA", lo, hi, "M2w", H2 if lo else 0, H2 + V, "LG")
+    clear("b6", 128)
+    for b in ALL:
+        mm(at("b6", 0, 128), at("ZM", 15 - b, 143 - b), at("GA", 128 * b, 128 * b + 128), False)
+    cp("v", at("GO", 0, 128), at("b6", 0, 128))
+    dma("y", T.goal[:], T.GO[:], [("GO", 0, 128)], [], "dgo", 2000.0)
 
-    bH, bL, bA = ("b4", "b1"), ("b6", "b6"), ("b5", "b5")
-    gather("s", "GA", GB[3], GB[3] + 2048, "W1", 0, OWN2, "L2")
-    gather("s", "GA", GB[3] + 2048, 8192, "W1", 0, OWN2, "L2")
-    gather("s", "GA", 0, GB[2], "W1", 0, HALO2, "L2")
-    fused_costs(K2, "L", 2, "W1", 0, OWN2, "L2", bL)
-    run(costs(K2, "H", 3, bH, (0, 1)))
-    first_half(K2, "H", bH)
-    run(costs(K2, "H", 3, bH, (2, 3)), best_of(K2, "L", bL))
-    spread("DB", BK, "B2w", 16, 4, 8, "b7", "s")
-    run(best_of(K2, "H", bH, True), costs(K2, "A", 0, bA))
-    spread("DB", BK, "B2w", 16, 8, 12, "b2", "s")
-    run(costs(K2, "A", 1, bA))
-    q1_out(0)
-    spread("DB", BK, "B2w", 16, 12, 16, "b7", "s")
-    q1_out(3)
-    for r in range(16):
-        i, j = r // 4, r % 4
-        k = 4 * min(i, j) + max(i, j)
-        dma("y", T.q1[r::16, :], T.C1f[k::16, :], [("C1f", 0, V)], [("q1#%d" % r, 0, V)], "dq1", 16 * (r + 1))
-    run(best_of(K2, "A", bA))
-    spread("DB", BK, "B2w", 16, 0, 4, "b7", "v")
-    share("B2w", "xB2", 16, NC, 16 + V)
-    numbers(K2, "H", 3, bH)
-    numbers(K2, "A", 0, bA)
-    numbers(K2, "A", 1, bA)
-    for b in range(16):
-        l = ("TB", 128 * b, 128 * b + 128)
-        mm(("b0", 0, 128), ap(*l), T.Mw[:, b:V:16], b == 0, b == 15, [l, ("Mw", 0, V)])
-
-    gather("s", "GB", GB[3], GB[3] + 2048, "B2w", 0, OWN2, "L2")
-    gather("s", "GB", GB[3] + 2048, 8192, "B2w", 0, OWN2, "L2")
-    gather("s", "GB", 0, GB[1], "B2w", 0, HALO2, "L2")
-    gather("s", "GB", GB[2], GB[3], "B2w", 0, OWN2, "L2")
-    run(choice(K2, "H", bH, "VK2"), choice(K2, "L", bL, "VK2"))
-    number_to_place(("b0", 0, 16), 16, 0, V, NB)
-    cp("v", ("LG", 0, 16), ("mA", 0, 16))
-    ts(("LG", 16, 128), ("b0", 16, 128), float(-own), None, A.add)
-    bests(K2, "H", 3, "b2")
-    run(choice(K2, "A", bA, "VK2"))
-    run(move_of(K2, "H", "b2"))
-    gather("v", "GB", GB[1], GB[2], "B2w", 0, HALO2, "L2")
-    bests(K2, "A", 0, "b0")
-    bests(K2, "A", 1, "b0")
-    run(move_of(K2, "A", "b0"))
-    spread("DM", MK, "M2w", 0, 0, 4, "b5", "v")
-    share("M2w", "xM2", 0, NB, V)
-    spread("DM", MK, "M2w", 0, 8, 12, "b7", "s")
-    spread("DM", MK, "M2w", 0, 12, 16, "b3", "s")
-    bests(K2, "L", 2, "b1")
-    run(move_of(K2, "L", "b1"))
-    spread("DM", MK, "M2w", 0, 4, 8, "b4", "v")
-
-    gather("s", "GA", 1024, 2048, "M2w", 0, V, "LG")
-    gather("v", "GA", 256, 1024, "M2w", 0, V, "LG")
-    gather("v", "GA", 0, 256, "M2w", 0, HALO1, "LG")
-    order = [8, 9, 10, 11, 12, 13, 14, 15, 2, 3, 4, 5, 6, 7, 0, 1]
-    for b in order:
-        l, a = ("TB", 128 * b, 128 * b + 128), ("GA", 128 * b, 128 * b + 128)
-        mm(("b6", 0, 128), ap(*l), ap(*a), b == order[0], b == order[-1], [l, a])
-    cp("v", ("GO", 0, 128), ("b6", 0, 128))
-    dma("y", T.goal[:], T.GO[:], [("GO", 0, 128)], [("goal", 0, V)], "dgo")
-
-    finish("y", [("dq1", 256), ("dgo", 16)])
-    finish("g", [("rl", sent[0])] + [("d%d" % i, 16) for i in range(9)] + [(x, 3 * ne) for x in EX])
+    issue([("y", [("dq1", 16 * len(STORES)), ("dgo", 16)]),
+           ("g", [("d%d" % i, 16) for i in range(1 + 2 * len(LOADS))] + [("l" + x, ne) for x in sent] + [("x" + x, 3 * ne) for x in sent])])

@@ -1,59 +1,70 @@
+import numpy as np
 from concourse.bass import DstId, RemoteDMATransfer
 from concourse.mybir import AluOpType as A, ActivationFunctionType as F
 
 N, V, NB, NC = 4, 2048, 256, 512
 H1, H2 = 3 * NB, 3 * NC
-CH = [(0, 2), (2, 4), (4, 8), (8, 12), (12, 14), (14, 16)]
-LOADS = [(0, 2), (2, 4), (4, 8), (8, 12), (12, 14), (14, 16)]
-STORES = [(0, 1024), (1024, 2048)]
+XR, XS, XB, XH, XE = H1 + NB, H1 + V, H1 + 2 * V - NB, H1 + 2 * V, 2 * (H1 + V)
 PLAN = dict(
+    ch=[(0, 2), (2, 4), (4, 8), (8, 12), (12, 14), (14, 16)],
+    qload=[(0, 2), (2, 4), (4, 8), (8, 12), (12, 14), (14, 16)], pload=[(0, 4), (4, 8), (8, 12), (12, 16)], nbat=99, lq="ys", out="s",
+    qdma=[(0, 2), (2, 4), (4, 8), (8, 12), (12, 14), (14, 16)],
+    sum0=[(0, 2, "b5", ("b7",)), (2, 4, "b4", ("b6",)), (4, 8, "b5", ("b7",)), (8, 12, "b4", ("b6",)), (12, 16, "b5", ("b0", "b7"))],
     fused1={0: (0, 1, 2, 3), 1: (0, 1, 2, 3), 5: (3,)}, fused2={0: (0, 1, 2, 3), 1: (0, 1, 2, 3), 5: (3,)},
     cost1=[("b4", (1, 0), ("b6",)), ("b5", (2, 3), ("b7", "b6")), ("b0", (4, 5), ("b4", "b1"))],
     cost2=[("b4", (1, 0), ("b6",)), ("b5", (2, 3), ("b7", "b6")), ("b0", (4, 5), ("b4", "b1"))],
-    test1=[("b2", (1, 0), ("b5",), "b4"), ("b3", (2, 3), ("b6", "b7"), "b0"), ("b2", (4, 5), ("b5", "b4"), "b7")],
-    halo=("b5", "b5", "b6", "b6"),
-    pull=[((1,), "b4", ("b6",), "b5"), ((0,), "b4", ("b6",), "b7"), ((2,), "b4", ("b6",), "b5"), ((3,), "b4", ("b6",), "b7"),
-          ((4, 5), "b4", ("b6", "b7"), "b5")],
-    test2=[("b2", (0,), ("b7",)), ("b3", (1, 2), ("b5", "b0", "b7")), ("b2", (3, 4), ("b1", "b7", "b5")), ("b3", (5,), ("b0",))],
-    margin=1000.0, q1="sentW1", turns=4, far=2500.0, rate=100.0, once=3000.0, firstx="W", lrate=250.0, gl="s", plain=(), soon=(), cross=350.0, ago=1e9, xw=128, fix="s",
-    grain=(1, 1, 1, 1, 1, 1), cgrain=(1, 1, 1, 1, 1, 1), sgrain=(1, 1, 1, 1, 1, 1),
+    test1=[("b2", (1, 0), ("b5",), "b4", False), ("b3", (2, 3), ("b6", "b7"), "b0", True), ("b2", (4, 5), ("b5", "b4"), "b7", False)],
+    halo=("b5", "b6"),
+    pull=[((1,), "b4", ("b4",), "b5"), ((0,), "b6", ("b6",), "b7"), ((2,), "b4", ("b4",), "b5"), ((3,), "b6", ("b6",), "b7"),
+          ((4, 5), "b0", ("b4", "b0"), "b5")],
+    test2=[("b2", (0,), ("b7",)), ("b3", (1, 2), ("b5", "b0")), ("b4", (3, 4), ("b1", "b7")), ("b2", (5,), ("b0",))],
+    last=((256, 1024), (1024, 1536), (1536, 2048), (0, 256)), stores=[(0, 1024, "W1"), (1024, 2048, "W1")], later=(),
+    grain=(2, 2, 1, 1, 2, 2), margin=1000.0, turns=4, far=2100.0, rate=150.0, once=2800.0, lrate=330.0, near=1900.0, cross=300.0,
+    slow=1.0, pick=1.56, fix="s", dear=1.0, rep=("b6", "b7"), seed=0, tries=0, shake=600.0,
+    flow=0, step=100.0, soon=300.0, idle=2.0, spare=1000.0, mend=26000, heat=60.0, pull_in=0.3, roam=0.3, early={}, stag=0.0,
+    cases=[(1.0, dict(v=1.0, s=1.0, p=1.0, g=1.0), 1.0, 250.0, 1.0, 1.0), (1.28, dict(v=1.4, s=1.1, p=1.1, g=1.3), 1.0, 300.0, 1.1, 1.4),
+           (1.17, dict(v=1.05, s=1.05, p=1.45, g=1.5), 0.85, 300.0, 1.0, 1.2), (1.22, dict(v=1.2, s=1.2, p=1.2, g=1.2), 0.8, 420.0, 1.4, 2.0)],
+    opens="W", wary=1.2, turned=("ZB", "ZX"),
 )
+FOUND = {}
 NONE = float(1 << 24)
 FAR = 32768.0
 R16, R8 = 1.5 * 2.0 ** 39, 1.5 * 2.0 ** 31
 EPS = 2.0 ** -14
-CYC, PE, PICK, HOP = 0.83, 0.42, 1.56, 130.0
+LIFT = 1024.0
+HOP = 115.0
 
 SCRATCH = {}
 for _n, _w, _t in (
-        ("Qw", V, "float32"), ("Pb", V, "bfloat16"), ("nbi", 512, "int32"), ("Cf", V, "float32"), ("Ch", H1 + V, "float16"),
+        ("Qw", V, "float32"), ("Pb", V, "bfloat16"), ("Cf", V, "float32"), ("Ch", H1 + V, "float16"),
         ("W", H1 + V, "bfloat16"), ("W1", H2 + V + 16, "bfloat16"), ("Bw", H1 + V, "bfloat16"), ("B2w", H2 + V + 16, "bfloat16"),
-        ("M2w", H2 + V, "bfloat16"), ("X", 2 * (H1 + V), "float32"),
-        ("L1", 512, "uint16"), ("LC", 512, "uint16"), ("L2", 512, "uint16"), ("LG", 128, "uint16"),
-        ("GL", 512, "float32"), ("GLh", 512, "float16"), ("P2", 512, "float16"), ("FL", 128, "float16"), ("CT", 512, "float32"),
-        ("CO", 128, "float32"), ("NI", 64, "int32"), ("IX", 64, "int32"), ("CA", 64, "int32"), ("ma", 128, "float32"),
-        ("mb", 128, "float32"), ("GA", 8192, "bfloat16"), ("GB", 8192, "bfloat16"), ("GH", 8192, "float16"), ("PR", 8192, "float32"),
-        ("PRS", V, "float32"), ("DS", V, "bfloat16"), ("DB", V, "bfloat16"), ("DM", V, "bfloat16"), ("ON", 128, "bfloat16"),
-        ("ZZ", 128, "bfloat16"), ("Id", 128, "bfloat16"), ("Idh", 128, "float16"), ("PM", 128, "bfloat16"), ("PMh", 128, "float16"),
-        ("E8", 8, "bfloat16"), ("E32", 32, "bfloat16"), ("wA", 8, "float32"), ("wS", 8, "float32"), ("WC0", 64, "float32"),
-        ("WC", 72, "float32"), ("WO", 64, "bfloat16"), ("WB", 40, "bfloat16"), ("WE", 40, "bfloat16"), ("WN", 32, "bfloat16"),
-        ("ZB", 144, "bfloat16"), ("ZX", 144, "float16"), ("ZG", 144, "float32"), ("ZM", 144, "bfloat16"), ("RZ", 240, "float16"),
-        ("Rep", 1024, "float16"), ("RS", 256, "bfloat16"), ("ci", 8, "int32"), ("cf", 32, "float32"), ("VC", 128, "float32"),
-        ("GC", 128, "float32"), ("EV", 128, "float32"), ("MS", 512, "float32"), ("NF", 512, "bfloat16"), ("WD", 512, "float32"),
+        ("M2w", H2 + V, "bfloat16"), ("X", XE, "float32"), ("L1", 512, "uint16"), ("LC", 512, "uint16"), ("L2", 512, "uint16"),
+        ("LG", 128, "uint16"), ("GL", 512, "float16"), ("PL", 512, "float32"), ("PO", 128, "float32"), ("FL", 128, "float16"),
+        ("NCT", 512, "bfloat16"), ("CO", 128, "bfloat16"), ("NI", 64, "int32"), ("IX", 64, "int32"),
+        ("CA", 64, "int32"), ("ma", 128, "float32"), ("mb", 128, "float32"), ("GA", 8192, "bfloat16"), ("GB", 8192, "bfloat16"),
+        ("GH", 8192, "float16"), ("PR", 8192, "float32"), ("PRS", V, "float32"), ("DS", V, "bfloat16"), ("DB", V, "bfloat16"),
+        ("ON", 128, "bfloat16"), ("ZZ", 128, "bfloat16"), ("Id", 128, "bfloat16"), ("Idh", 128, "float16"), ("PM", 128, "bfloat16"),
+        ("PMh", 128, "float16"), ("TT", 512, "float16"), ("wA", 8, "float32"), ("WC01", 64, "float32"),
+        ("WC02", 64, "float32"), ("WC1", 72, "float32"), ("WC2", 72, "float32"), ("WO1", 64, "bfloat16"), ("WO2", 64, "bfloat16"),
+        ("WB", 40, "bfloat16"), ("WE", 40, "bfloat16"), ("WN", 32, "bfloat16"), ("ZB", 144, "bfloat16"), ("ZX", 144, "float16"),
+        ("ZM", 144, "bfloat16"), ("RZ", 240, "float16"), ("Rep", 1024, "float16"), ("RS", 256, "bfloat16"), ("ci", 8, "int32"),
+        ("cf", 40, "float32"), ("EV", 128, "float32"), ("MS", 512, "float32"), ("NF", 512, "bfloat16"), ("WD", 512, "float32"),
         ("MV", 512, "float32"), ("r8", 128, "float32"), ("cl", 128, "bfloat16"), ("XD", 256, "float16"), ("XT", 768, "float16"),
-        ("XH", 768, "float16"), ("GO", 128, "float32"), ("Dh", 128, "bfloat16"), ("Dl", 128, "bfloat16")):
+        ("XF", 384, "float16"), ("GO", 128, "float32"), ("Dh", 128, "bfloat16"), ("Dl", 128, "bfloat16"), ("PMq", 128, "float16"),
+        ("PMp", 128, "float16"), ("WU", 72, "float32"), ("WS0", 64, "bfloat16"), ("WS", 72, "bfloat16"), ("EG", 128, "bfloat16")):
     SCRATCH[_n] = ("sbuf", [128, _w], _t)
+SCRATCH["nbi"] = ("sbuf", [128, 4, 128], "int32")
 for _i in range(8):
     SCRATCH["b%d" % _i] = ("psum", [128, 512], "float32")
 EX = ["C", "W", "B", "X", "W1", "Wl", "B2", "Bl", "M2"]
-SEMAPHORES = ["v", "s", "p", "g", "dq1", "dgo"] + ["d%d" % i for i in range(1 + 2 * len(LOADS))] + ["x" + e for e in EX] + ["l" + e for e in EX]
+SEMAPHORES = ["v", "s", "p", "g"] + [k + e for k in "xl" for e in EX] + ["d%d" % i for i in range(40)]
 
 
 def make(g, T):
     QO = {"v": g.vector, "s": g.scalar, "p": g.tensor, "y": g.sync, "g": g}
-    calls, acc = [], {}
+    calls, acc, marks = [], {}, []
 
-    def call(ways, r, w, tok=None, late=0.0, behind=None, first=0.0, group=None, stop=None):
+    def call(ways, r, w, tok=None, late=0.0, behind=None, first=0.0, group=None, stop=None, move=0.0, picks=False):
         before = {}
         for lst, wr in ((r, False), (w, True)):
             for key, lo, hi in [x[:3] for x in lst]:
@@ -74,14 +85,23 @@ def make(g, T):
                 if wr and not group:
                     acc[b] = [a for a in acc.get(b, []) if not ((part is None or part == a[1]) and lo <= a[2] and a[3] <= hi)]
                 acc.setdefault(b, []).append((i, part, lo, hi, wr))
-        calls.append(dict(ways=ways, before=before, tok=tok, late=late, behind=behind, first=first, group=group, stop=stop))
+        calls.append(dict(ways=ways, before=before, tok=tok, late=late, behind=behind, first=first, group=group, stop=stop, move=move,
+                          picks=picks))
         return i
 
     def must_wait(a, qa, c, qc, k):
         return a["tok"] is not None or c["tok"] is not None or qa != qc or (k == 2 and qc != "p")
 
+    def room(spans, t, ns):
+        for a, e in spans:
+            if t + ns <= a:
+                break
+            if e > t:
+                t = e
+        return t
+
     def sweep(order, links, back):
-        busy = {q: [] for q in QO}
+        busy = {q: [] for q in list(QO) + ["m"]}
         for i in order:
             c = calls[i]
             best = None
@@ -90,17 +110,22 @@ def make(g, T):
                 for j, k in links[i]:
                     a = calls[j]
                     if must_wait(c, q, a, a["q"], k) if back else must_wait(a, a["q"], c, q, k):
-                        t = max(t, a["end"] + (HOP if q == a["q"] else PLAN["cross"]))
+                        t = max(t, a["end"] + (HOP if q == a["q"] else PLAN["cross"] if (a["q"] if back else q) else 0.0))
                     else:
                         t = max(t, a["end"])
-                t += c["late"] if back else 0.0
-                for a, e in busy.get(q, []):
-                    if t + ns <= a:
-                        break
-                    t = max(t, e)
-                if best is None or t + ns < best[0]:
-                    best = (t + ns, q, t)
-            c["q"], c["at"], c["end"] = best[1], best[2], best[0] + (0.0 if back else c["late"])
+                t += c["late"] + c["move"] if back else 0.0
+                t = room(busy.get(q, []), t, ns)
+                worth = t + ns * (PLAN["dear"] if q == "v" else 1.0)
+                if best is None or worth < best[3]:
+                    best = (t + ns, q, t, worth)
+            c["q"], c["at"], c["end"] = best[1], best[2], best[0]
+            if c["move"] and not back:
+                t = room(busy["m"], best[2] + 0.7 * c["late"], c["move"])
+                busy["m"].append((t, t + c["move"]))
+                busy["m"].sort()
+                c["end"] = t + c["move"] + 0.3 * c["late"]
+            elif not back:
+                c["end"] += c["late"]
             if best[1]:
                 busy[best[1]].append((best[2], best[0]))
                 busy[best[1]].sort()
@@ -113,21 +138,230 @@ def make(g, T):
         way = [0.0] * n
         for i in range(n - 1, -1, -1):
             c = calls[i]
-            way[i] += c["late"] + min([x[1] for x in c["ways"].values()] or [0.0])
+            way[i] += c["late"] + c["move"] + min([x[1] for x in c["ways"].values()] or [0.0])
             for j, k in before[i]:
                 after[j].append((i, k))
-                calls[j]["first"] = max(calls[j]["first"], c["first"])
                 one = k == 1 and list(calls[j]["ways"]) == list(c["ways"]) or list(calls[j]["ways"]) == list(c["ways"]) == ["p"]
                 way[j] = max(way[j], way[i] + (1.0 if one else HOP))
-        best = None
-        for turn in range(PLAN["turns"]):
-            order = sorted(range(n), key=lambda x: (-way[x] - calls[x]["first"], x))
-            t = sweep(order, before, False)
-            if best is None or t < best[0]:
-                best = (t, order)
-            sweep(sorted(range(n), key=lambda x: (-calls[x]["end"], -x)), after, True)
-            way = [c["end"] for c in calls]
-        sweep(best[1], before, False)
+        if PLAN["flow"] and "order" not in FOUND:
+            way = [-PLAN["step"] * i for i in range(n)]
+            for i in range(marks[0] - 1, -1, -1):
+                way[i] = max([way[j] for j, k in after[i]] or [0.0]) + PLAN["soon"]
+            flow(way, before, after)
+            FOUND["order"], FOUND["time"] = mend(before, after)
+        if "order" not in FOUND:
+            for c in calls:
+                if c["move"] and "g" in c["ways"]:
+                    c["late"], c["move"] = c["late"] * PLAN["wary"], c["move"] * PLAN["wary"]
+            best, rng = None, np.random.default_rng(PLAN["seed"])
+            for turn in range(PLAN["turns"] + PLAN["tries"]):
+                if turn >= PLAN["turns"]:
+                    way = list(best[2] + PLAN["shake"] * rng.random() * rng.standard_normal(n))
+                order = ready(sorted(range(n), key=lambda x: (-way[x] - calls[x]["first"], x)), before)
+                sweep(order, before, False)
+                t = sum(replay(before, *x) / x[0] for x in PLAN["cases"])
+                if best is None or t < best[0]:
+                    best = (t, order, np.array(way))
+                if turn < PLAN["turns"]:
+                    sweep(ready(sorted(range(n), key=lambda x: (-calls[x]["end"], -x)), after), after, True)
+                    way = [c["end"] for c in calls]
+            sweep(best[1], before, False)
+            for c in calls:
+                if c["move"] and "g" in c["ways"]:
+                    c["late"], c["move"] = c["late"] / PLAN["wary"], c["move"] / PLAN["wary"]
+            FOUND["order"], FOUND["time"] = mend(before, after)
+        for k, (i, q) in enumerate(FOUND["order"]):
+            calls[i]["q"], calls[i]["at"] = q, float(k)
+
+    def mend(before, after):
+        n, names = len(calls), list(QO) + [None]
+        rng = np.random.default_rng(PLAN["seed"])
+        seq = sorted(range(n), key=lambda x: (calls[x]["at"], x))
+        qs = [names.index(c["q"]) for c in calls]
+        tok = [c["tok"] is not None for c in calls]
+        pre = [[(j, tok[j] or tok[i], k == 2) for j, k in before[i]] for i in range(n)]
+        late, move = [c["late"] for c in calls], [c["move"] for c in calls]
+        cost = [[[c["ways"][q][1] * (1.0 if c["tok"] else slow[q]) * (picks if c["picks"] else 1.0) if q in c["ways"] else 0.0 for q in names]
+                 for c in calls] for whole, slow, picks, wake, near, far in PLAN["cases"]]
+
+        def times(seq, qs, case, a, old):
+            wake, near, far = PLAN["cases"][case][3:]
+            ns, a = cost[case], a // 32
+            end, why, marks = list(old[1]), list(old[2]), old[3][:a + 1]
+            free, last = list(marks[a][0]), list(marks[a][1])
+            for k in range(32 * a, n):
+                if k % 32 == 0 and k > 32 * a:
+                    marks.append((list(free), list(last)))
+                i = seq[k]
+                q = qs[i]
+                t = free[q] if q < 5 else 0.0
+                w = last[q]
+                for j, dma, read in pre[i]:
+                    e = end[j]
+                    if e + wake > t:
+                        if q < 5:
+                            if qs[j] != q:
+                                e += wake
+                            elif dma or (read and q != 2):
+                                e += wake * 0.45
+                        if e > t:
+                            t, w = e, j
+                why[i], last[q] = w, i
+                free[q] = e = t + ns[i][q]
+                if move[i]:
+                    lag = far if q == 4 else near
+                    free[6] = max(free[6], t + 0.7 * lag * late[i]) + lag * move[i]
+                    end[i] = free[6] + 0.3 * lag * late[i]
+                else:
+                    end[i] = e + late[i]
+            return max(end), end, why, marks
+
+        def judge(seq, qs, a, old):
+            xs = [times(seq, qs, k, a, old[k]) for k in range(len(cost))]
+            return sum((x[0] + PLAN["pull_in"] * sum(x[1]) / n) / PLAN["cases"][k][0] for k, x in enumerate(xs)), xs
+
+        def ahead(seq, a, b):
+            i, p = seq[b], seq[a]
+            need = {i}
+            for x in reversed(seq[a:b + 1]):
+                if x in need:
+                    need.update(j for j, d, r in pre[x])
+            if p in need or calls[p]["first"] > 1e8:
+                return None
+            mid = seq[a:b + 1]
+            return seq[:a] + [x for x in mid if x in need] + [x for x in mid if x not in need] + seq[b + 1:]
+
+        now, xs = judge(seq, qs, 0, [(0.0, [0.0] * n, [-1] * n, [([0.0] * 7, [-1] * 7)])] * len(cost))
+        best = (now, seq, qs)
+        for turn in range(PLAN["mend"]):
+            t, end, why, marks = xs[int(rng.integers(len(xs)))]
+            i, chain = end.index(t), []
+            while i >= 0:
+                chain.append(i)
+                i = why[i]
+            i = chain[int(rng.integers(len(chain)))] if rng.random() > PLAN["roam"] else int(rng.integers(n))
+            s2, q2, a, p = seq, qs, seq.index(i), why[i]
+            if len(calls[i]["ways"]) > 1 and rng.random() < 0.4:
+                q2 = list(qs)
+                q2[i] = 1 - qs[i]
+                near = [k for k in range(max(0, a - 40), min(n, a + 40)) if qs[seq[k]] == q2[i] and len(calls[seq[k]]["ways"]) > 1]
+                if near and rng.random() < 0.5:
+                    k = near[int(rng.integers(len(near)))]
+                    q2[seq[k]], a = qs[i], min(a, k)
+            elif p >= 0 and qs[p] == qs[i] and all(j != p for j, d, r in pre[i]) and rng.random() < 0.8:
+                while rng.random() < 0.4 and why[p] >= 0 and qs[why[p]] == qs[i]:
+                    p = why[p]
+                a, b = seq.index(p), a
+                s2 = ahead(seq, a, b)
+            else:
+                nxt = [k for k in range(a + 1, min(n, a + 80)) if qs[seq[k]] == qs[i]][:8]
+                s2 = ahead(seq, a, nxt[int(rng.integers(len(nxt)))]) if nxt else None
+            if s2 is None:
+                continue
+            t2, x2 = judge(s2, q2, a, xs)
+            if t2 < now + PLAN["heat"] * (1 - turn / PLAN["mend"]) * -np.log(rng.random()):
+                seq, qs, now, xs = s2, q2, t2, x2
+                if now < best[0]:
+                    best = (now, seq, qs)
+        xs = judge(best[1], best[2], 0, xs)[1]
+        return [(i, names[best[2][i]]) for i in best[1]], sum(x[0] / PLAN["cases"][k][0] for k, x in enumerate(xs))
+
+    def behind(before, after, placed):
+        n = len(calls)
+        way, nxt = [0.0] * n, {}
+        for i in sorted(range(n), key=lambda x: (-calls[x]["at"], -x)) if placed else range(n - 1, -1, -1):
+            c = calls[i]
+            q = c["q"] if placed else min(c["ways"], key=lambda x: c["ways"][x][1]) if c["ways"] else None
+            ns, t = c["ways"][q][1] if q else 0.0, 0.0
+            for j, k in after[i]:
+                d = calls[j]
+                q2 = d["q"] if placed else q if q in d["ways"] else list(d["ways"] or [None])[0]
+                t = max(t, way[j] + ((HOP if q == q2 else PLAN["cross"]) if q2 and must_wait(c, q, d, q2, k) else 0.0))
+            way[i] = ns + max(t + c["late"] + c["move"], way[nxt[q]] if q in nxt else 0.0)
+            if placed and q:
+                nxt[q] = i
+        return way
+
+    def flow(way, before, after):
+        left = [len(b) for b in before]
+        free = {q: 0.0 for q in list(QO) + ["m"]}
+        open_ = {q: {} for q in QO}
+
+        def offer(i):
+            c = calls[i]
+            for q in c["ways"] or [None]:
+                t = 0.0
+                for j, k in before[i]:
+                    a = calls[j]
+                    t = max(t, a["end"] + ((HOP if q == a["q"] else PLAN["cross"]) if q and must_wait(a, a["q"], c, q, k) else 0.0))
+                if q:
+                    open_[q][i] = t
+                else:
+                    c["q"], c["at"], c["end"] = None, t, t
+                    done(i)
+
+        def done(i):
+            for j, k in after[i]:
+                left[j] -= 1
+                if not left[j]:
+                    offer(j)
+
+        for i in [i for i, x in enumerate(left) if not x]:
+            offer(i)
+        while any(open_.values()):
+            picks = []
+            for q, o in open_.items():
+                if o:
+                    t0 = free[q]
+                    i = max(o, key=lambda x: (way[x] + calls[x]["first"] - PLAN["idle"] * max(0.0, o[x] - t0)
+                                              - (PLAN["spare"] if q == "v" and len(calls[x]["ways"]) > 1 else 0.0), -x))
+                    picks.append((max(t0, o[i]) + (1.0 if q == "v" else 0.0), q, i))
+            t, q, i = min(picks)
+            c = calls[i]
+            t = max(free[q], open_[q][i])
+            for x in c["ways"]:
+                del open_[x][i]
+            free[q] = t + c["ways"][q][1]
+            c["q"], c["at"], c["end"] = q, t, free[q] + c["late"]
+            if c["move"]:
+                free["m"] = max(free["m"], t + 0.7 * c["late"]) + c["move"]
+                c["end"] = free["m"] + 0.3 * c["late"]
+            done(i)
+
+    def replay(before, whole, slow, picks, wake, near, far):
+        free, end = {}, {}
+        for i in sorted(range(len(calls)), key=lambda x: (calls[x]["at"], x)):
+            c = calls[i]
+            q = c["q"]
+            t = t0 = free.get(q, 0.0) if q else 0.0
+            for j, k in before[i]:
+                hop = must_wait(calls[j], calls[j]["q"], c, q, k) and q
+                t = max(t, end[j] + ((wake * 0.45 if q == calls[j]["q"] else wake) if hop else 0.0))
+            ns = c["ways"][q][1] * (slow[q] if c["tok"] is None else 1.0) * (picks if c["picks"] else 1.0) if q else 0.0
+            free[q] = t + ns
+            if c["move"]:
+                lag = far if q == "g" else near
+                free["m"] = max(free.get("m", 0.0), t + 0.7 * lag * c["late"]) + lag * c["move"]
+                end[i] = free["m"] + 0.3 * lag * c["late"]
+            else:
+                end[i] = t + ns + c["late"]
+        return max(end.values())
+
+    def ready(order, links):
+        seen, out = set(), []
+        for i in order:
+            todo = [i]
+            while todo:
+                j = todo[-1]
+                left = [k for k, x in links[j] if k not in seen]
+                if left:
+                    todo.extend(left)
+                else:
+                    todo.pop()
+                    if j not in seen:
+                        seen.add(j)
+                        out.append(j)
+        return out
 
     def issue(ends):
         place()
@@ -139,7 +373,7 @@ def make(g, T):
             c["stop"][0] = True
         cnt = {"v": 0, "s": 0, "p": 0, "g": 0}
         known = {q: {} for q in QO}
-        clk, ends_of = {}, {q: [] for q in "vsp"}
+        clk = {}
         for i in sorted(range(len(calls)), key=lambda x: (calls[x]["at"], x)):
             c = calls[i]
             q = c["q"]
@@ -151,8 +385,6 @@ def make(g, T):
             for j, kind in c["before"].items():
                 ch, m = calls[j]["done"]
                 if must_wait(calls[j], calls[j]["q"], c, q, kind) and k.get(ch, 0) < m:
-                    while ch in ends_of and ch != q and m < cnt[ch] and ends_of[ch][m] + PLAN["ago"] <= c["at"]:
-                        m += 1
                     todo[ch] = max(m, todo.get(ch, 0))
             items = sorted(todo.items())
             for ch, m in items:
@@ -163,29 +395,30 @@ def make(g, T):
                     k[c3] = max(m3, k.get(c3, 0))
             x = c["ways"][q][0](QO[q])
             if c["tok"] is None:
-                cnt[q] += 1
-                ends_of.get(q, []).append(c["end"])
+                for y in x if q == "p" else [x]:
+                    cnt[q] += 1
+                    y.then_inc(T.sem[q], 1)
                 c["done"] = (q, cnt[q])
-                x.then_inc(T.sem[q], 1)
             else:
                 c["done"] = c["tok"]
             clk[c["done"]] = dict(k)
             clk[c["done"]][c["done"][0]] = c["done"][1]
-        for q, toks in ends:
-            for ch, m in toks + ([x for x in cnt.items()] if q == "g" else []):
-                QO[q].wait_ge(T.sem[ch], m)
+        for ch, m in list(cnt.items()) + ends:
+            (g.sync if ch[0] == "d" else g).wait_ge(T.sem[ch], m)
 
-    return call, issue
+    return call, issue, lambda: marks.append(len(calls))
 
 
 def rank_program(g, core, T, topo):
     rank = T.rank_of(core)
     if rank is None:
         return
-    call, issue = make(g, T)
+    call, issue, mark = make(g, T)
     own = V * rank
     others = [c for c in T.cores if c != core]
-    R, ALL = range(4), range(16)
+    R, ALL, CH = range(4), range(16), PLAN["ch"]
+    CYC, PE, PICK = 0.83 * PLAN["slow"], 0.42 * PLAN["slow"], PLAN["pick"]
+    ends = []
 
     def at(b, lo, hi, step=1, part=None, rows=128):
         return (b if part is None else "%s#%d" % (b, part), lo, hi, T[b][0:rows, lo:hi:step], b, len(range(lo, hi, step)))
@@ -197,7 +430,7 @@ def rank_program(g, core, T, topo):
         return CYC * max(64, n / 2 if all(kind(x) in ("bfloat16", "float16", "uint16") for x in xs) else n)
 
     def act(n):
-        return CYC * (100 + n)
+        return CYC * (140 + n)
 
     def pick(ways, q):
         return {k: x for k, x in ways.items() if k in q}
@@ -231,31 +464,40 @@ def rank_program(g, core, T, topo):
                     "s": (lambda e: e.activation(o[3], a[3], F.Identity, scale=col[3]), act(o[5]))}
         call(pick(ways, q), [a, col] + ([bias] if bias else []), [o])
 
-    opened = {}
+    opened, run = {}, []
 
-    def mm(o, lt, rh, start, stop=None, r=(), w=()):
+    def mm(o, lt, rh, start, stop=None, r=(), w=(), more=False):
         ns = PE * max(min(64, lt[5]), rh[5]) * (4 if kind(lt) == "float32" else 1)
         if start:
             opened[o[4]] = opened.get(o[4], 0) + 1
         flag = [bool(stop)]
-        call({"p": (lambda e: e.matmul(o[3], lt[3], rh[3], start, flag[0]), ns)}, [lt, rh] + list(r), [o] + list(w),
-             group=None if start or stop is not None else (o[4], opened[o[4]]), stop=flag)
+        run.append((lambda e: e.matmul(o[3], lt[3], rh[3], start, flag[0]), ns, [lt, rh] + list(r), [o] + list(w),
+                    None if start or stop is not None else (o[4], opened[o[4]]), flag))
+        if not more:
+            xs = list(run)
+            run.clear()
+            call({"p": (lambda e: [x[0](e) for x in xs], sum(x[1] for x in xs))}, sum([x[2] for x in xs], []), sum([x[3] for x in xs], []),
+                 group=xs[-1][4], stop=flag)
 
     def fill(o, x):
         call({"v": (lambda e: e.memset(o[3], x), vec(o[5], o))}, [], [o])
 
-    def dma(q, out, in_, r, w, sem, late, total=16):
-        call({q: (lambda e: e.dma_start(out, in_).then_inc(T.sem[sem], 16), 60.0)}, r, w, (sem, total), late, None,
-             0.0 if r else 1e9 - 1e3 * late)
+    def dma(q, out, in_, r, w, size, first=0.0):
+        sem = "d%d" % len([x for x in ends if x[0][0] == "d"])
+        ends.append((sem, 16))
+        call({q: (lambda e: e.dma_start(out, in_).then_inc(T.sem[sem], 16), 60.0)}, r, w, (sem, 16), PLAN["near"], None, first,
+             move=size / PLAN["lrate"])
 
     def gather(q, out, lo, hi, win, w0, w1, offs):
         o, wn, of = at(out, lo, hi), at(win, w0, w1), at(offs, lo // 16, hi // 16)
         ns = CYC * PICK * (hi - lo)
         call(pick({"v": (lambda e: e.tensor_copy(o[3], wn[3].indirect(of[3])), 50 + ns),
-                   "s": (lambda e: e.activation(o[3], wn[3].indirect(of[3]), F.Copy), 65 + ns)}, q), [wn, of], [o])
+                   "s": (lambda e: e.activation(o[3], wn[3].indirect(of[3]), F.Copy), 65 + ns)}, q), [wn, of], [o], picks=True,
+             first=PLAN["stag"] * (8192 - lo) / 8192)
 
     def gather_times(o, wn, of, c):
-        call({"v": (lambda e: e.tensor_tensor(o[3], wn[3].indirect(of[3]), c[3], A.mult), 50 + CYC * PICK * o[5])}, [wn, of, c], [o])
+        call({"v": (lambda e: e.tensor_tensor(o[3], wn[3].indirect(of[3]), c[3], A.mult), 50 + CYC * PICK * o[5])}, [wn, of, c], [o],
+             picks=True)
 
     def g_sel(o, i, pat, c, base, cm):
         call({"g": (lambda e: e.affine_select(o[3], i[3], pat, c, 0.0, base, cm), 170 + 2 * CYC * o[5])}, [i], [o])
@@ -264,8 +506,8 @@ def rank_program(g, core, T, topo):
         call({"g": (lambda e: e.iota(o[3], pat, base, cm, allow_small_or_imprecise_dtypes=True), 130 + 2 * CYC * o[5])}, [], [o], None, late)
 
     def g_zero(b, lo, hi):
-        for a in range(lo, hi, 512):
-            g_iota(at(b, a, min(hi, a + 512)), [[0, min(hi, a + 512) - a]], 0, 0, PLAN["margin"])
+        for a in range(lo, hi, 256):
+            g_iota(at(b, a, a + 256), [[0, 256]], 0, 0, PLAN["margin"])
 
     def cls(d, k, b0, b1):
         return ("%s#%d" % (d, k), 128 * b0, 128 * b1, T[d][:, 128 * b0 + k:128 * b1:16], d, 8 * (b1 - b0))
@@ -274,32 +516,35 @@ def rank_program(g, core, T, topo):
         b0, b1 = [c for c in CH if c[0] <= b < c[1]][0]
         return 512 * b0 + 128 * (s * (b1 - b0) + b - b0)
 
-    Id, Idh, E8 = at("Id", 0, 128), at("Idh", 0, 128), at("E8", 0, 8)
+    Id, Idh, E8 = at("Id", 0, 128), at("Idh", 0, 128), at("EG", 0, 128, 16)
 
-    col = 128 / PLAN["lrate"]
-    for i, (b0, b1) in enumerate(LOADS):
-        a, e, n = 128 * b0, 128 * b1, 2048 if i else 0
-        dma("y", T.Qw[:, a:e], T.qu[:, a:e], [], [("Qw", a, e)], "d%d" % (2 + 2 * i), 1900.0 + (n + 2 * a + 4 * e) * col)
-        dma("s", T.Pb[:, a:e], T.po[:, a:e], [], [("Pb", a, e)], "d%d" % (1 + 2 * i), 1900.0 + (n + 6 * e) * col)
-        if i == 0:
-            dma("s", T.nbi[:], T.nb[:], [], [("nbi", 0, 512)], "d0", 1900.0 + (2048 + 6 * e) * col)
+    loads = [("Qw", T.qu, 512, x) for x in PLAN["qdma"]]
+    for b0, b1 in PLAN["pload"]:
+        loads.insert([i for i, x in enumerate(loads) if x[0] == "Qw" and x[3][1] > b0][0], ("Pb", T.po, 256, (b0, b1)))
+    loads.insert(PLAN["nbat"], None)
+    for i, x in enumerate(loads):
+        q = PLAN["lq"][i % len(PLAN["lq"])]
+        if x:
+            a, e = 128 * x[3][0], 128 * x[3][1]
+            dma(q, T[x[0]][:, a:e], x[1][:, a:e], [], [(x[0], a, e)], x[2] * (e - a), 1e9 - 1e6 * i)
+        else:
+            dma(q, T.nbi[:], T.nb[:], [], [("nbi", 0, 512)], 128 * 2048, 1e9 - 1e6 * i)
 
     msk = topo.mask(core, others[0])
     for c in others[1:]:
         msk &= topo.mask(core, c)
     ne = bin(msk).count("1")
-
     sent = []
 
     def share(b, name, lo, w, to=None, pitch=None, after=(), off=0):
         to, pitch = to or b, pitch or w
-        sent.append(name)
+        ends.extend([("l" + name, ne), ("x" + name, 3 * ne)])
         ids = [DstId(rid=topo.addr(c)[0], pnc=topo.addr(c)[1]) for c in others]
         dst = [T[to][:, pitch * k + off:pitch * k + off + w] for k in [(rank - T.rank_of(c) - 1) % N for c in others]]
         tr = RemoteDMATransfer(dst_ids=ids, dma_engine_mask=msk, remote_sem=T.sem["x" + name], srcs=[T[b][:, lo:lo + w]], dsts=dst)
-        late = PLAN["far"] + 3 * 128 * w * 2 / PLAN["rate"] + (PLAN["once"] if name == "W" else 0.0)
         i = call({"g": (lambda e: e.remote_dma_fused([tr], local_sem=T.sem["l" + name]), 300.0)}, [(b, lo, lo + w)] + list(after),
-                 [("sent" + name, 0, 1)], ("l" + name, ne), late, None, 1e6 if name in PLAN["soon"] else 0.0)
+                 [("sent" + name, 0, 1)], ("l" + name, ne), PLAN["far"] + (0.0 if sent else PLAN["once"]), first=PLAN["early"].get(name, 0.0), move=3 * 128 * w * 2 / PLAN["rate"])
+        sent.append(name)
         call({}, [], [(to, pitch * k + off, pitch * k + off + w) for k in range(3)], ("x" + name, 3 * ne), 0.0, i)
 
     def ci(k):
@@ -308,200 +553,218 @@ def rank_program(g, core, T, topo):
     def cf(k):
         return at("cf", k, k + 1)
 
-    ROW, LOW, UP, W6, WCOST, CODE, NCODE, RA, RX, RQ, B012, NB012, B34, B56, SW, SB = [cf(k) for k in range(16)]
+    ROW, LOW, UP, W6, WCOST, CODE1, CODE2, NCODE1, NCODE2, RA, RX, RQ, BEST, NBEST, STEP, NUM, ENUM, GOAL, SW, SB, RB, SINK, ALONE = [cf(k) for k in range(23)]
     fill(at("ON", 0, 128), 1.0)
     call({"g": (lambda e: e.iota(ci(0)[3], [[0, 1]], 0, 1), 130.0)}, [], [ci(0)])
-    g_sel(E8, at("ON", 0, 8), [[-16, 8]], A.is_ge, 0, 1)
-    g_sel(E8, E8, [[16, 8]], A.is_ge, 15, -1)
     g_sel(Id, at("ON", 0, 128), [[-1, 128]], A.is_equal, 0, 1)
-    g_iota(at("VC", 0, 128), [[128, 16], [0, 8]], own, 1)
-    g_sel(at("E32", 0, 32), at("ON", 0, 32), [[-16, 8], [0, 4]], A.is_ge, 0, 1)
-    g_sel(at("E32", 0, 32), at("E32", 0, 32), [[16, 8], [0, 4]], A.is_ge, 15, -1)
-    for b0, b1 in CH:
-        g_iota(at("CT", 32 * b0, 32 * b1), [[0, 4], [16, 8 * (b1 - b0)]], 128 * b0, 0)
-    g_iota(at("CO", 0, 128), [[16, 128]], 0, 0)
-    fill(at("DS", 0, 512), 0.0)
-    g_zero("DS", 512, V)
-    g_zero("DB", 0, V)
-    g_zero("XT", 0, 512)
-    g_zero("DM", 0, V)
-    for k in range(3):
-        g_zero("M2w", NC * k + NB, NC * k + NC)
-    for b in ("WC0", "WC", "WO", "WB", "WE", "ZZ", "ZB", "ZX", "ZG", "ZM", "RZ", "RS"):
+    g_sel(at("EG", 0, 128), at("ON", 0, 128), [[-16, 8], [0, 16]], A.is_ge, 0, 1)
+    g_sel(at("EG", 0, 128), at("EG", 0, 128), [[16, 8], [0, 16]], A.is_ge, 15, -1)
+    for b in ("WC01", "WC02", "WC1", "WC2", "WO1", "WO2", "WB", "WE", "ZB", "ZX", "ZM", "RZ", "RS"):
         fill(at(b, 0, T[b].shape[1]), 0.0)
-    fill(at("NF", 0, 512, 4, 0), 0.0)
     fill(at("RS", 0, 256, 4), 1e9)
+    fill(at("NF", 0, 512, 4, 0), 0.0)
+    fill(at("XT", 0, 128), 0.0)
     ts(ci(1), ci(0), 15, None, A.bitwise_and)
     ts(ci(2), ci(1), 2, None, A.logical_shift_right)
     ts(ci(3), ci(1), 3, None, A.bitwise_and)
     cp("v", ROW, ci(1))
     tt(LOW, ci(3), ci(2), A.is_lt)
-    tt(cf(16), ci(3), ci(2), A.is_gt)
-    tt(cf(17), ci(3), ci(2), A.is_equal)
-    ts(cf(18), ROW, 9.0, None, A.is_equal)
-    ts(RA, ROW, 4.0, None, A.is_equal)
-    ts(cf(19), ROW, 8.0, None, A.is_equal)
-    ts(B012, ROW, 3.0, None, A.is_lt)
-    ts(NB012, ROW, 3.0, -1.0, A.is_lt, A.mult)
-    ts(cf(20), ROW, 5.0, None, A.is_lt)
-    ts(cf(21), ROW, 7.0, None, A.is_lt)
+    tt(cf(24), ci(3), ci(2), A.is_gt)
+    tt(cf(25), ci(3), ci(2), A.is_equal)
+    ts(UP, LOW, -1.0, 1.0, A.mult, A.add)
+    ts(cf(26), ci(3), 0.0, LOW, A.is_equal, A.mult)
+    ts(W6, cf(24), 2.0, cf(25), A.mult, A.add)
+    tt(WCOST, W6, cf(26), A.add)
+    tt(CODE1, LOW, cf(26), A.subtract)
+    ts(cf(27), ROW, 14.0, 3.0, A.is_equal, A.mult)
+    tt(CODE2, CODE1, cf(27), A.add)
+    ts(NCODE1, CODE1, -1.0, None, A.mult)
+    ts(NCODE2, CODE2, -1.0, None, A.mult)
+    ts(cf(28), ROW, 8.0, None, A.is_equal)
+    ts(cf(34), ROW, 12.0, None, A.is_equal)
+    ts(RA, ROW, 4.0, cf(34), A.is_equal, A.subtract)
+    tt(RB, RA, RA, A.mult)
+    ts(RX, cf(28), FAR / LIFT, RA, A.mult, A.add)
+    ts(cf(36), UP, cf(28), 3 * LIFT, A.add, A.mult)
+    ts(SINK, RB, -4 * LIFT, cf(36), A.mult, A.subtract)
+    ts(RQ, SINK, 0.0, 4 * LIFT, A.is_lt, A.mult)
+    ts(ALONE, RB, 60 * LIFT, -64 * LIFT, A.mult, A.add)
+    ts(cf(35), cf(28), -1.0, None, A.mult)
+    ts(cf(29), ROW, 12.0, None, A.is_lt)
+    ts(BEST, ci(3), 0.0, cf(29), A.is_equal, A.mult)
+    ts(NBEST, BEST, -1.0, None, A.mult)
+    ts(cf(30), ROW, 2.0, None, A.is_equal)
+    ts(STEP, ROW, 12.0, cf(30), A.is_equal, A.add)
+    ts(NUM, ci(3), 2.0, cf(30), A.is_equal, A.subtract)
+    ts(ENUM, NUM, EPS, None, A.mult)
+    tt(cf(31), BEST, cf(28), A.subtract)
+    tt(GOAL, cf(31), NUM, A.add)
     ts(SW, ROW, 4.0, NONE, A.is_equal, A.mult)
     ts(SB, ROW, 0.0, NONE, A.is_equal, A.mult)
-    ts(UP, LOW, -1.0, 1.0, A.mult, A.add)
-    ts(cf(22), ci(3), 0.0, LOW, A.is_equal, A.mult)
-    ts(W6, cf(16), 2.0, cf(17), A.mult, A.add)
-    ts(CODE, ROW, 13.0, cf(18), A.is_equal, A.add)
-    ts(RX, cf(19), FAR, RA, A.mult, A.add)
-    tt(B34, cf(20), B012, A.subtract)
-    ts(B56, cf(21), cf(20), EPS, A.subtract, A.mult)
-    tt(RQ, UP, cf(19), A.add)
-    tt(WCOST, W6, cf(22), A.add)
-    ts(NCODE, CODE, -1.0, None, A.mult)
-    cp("s", at("wA", 0, 8), E8)
-    cp("s", Idh, Id)
-    cp("s", at("ZM", 15, 143, 16), E8)
-    for o, col in ((at("WC0", 0, 64, 8, 0), WCOST), (at("WC0", 1, 64, 8, 1), CODE), (at("WC", 6, 70, 8, 0), WCOST),
-                   (at("WC", 7, 71, 8, 1), CODE), (at("WC", 5, 69, 8, 2), NCODE), (at("WO", 7, 64, 8), NCODE),
-                   (at("WB", 3, 35, 4), B012), (at("WE", 3, 35, 4), B56), (at("ZB", 15, 143, 16), B34), (at("ZX", 15, 143, 16), RX),
-                   (at("ZG", 15, 143, 16), RA), (at("RZ", 112, 128, 2, 0), RQ), (at("RZ", 113, 128, 2, 1), RA), (at("wS", 0, 8), W6)):
-        scaled("s", o, E8, col)
-    scaled("s", at("PM", 0, 128), Id, UP)
+    cp("vs", at("wA", 0, 8), E8)
+    cp("vs", Idh, Id)
+    for o, col in ((at("WC01", 0, 64, 8, 0), WCOST), (at("WC01", 1, 64, 8, 1), CODE1), (at("WC1", 6, 70, 8, 0), WCOST),
+                   (at("WC1", 7, 71, 8, 1), CODE1), (at("WC1", 5, 69, 8, 2), NCODE1), (at("WO1", 7, 64, 8), NCODE1),
+                   (at("WC02", 0, 64, 8, 0), WCOST), (at("WC02", 1, 64, 8, 1), CODE2), (at("WC2", 6, 70, 8, 0), WCOST),
+                   (at("WC2", 7, 71, 8, 1), CODE2), (at("WC2", 5, 69, 8, 2), NCODE2), (at("WO2", 7, 64, 8), NCODE2),
+                   (at("WB", 3, 35, 4), BEST), (at("WE", 3, 35, 4), ENUM), (at("ZB", 15, 143, 16), STEP), (at("ZX", 15, 143, 16), RX),
+                   (at("ZM", 15, 143, 16), GOAL), (at("RZ", 112, 128, 2, 0), RQ), (at("RZ", 113, 128, 2, 1), RA)):
+        scaled("vs", o, E8, col)
+    scaled("vs", at("PM", 0, 128), Id, UP)
     g_iota(at("GO", 0, 128), [[1, 128]], 0, -1)
-    tt(cf(23), ci(3), ci(2), A.subtract)
-    ts(cf(24), cf(23), 3.0, None, A.mult)
-    ts(at("r8", 0, 128), at("GO", 0, 128), cf(24), cf(16), A.is_equal, A.mult)
-    scaled("s", at("PMh", 0, 128), Id, UP)
-    tt(at("PMh", 0, 128), at("PMh", 0, 128), at("r8", 0, 128), A.add)
-    scaled("s", at("WN", 0, 32), at("E32", 0, 32), NB012)
-    scaled("s", at("W1", H2 + V, H2 + V + 16), at("ON", 0, 16), SW)
-    scaled("s", at("B2w", H2 + V, H2 + V + 16), at("ON", 0, 16), SB)
+    tt(cf(32), ci(3), ci(2), A.subtract)
+    ts(cf(33), cf(32), 3.0, None, A.mult)
+    ts(at("r8", 0, 128), at("GO", 0, 128), cf(33), cf(24), A.is_equal, A.mult)
+    tt(at("PMh", 0, 128), at("PM", 0, 128), at("r8", 0, 128), A.add)
+    cp("vs", at("PMq", 0, 128), at("PM", 0, 128))
+    scaled("vs", at("PMp", 0, 128), at("EG", 0, 128), cf(35))
+    tt(at("PMp", 0, 128), at("PMp", 0, 128), at("PMh", 0, 128), A.add)
+    if PLAN["fix"] == "p":
+        for b in ("WU", "WS0", "WS"):
+            fill(at(b, 0, T[b].shape[1]), 0.0)
+        for o, col in ((at("WU", 6, 70, 8), W6), (at("WS0", 0, 64, 8, 0), cf(26)), (at("WS0", 1, 64, 8, 1), CODE2), (at("WS", 6, 70, 8, 0), cf(26)),
+                       (at("WS", 7, 71, 8, 1), CODE2), (at("WS", 5, 69, 8, 2), NCODE2)):
+            scaled("vs", o, E8, col)
     for k in range(8):
-        mm(at("b%d" % (k // 4), 128 * (k % 4), 128 * (k % 4) + 128), at("RZ", 112 - 16 * k, 240 - 16 * k), Idh, True, True)
+        mm(at(PLAN["rep"][k // 4], 128 * (k % 4), 128 * (k % 4) + 128), at("RZ", 112 - 16 * k, 240 - 16 * k), Idh, True, True, more=k % 4 < 3)
     for k in (0, 1):
-        cp("s", at("Rep", 512 * k, 512 * k + 512), at("b%d" % k, 0, 512))
+        cp("vs", at("Rep", 512 * k, 512 * k + 512), at(PLAN["rep"][k], 0, 512))
+    scaled("vs", at("WN", 0, 32), at("EG", 0, 128, 4), NBEST)
+    scaled("vs", at("W1", H2 + V, H2 + V + 16), at("ON", 0, 16), SW)
+    scaled("vs", at("B2w", H2 + V, H2 + V + 16), at("ON", 0, 16), SB)
+    g_iota(at("EV", 0, 128), [[128, 16], [0, 8]], own, 1)
+    ts(at("EV", 0, 128), at("EV", 0, 128), EPS, None, A.mult)
+    for d, ks, r in (("DS", (9, 13, 14), NC), ("DB", (6, 10, 14), V)):
+        if d == "DS":
+            fill(at(d, 0, V), 0.0)
+        else:
+            for a in range(0, V, 512):
+                o, x = at(d, a, a + 512), at("Pb", a, a + 512)
+                call({"v": (lambda e, o=o: e.memset(o[3], 0.0), vec(512, o)),
+                      "s": (lambda e, o=o, x=x: e.activation(o[3], x[3], F.Copy, scale=0.0), act(512))}, [x], [o])
+        g_iota(cls(d, ks[0], 0, 16), [[0, 128]], 0, 1)
+        g_iota(cls(d, ks[1], 0, 16), [[128, 16], [0, 8]], 0, 0)
+        g_iota(cls(d, ks[2], 0, 16), [[0, 128]], r * rank, 0)
+    for (b0, b1), (c0, c1) in zip(CH[::2], CH[1::2]):
+        g_iota(at("NCT", 32 * b0, 32 * c1), [[-128 * (b1 - b0), 2], [0, 4], [-16, 8 * (b1 - b0)]], -128 * b0, 0)
+    g_iota(at("CO", 0, 128), [[16, 128]], 0, 0)
 
-    vc, gc = at("VC", 0, 128), at("GC", 0, 128)
-    ts(gc, vc, float(-1536 * rank), None, A.add)
-    cp("s", cls("DS", 9, 0, 16), gc)
-    tt(cls("DS", 13, 0, 16), gc, cls("DS", 9, 0, 16), A.subtract)
-    cp("s", cls("DB", 5, 0, 16), vc)
-    tt(cls("DB", 6, 0, 16), vc, cls("DB", 5, 0, 16), A.subtract)
-    ts(at("EV", 0, 128), vc, EPS, None, A.mult)
-    cp("s", cls("DM", 2, 0, 16), cls("DB", 5, 0, 16))
-    cp("s", cls("DM", 3, 0, 16), cls("DB", 6, 0, 16))
+    def slots(b0, b1):
+        return ("nbi", 0, 512, T.nbi[:, :, 8 * b0:8 * b1], "nbi", 32 * (b1 - b0))
 
-    for s in R:
-        ts(at("NI", 16 * s, 16 * s + 16), at("nbi", 128 * s, 128 * s + 16), float(V * (3 - rank)), None, A.add)
-    ts(at("MV", 0, 512), at("nbi", 0, 512), float(-own), None, A.add)
+    ts(at("NI", 0, 64), slots(0, 2), float(V * (3 - rank)), None, A.add)
     for b0, b1 in CH[1:]:
-        for s in R:
-            lo, n = gcol(b0, s) // 16, 8 * (b1 - b0)
-            cp(PLAN["gl"], at("GL", lo, lo + n), at("MV", 128 * s + 8 * b0, 128 * s + 8 * b1))
-    ts(at("IX", 0, 64), at("NI", 0, 64), 11, 3, A.logical_shift_right, A.bitwise_and)
-    ts(at("CA", 0, 64), at("NI", 0, 64), V - 1, None, A.bitwise_and)
-    ts(at("ma", 0, 64), at("IX", 0, 64), 256.0, None, A.mult)
-    ts(at("ma", 64, 128), at("IX", 0, 64), 512.0, 512.0, A.mult, A.add)
-    ts(at("mb", 64, 128), at("IX", 0, 64), float(3 - rank), float(-V), A.is_ge, A.mult)
-    tt(at("mb", 0, 64), at("ma", 0, 64), at("CA", 0, 64), A.add)
+        ts(at("GL", 32 * b0, 32 * b1), slots(b0, b1), float(-own), None, A.add)
+    ix, ca = at("IX", 0, 64), at("CA", 0, 64)
+    ts(ix, at("NI", 0, 64), 11, 3, A.logical_shift_right, A.bitwise_and)
+    ts(ca, at("NI", 0, 64), V - 1, None, A.bitwise_and)
+    ts(at("ma", 0, 64), ix, 256.0, None, A.mult)
+    ts(at("ma", 64, 128), ix, 512.0, 512.0, A.mult, A.add)
+    ts(at("mb", 64, 128), ix, float(3 - rank), float(-V), A.is_ge, A.mult)
+    tt(at("PL", 0, 64), at("ma", 0, 64), ca, A.add)
     tt(at("ma", 64, 128), at("ma", 64, 128), at("mb", 64, 128), A.add)
+    cp("v", at("L1", 0, 64), at("PL", 0, 64))
     cp("v", at("L1", 64, 128), at("GL", 64, 128))
     ts(at("L1", 128, 512), at("GL", 128, 512), float(-NB), None, A.add)
-    cp("v", at("L1", 0, 64), at("mb", 0, 64))
-    tt(at("GL", 0, 64), at("ma", 64, 128), at("CA", 0, 64), A.add)
-    ts(at("P2", 0, 64), at("mb", 0, 64), 2.0, None, A.mult)
-    ts(at("P2", 64, 128), at("GL", 64, 128), 2.0, None, A.mult)
-    ts(at("P2", 128, 512), at("GL", 128, 512), float(-NB), 2.0, A.add, A.mult)
-    cp("s", at("GLh", 0, 512), at("GL", 0, 512))
-    ts(at("FL", 0, 64), at("CA", 0, 64), float(NB), float(V), A.is_ge, A.mult)
+    tt(at("GL", 0, 64), at("ma", 64, 128), ca, A.add)
+    cp("vs", at("PL", 64, 512), at("L1", 64, 512))
+    ts(at("FL", 0, 64), ca, float(NB), float(V), A.is_ge, A.mult)
     ts(at("FL", 64, 128), at("GL", 64, 128), float(NB), float(V), A.is_ge, A.mult)
-    ts(at("CT", 0, 512), at("CT", 0, 512), ROW, None, A.add)
-    ts(at("CO", 0, 128), at("CO", 0, 128), ROW, None, A.add)
+    ts(at("mb", 0, 64), ix, 3.0, float(XH - XB + H1), A.is_lt, A.mult)
+    ts(at("PO", 0, 128), at("FL", 0, 128), -1.0, float(XB - H1), A.mult, A.add)
+    tt(at("PO", 0, 64), at("PO", 0, 64), at("mb", 0, 64), A.add)
 
-    def s_sum(bank, w, b0, b1):
+    def s_sum(bank, b0, b1):
         for b in range(b0, b1):
-            mm(at(bank, 8 * b, 8 * b + 8), at("PRS", 128 * b, 128 * b + 128), at(w, 0, 8), True, True)
+            mm(at(bank, 8 * b, 8 * b + 8), at("PRS", 128 * b, 128 * b + 128), at("wA", 0, 8), True, True, more=b % 2 == 0)
 
     def pieces(d, ks, src, b0, b1):
         hi, mid, lo = [cls(d, k, b0, b1) for k in ks]
         r8 = at("r8", 8 * b0, 8 * b1)
         ts(r8, src, R8, -R8, A.add, A.add)
-        ts(hi, src, R16, -R16, A.add, A.add)
+        cp("vs" if kind(src) != "psum" else "v", hi, src)
         tt(lo, src, r8, A.subtract)
         tt(mid, r8, hi, A.subtract)
 
-    def spread(d, win, base, b0, b1, bank, with_p=False, q="vs"):
+    def spread(d, win, base, b0, b1, bank, with_p=False):
         if with_p:
             mm(at(bank, 0, 128 * (b1 - b0)), at("PM", 0, 128), at("Pb", 128 * b0, 128 * b1), True, False)
         for b in range(b0, b1):
-            mm(at(bank, 128 * (b - b0), 128 * (b - b0) + 128), at(d, 128 * b, 128 * b + 128), Id, not with_p, None if with_p else True)
-        cp(q, at(win, base + 128 * b0, base + 128 * b1), at(bank, 0, 128 * (b1 - b0)))
+            mm(at(bank, 128 * (b - b0), 128 * (b - b0) + 128), at(d, 128 * b, 128 * b + 128), Id, not with_p, None if with_p else True,
+               more=b < b1 - 1)
+        cp("vs", at(win, base + 128 * b0, base + 128 * b1), at(bank, 0, 128 * (b1 - b0)))
 
     def c_bank(b0, b1):
         return at("b%d" % (b0 // 4), 128 * (b0 % 4), 128 * (b0 % 4 + b1 - b0))
 
-    def start_c(b0, b1, stop):
-        mm(c_bank(b0, b1), Idh if stop else at("PMh", 0, 128), at("Ch", H1 + 128 * b0, H1 + 128 * b1), True, stop)
+    def blocks(xs):
+        return min(CH[x][0] for x in xs), max(CH[x][1] for x in xs)
+
+    def shares(b0, b1, banks):
+        n = -(-(b1 - b0) // len(banks))
+        return [(b0 + n * i, min(b1, b0 + n * i + n), bank) for i, bank in enumerate(banks)]
+
+    def by_bank(b0, b1):
+        return [(max(b0, k), min(b1, k + 4)) for k in range(0, 16, 4) if max(b0, k) < min(b1, k + 4)]
+
+    def plain(fused, b0, b1):
+        return any(c0 < b1 and b0 < c1 and len(fused.get(x, ())) < 4 for x, (c0, c1) in enumerate(CH))
 
     SK = [4, 8, 12]
-    for i, (b0, b1) in enumerate(LOADS):
+    mark()
+    for b0, b1 in PLAN["pload"]:
+        for c0, c1 in by_bank(b0, b1):
+            mm(c_bank(c0, c1), Id, at("Pb", 128 * c0, 128 * c1), True, True)
+    for b0, b1 in PLAN["qload"]:
         a, e = 128 * b0, 128 * b1
-        q, bank = at("Qw", a, e), "b4" if i % 2 else "b5"
-        scaled("s", at("Ch", H1 + a, H1 + e), q, UP, LOW)
-        start_c(b0, b1, True)
-        if i in PLAN["plain"]:
-            tt(at("PRS", a, e), at("Pb", a, e), q, A.mult)
-            s_sum(bank, "wA", b0, b1)
-        else:
-            tt(at("PRS", a, e), at("Pb", a, e), c_bank(b0, b1), A.mult)
-            s_sum(bank, "wS", b0, b1)
+        tt(at("PRS", a, e), at("Qw", a, e), c_bank(b0, b1), A.mult)
+        scaled("s", at("Ch", H1 + a, H1 + e), at("Qw", a, e), UP, LOW)
+        if b0 == 0 and PLAN["opens"] == "C":
+            share("Ch", "C", H1, NB)
+    for b0, b1, bank, back in PLAN["sum0"]:
+        s_sum(bank, b0, b1)
         pieces("DS", SK, at(bank, 8 * b0, 8 * b1), b0, b1)
-        spread("DS", "W", H1, b0, b1, "b6" if i % 2 else "b7", True)
-        if i == 0:
-            if PLAN["firstx"] == "C":
-                share("Ch", "C", H1, NB)
+        for c0, c1, k in shares(b0, b1, back):
+            spread("DS", "W", H1, c0, c1, k, True)
+        if b0 == 0:
             share("W", "W", H1, NB)
-    if PLAN["firstx"] == "W":
+    for b0, b1 in PLAN["qload"]:
+        if plain(PLAN["fused1"], b0, b1):
+            mm(c_bank(b0, b1), Idh, at("Ch", H1 + 128 * b0, H1 + 128 * b1), True, True)
+    if PLAN["opens"] == "W":
         share("Ch", "C", H1, NB, after=[("Qw", 0, V), ("Pb", 0, V), ("sentW", 0, 1)])
 
-    def clear(bank, n):
-        mm(at(bank, 0, n), at("ZZ", 0, 128), at("Pb", 0, n), True, False)
-
-    def cost_start(bank, b0, b1, win, base):
-        clear(bank, 64 * (b1 - b0))
+    def costs(bank, xs, win, base, window, offs, fused, c, cb, k):
+        b0, b1 = blocks(xs)
         for b in range(b0, b1):
-            mm(at(bank, 64 * (b - b0), 64 * (b - b0) + 64), at(win, base + 128 * b, base + 128 * b + 128), at("WO", 0, 64), False)
+            mm(at(bank, 64 * (b - b0), 64 * (b - b0) + 64), at(win, base + 128 * b, base + 128 * b + 128), at("WO" + k, 0, 64), b == b0,
+               more=b % 4 < 3 and b0 < b < b1 - 1)
+        for x in xs:
+            c0, c1 = CH[x]
+            for s in R:
+                lo, n = gcol(c0, s), 128 * (c1 - c0)
+                if s in fused.get(x, ()):
+                    gather_times(at("PR", lo, lo + n), at(win, *window(x)), at(offs, lo // 16, (lo + n) // 16), at(c, cb + 128 * c0, cb + 128 * c1))
+                else:
+                    gather("s", "GA", lo, lo + n, win, *window(x), offs)
+                    tt(at("PR", lo, lo + n), at("GA", lo, lo + n), c_bank(c0, c1), A.mult)
+            for s in R:
+                w = at("WC0" + k, 0, 64) if s == 0 else at("WC" + k, 6 - 2 * s, 70 - 2 * s)
+                apart = k == "2" and PLAN["fix"] == "p" and s not in fused.get(x, ())
+                for src, w in ((("PR", at("WU", 6 - 2 * s, 70 - 2 * s)), ("GA", at("WS", 6 - 2 * s, 70 - 2 * s) if s else at("WS0", 0, 64)))
+                               if apart else (("PR", w),)):
+                    for b in range(c0, c1):
+                        mm(at(bank, 64 * (b - b0), 64 * (b - b0) + 64), at(src, gcol(b, s), gcol(b, s) + 128), w, False, more=b < c1 - 1)
 
-    def cost_sums(bank, b0, x, s):
-        w = at("WC0", 0, 64) if s == 0 else at("WC", 6 - 2 * s, 70 - 2 * s)
-        k = PLAN["sgrain"][x]
-        lo = gcol(CH[x][0], s - s % k)
-        for b in range(*CH[x]):
-            mm(at(bank, 64 * (b - b0), 64 * (b - b0) + 64), at("PR", gcol(b, s), gcol(b, s) + 128), w, False,
-               r=[("PR", lo, lo + 128 * k * (CH[x][1] - CH[x][0]))])
-
-    def costs(x, win, w0, w1, offs, bank, b0, fused, c, base):
-        c0, c1 = CH[x]
-        for s in R:
-            lo, n, k = gcol(c0, s), 128 * (c1 - c0), c0 // 4
-            if s in fused:
-                gather_times(at("PR", lo, lo + n), at(win, w0, w1), at(offs, lo // 16, (lo + n) // 16), at(c, base + 128 * c0, base + 128 * c1))
-            else:
-                m = min(PLAN["cgrain"][x], 4 - s - len([f for f in fused if f > s]))
-                if s % PLAN["cgrain"][x] == 0:
-                    gather("s", "GA", lo, lo + m * n, win, w0, w1, offs)
-                tt(at("PR", lo, lo + n), at("GA", lo, lo + n), at("b%d" % k, 128 * c0 - 512 * k, 128 * c1 - 512 * k), A.mult)
-        for s in R:
-            cost_sums(bank, b0, x, s)
-
-    def slots_of(out, x, win, w0, w1, offs, q="vs"):
+    def slots_of(out, x, win, w0, w1, offs):
         n, k = 128 * (CH[x][1] - CH[x][0]), PLAN["grain"][x]
         for s in range(0, 4, k):
-            gather(q, out, gcol(CH[x][0], s), gcol(CH[x][0], s) + k * n, win, w0, w1, offs)
+            gather("vs", out, gcol(CH[x][0], s), gcol(CH[x][0], s) + k * n, win, w0, w1, offs)
 
     def best_of(bank, b0, b1):
         n = b1 - b0
         scan(at("MS", 32 * b0, 32 * b1), at("RS", 0, 32 * n), at(bank, 0, 64 * n, 2), A.add, A.min)
-        pieces("DB", [0, 1, 2], at("MS", 32 * b0 + 3, 32 * b1, 4), b0, b1)
+        pieces("DB", [0, 4, 8], at("MS", 32 * b0 + 3, 32 * b1, 4), b0, b1)
 
     def choice_of(bank, b0, b1, hi, lo):
         n = b1 - b0
@@ -509,196 +772,188 @@ def rank_program(g, core, T, topo):
             tt(at("NF", 32 * b0 + s, 32 * b1, 4, s), at(bank, 2 * s, 64 * n, 8), at("MS", 32 * b0 + s - 1, 32 * b1, 4), A.is_ge)
         scan(at("WD", 32 * b0, 32 * b1), at("NF", 32 * b0, 32 * b1), at(bank, 1, 64 * n, 2), A.mult, A.add)
         dd = at("WD", 32 * b0 + 3, 32 * b1, 4)
-        cp("v", hi, dd)
+        cp("vs", hi, dd)
         tt(lo, dd, hi, A.subtract)
 
-    def test_start(bank, b0, b1, win, base):
-        clear(bank, 32 * (b1 - b0))
+    def tests(bank, xs, win, base, window, offs):
+        b0, b1 = blocks(xs)
         for b in range(b0, b1):
-            mm(at(bank, 32 * (b - b0), 32 * (b - b0) + 32), at(win, base + 128 * b, base + 128 * b + 128), at("WN", 0, 32), False,
-               w=[("less", 5 * b + 4, 5 * b + 5)])
-
-    def test_sums(bank, b0, x):
-        for s in R:
-            for b in range(*CH[x]):
-                o, l, whole = at(bank, 32 * (b - b0), 32 * (b - b0) + 32), at("GB", gcol(b, s), gcol(b, s) + 128), ("less", 5 * b + s, 5 * b + s + 1)
-                mm(o, l, at("WB", 3 - s, 35 - s), False, w=[whole])
-                mm(o, l, at("WE", 3 - s, 35 - s), False, r=[whole, ("less", 5 * b + 4, 5 * b + 5)])
+            mm(at(bank, 32 * (b - b0), 32 * (b - b0) + 32), at(win, base + 128 * b, base + 128 * b + 128), at("WN", 0, 32), b == b0,
+               w=[("less", b, b + 1)], more=b % 4 < 3 and b0 < b < b1 - 1)
+        for x in xs:
+            slots_of("GB", x, win, *window(x), offs)
+            for s in R:
+                for w in ("WB", "WE"):
+                    for b in range(*CH[x]):
+                        mm(at(bank, 32 * (b - b0), 32 * (b - b0) + 32), at("GB", gcol(b, s), gcol(b, s) + 128), at(w, 3 - s, 35 - s), False,
+                           r=[("less", b, b + 1)], more=w == "WB" or b < CH[x][1] - 1)
 
     def collapses(o, bank, b0, b1):
         n = b1 - b0
         scan(at("MV", 32 * b0, 32 * b1), at("RS", 0, 32 * n), at(bank, 0, 32 * n), A.add, A.min)
         tt(o, at("MV", 32 * b0 + 3, 32 * b1, 4), at("EV", 8 * b0, 8 * b1), A.is_gt)
 
-    def tables(z, src, lo, hi, bank, firsts):
+    def tables(z, src, first, lo, hi, bank, firsts):
         o = at(bank, lo // 16, hi // 16)
+        if z in PLAN["turned"] and (hi - lo) % 2048 == 0:
+            for a in range(lo, hi, 2048):
+                t, x = at(bank, a // 16, a // 16 + 128), at("TT", a // 16, a // 16 + 128)
+                for b in ALL:
+                    mm(at(bank, a // 16 + b, a // 16 + 128, 16), at(src, first + a + b, first + a + 2048, 16), at(z, 15, 143, 16), True, True,
+                       more=b % 8 < 7)
+                cp("vs", x, t)
+            for i, c in enumerate(firsts):
+                c = at(c, lo // 16, hi // 16)
+                mm(o, Idh if kind(c) == "float16" else Id, c, i == 0)
+            for a in range(lo, hi, 2048):
+                mm(at(bank, a // 16, a // 16 + 128), at("TT", a // 16, a // 16 + 128), Idh, False)
+            return
         for i, c in enumerate(firsts):
-            mm(o, Idh, at(c, lo // 16, hi // 16), i == 0)
-        for b in ALL:
-            mm(o, at(z, 15 - b, 143 - b), at(src, lo + b, hi, 16), False)
+            c = at(c, lo // 16, hi // 16)
+            mm(o, Idh if kind(c) == "float16" else Id, c, i == 0)
+        for a in range(lo, hi, 1024):
+            for b in ALL:
+                mm(at(bank, a // 16, a // 16 + 64), at(z, 15 - b, 143 - b), at(src, first + a + b, first + a + 1024, 16), False, more=b % 8 < 7)
 
-    OWN2, ALL2 = (H2, H2 + V + 16), (0, H2 + V + 16)
-
-    def window1(x):
+    def one(x):
         return ((0, H1, H1 + NB)[min(x, 2)], H1 + V)
 
-    def blocks(xs):
-        return min(CH[x][0] for x in xs), max(CH[x][1] for x in xs)
-
-    def shares(b0, b1, banks):
-        n = (b1 - b0) // len(banks)
-        return [(b0 + n * i, b0 + n * i + n, bank) for i, bank in enumerate(banks)]
+    def two(x):
+        return (0 if x < 2 else H2, H2 + V + 16)
 
     for bank, xs, back in PLAN["cost1"]:
         b0, b1 = blocks(xs)
-        cost_start(bank, b0, b1, "W", H1)
-        for x in xs:
-            costs(x, "W", *window1(x), "L1", bank, b0, PLAN["fused1"].get(x, ()), "Ch", H1)
+        costs(bank, xs, "W", H1, one, "L1", PLAN["fused1"], "Ch", H1, "1")
         best_of(bank, b0, b1)
-        choice_of(bank, b0, b1, cls("DB", 3, b0, b1), cls("DB", 4, b0, b1))
+        choice_of(bank, b0, b1, cls("DB", 12, b0, b1), cls("DB", 2, b0, b1))
+        cp("vs", at("XD", 16 * b0 + 1, 16 * b1, 2, 1), at("WD", 32 * b0 + 3, 32 * b1, 4))
         for c0, c1, k in shares(b0, b1, back):
             spread("DB", "Bw", H1, c0, c1, k)
         if b0 == 0:
             share("Bw", "B", H1, NB)
+            if PLAN["opens"] == "B":
+                share("Ch", "C", H1, NB, after=[("sentB", 0, 1)])
 
-    def move1(bank, b0, b1, k, tb):
+    def planes(srcs, c0, p1, bank, rows=False):
+        n = 128 * len(srcs)
+        bank, second = bank if isinstance(bank, tuple) else (bank, None)
+        for j in (bank, second) if second else (bank,):
+            if j == bank:
+                mm(at(j, 0, n), at("PMq", 0, 128), at("Ch", c0, c0 + n), True)
+            for i, (b, lo, k, r) in enumerate(srcs):
+                mm(at(j, 128 * i, 128 * i + 128), at("Rep", 128 * k, 128 * k + 128, 1, None, r), at(b, lo, lo + 128, 1, None, r),
+                   j != bank, None if j == bank else True, more=i < len(srcs) - 1)
+        for a, e, p in p1:
+            over(at("X", p, p + e - a), at(bank, a, e), SINK)
+        if rows:
+            g_zero("X", c0, c0 + n)
+            dma("y", T.X[4::8, c0:c0 + n], T.X[4::8, p1[0][2]:p1[0][2] + n], [("X", p1[0][2], p1[0][2] + n)], [("X", c0, c0 + n)], 64 * n)
+        else:
+            over(at("X", c0, c0 + n), at(second or bank, 0, n), ALONE)
+
+    def over(o, a, col):
+        call({"v": (lambda e: e.tensor_scalar(o[3], a[3], col[3], 0.0, A.add, A.max), vec(o[5], o, a)),
+              "s": (lambda e: e.activation(o[3], a[3], F.Relu, bias=col[3]), act(o[5]))}, [a, col], [o])
+
+    for k, (bank, xs, back, lists, rows) in enumerate(PLAN["test1"]):
+        b0, b1 = blocks(xs)
+        tests(bank, xs, "Bw", H1, one, "L1")
         c, n = at("XD", 16 * b0, 16 * b1, 2, 0), 16 * (b1 - b0)
         collapses(c, bank, b0, b1)
-        tt(at("XD", 16 * b0 + 1, 16 * b1, 2, 1), at("WD", 32 * b0 + 3, 32 * b1, 4), c, A.mult)
-        mm(at(tb, 0, 128, 1, None, n), at("XD", 16 * b0, 16 * b1), Idh, True, True)
-        cp("vs", at("XT", 128 * k, 128 * k + 128, 1, None, n), at(tb, 0, 128, 1, None, n))
-
-    def planes(srcs, c0, bv, bs):
-        n = 128 * len(srcs)
-        for p, bank in ((1, bv), (0, bs)):
-            if p or bs != bv:
-                for i, (b, lo, k, rows) in enumerate(srcs):
-                    mm(at(bank, 128 * i, 128 * i + 128), at("Rep", 128 * k, 128 * k + 128, 1, None, rows), at(b, lo, lo + 128, 1, None, rows), True, True)
-            o = at("X", 2 * c0 + p, 2 * (c0 + n), 2, p)
-            if p:
-                tt(o, at(bank, 0, n), at("Ch", c0, c0 + n), A.mult)
-            else:
-                scaled("vs", o, at(bank, 0, n), RA)
-
-    def own_rows(k, b0, b1, c0, c1):
-        return [("XT", 128 * k, b - b0, 16 * (b1 - b0)) for b in range(c0, c1)]
-
-    def chose(lo, hi, bank):
-        tables("ZB", "GB", lo, hi, bank, ["GLh"])
-        t = at(bank, lo // 16, hi // 16)
-        tt(t, t, at("CT", lo // 16, hi // 16), A.is_equal)
-        tt(at("LC", lo // 16, hi // 16), t, at("P2", lo // 16, hi // 16), A.add)
-
-    for k, (bank, xs, back, lists) in enumerate(PLAN["test1"]):
-        b0, b1 = blocks(xs)
-        test_start(bank, b0, b1, "Bw", H1)
-        for x in xs:
-            slots_of("GB", x, "Bw", *window1(x), "L1")
-            test_sums(bank, b0, x)
-        k *= 2
-        move1(bank, b0, b1, k, "b1")
+        mm(at(bank, 0, 128, 1, None, n), at("XD", 16 * b0, 16 * b1), Idh, True, True)
+        cp("vs", at("XT", 128 * k, 128 * k + 128, 1, None, n), at(bank, 0, 128, 1, None, n))
         if b0 == 0:
-            share("XT", "X", 128 * k, PLAN["xw"], "XH")
-        if b1 - b0 > 4:
-            for c0, c1, j in shares(b0, b1, back):
-                planes(own_rows(k, b0, b1, c0, c1), H1 + 128 * c0, j, j)
-        else:
-            planes(own_rows(k, b0, b1, b0, b1), H1 + 128 * b0, back[0], back[-1])
-        chose(512 * b0, 512 * b1, lists)
-    ha, hb, hc, hd = PLAN["halo"]
-    planes([("XH", PLAN["xw"] * (i // 2), i % 2, 32) for i in range(4)], 0, ha, hb)
-    planes([("XH", 2 * PLAN["xw"], i, 32) for i in range(2)], 512, hc, hd)
-
-    def pulls(x):
-        c0, c1 = CH[x]
-        k = c0 // 4
-        for s in R:
-            lo = gcol(c0, s)
-            mm(at("b%d" % k, 128 * c0 - 512 * k, 128 * c1 - 512 * k), at("PMh", 0, 128), at("GH", lo, lo + 128 * (c1 - c0)), False)
-
-    def own_sum(b0, b1, bank):
-        tt(at("PRS", 128 * b0, 128 * b1), at("Pb", 128 * b0, 128 * b1), c_bank(b0, b1), A.mult)
-        s_sum(bank, "wA", b0, b1)
-        cp("s", at("Qw", 128 * b0, 128 * b1), c_bank(b0, b1))
-        for x, (c0, c1) in enumerate(CH):
-            n = len(PLAN["fused2"].get(x, ()))
-            if b0 <= c0 < b1 and n:
-                scaled("s", at("Cf", 128 * c0, 128 * c1), c_bank(c0, c1), UP, LOW)
-        if any(b0 <= c0 < b1 and len(PLAN["fused2"].get(x, ())) < 4 for x, (c0, c1) in enumerate(CH)):
-            scaled(PLAN["fix"], c_bank(b0, b1), c_bank(b0, b1), UP, LOW)
+            share("XT", "X", 128 * k, 128, "XF")
+        for c0, c1, j in shares(b0, b1, back):
+            p1 = [(0, NB, XB), (NB, 128 * c1, XS)] if c0 == 0 else [(0, 128 * (c1 - c0), XS + 128 * c0 - NB)]
+            planes([("XT", 128 * k, b - b0, n) for b in range(c0, c1)], H1 + 128 * c0, [p for p in p1 if p[0] < p[1]], j, rows)
+        for kk in (12, 2):
+            tt(cls("DB", kk, b0, b1), cls("DB", kk, b0, b1), c, A.mult)
+        tables("ZB", "GB", 0, 512 * b0, 512 * b1, lists, ["GL", "NCT"])
+        for a, e in ((32 * b0, min(128, 32 * b1)), (max(128, 32 * b0), 32 * b1)):
+            if a < e:
+                t = at(lists, a, e)
+                if a < 128:
+                    ts(t, t, ROW, None, A.is_equal)
+                    tt(t, t, at("PO", a, e), A.mult)
+                else:
+                    ts(t, t, ROW, float(XS - XR), A.is_equal, A.mult)
+                tt(at("LC", a, e), t, at("PL", a, e), A.add)
+    planes([("XF", 128 * (i // 2), i % 2, 32) for i in range(4)], 0, [(0, 512, XH)], PLAN["halo"][0])
+    planes([("XF", 256, i, 32) for i in range(2)], 512, [(0, 256, XH + 512)], PLAN["halo"][1])
 
     def around(o, x, n, cap):
         ts(at("ma", 0, n), x, float(NC), float(V), A.is_lt, A.mult)
         tt(at("mb", 0, n), x, at("ma", 0, n), A.add)
         ts(o, at("mb", 0, n), float(-NC), cap, A.add, A.min)
 
-    def next_list(lo, hi, bank):
-        tables("ZX", "GH", lo, hi, bank, ["GLh"])
-        ts(at("L2", lo // 16, hi // 16), at(bank, lo // 16, hi // 16), float(V), None, A.min)
-
-    cp("vs", cls("DS", 9, 0, 16), cls("DB", 5, 0, 16))
-    cp("vs", cls("DS", 13, 0, 16), cls("DB", 6, 0, 16))
     for xs, sums, back, lists in PLAN["pull"]:
         b0, b1 = blocks(xs)
-        start_c(b0, b1, False)
+        for c0, c1 in by_bank(b0, b1):
+            mm(c_bank(c0, c1), at("PMh", 0, 128), at("Ch", H1 + 128 * c0, H1 + 128 * c1), True)
         for x in xs:
-            slots_of("GH", x, "X", 2 * window1(x)[0], 2 * (H1 + V), "LC")
-            pulls(x)
-        own_sum(b0, b1, sums)
+            slots_of("GH", x, "X", *((0, XE), (H1, XH), (XR, XB))[min(x, 2)], "LC")
+            for s in R:
+                lo = gcol(CH[x][0], s)
+                mm(c_bank(*CH[x]), at("PMp", 0, 128), at("GH", lo, lo + 128 * (CH[x][1] - CH[x][0])), False)
+        for c0, c1 in by_bank(b0, b1):
+            tt(at("PRS", 128 * c0, 128 * c1), at("Pb", 128 * c0, 128 * c1), c_bank(c0, c1), A.mult)
+        s_sum(sums, b0, b1)
+        for x in xs:
+            if PLAN["fused2"].get(x):
+                scaled("s", at("Cf", 128 * CH[x][0], 128 * CH[x][1]), c_bank(*CH[x]), UP, LOW)
+        for c0, c1 in by_bank(b0, b1):
+            if c0 // 4 not in PLAN["later"]:
+                cp(PLAN["out"], at("Qw", 128 * c0, 128 * c1), c_bank(c0, c1))
+            if plain(PLAN["fused2"], c0, c1) and PLAN["fix"] != "p":
+                scaled(PLAN["fix"], c_bank(c0, c1), c_bank(c0, c1), UP, LOW)
         pieces("DS", SK, at(sums, 8 * b0, 8 * b1), b0, b1)
         for c0, c1, k in shares(b0, b1, back):
             spread("DS", "W1", H2, c0, c1, k, True)
         if b0 >= 4:
-            next_list(512 * b0, 512 * b1, lists)
+            tables("ZX", "GH", 0, 512 * b0, 512 * b1, lists, ["GL"])
+            ts(at("L2", 32 * b0, 32 * b1), at(lists, 32 * b0, 32 * b1), float(V), None, A.min)
         else:
             share("W1", "W1" if b0 == 0 else "Wl", H2 + 128 * b0, 128 * (b1 - b0), None, NC, (), 128 * b0)
-            tables("ZX", "GH", 512 * b0, 512 * b1, lists, ["GLh", "FL"])
+            tables("ZX", "GH", 0, 512 * b0, 512 * b1, lists, ["GL", "FL"])
             around(at("L2", 32 * b0, 32 * b1), at(lists, 32 * b0, 32 * b1), 32 * (b1 - b0), float(H2 + V))
-    for i, (a, e) in enumerate(STORES):
-        dma("y", T.q1[:, a:e], T.Qw[:, a:e], [("Qw", a, e), (PLAN["q1"], 0, 1)], [], "dq1", 12000.0 + 400 * i, 16 * (i + 1))
 
     for bank, xs, back in PLAN["cost2"]:
         b0, b1 = blocks(xs)
-        cost_start(bank, b0, b1, "W1", H2)
-        for x in xs:
-            costs(x, "W1", *(ALL2 if x < 2 else OWN2), "L2", bank, b0, PLAN["fused2"].get(x, ()), "Cf", 0)
+        costs(bank, xs, "W1", H2, two, "L2", PLAN["fused2"], "Cf", 0, "2")
+        for c0, c1 in by_bank(b0, b1):
+            if c0 // 4 in PLAN["later"]:
+                cp(PLAN["out"], at("Qw", 128 * c0, 128 * c1), c_bank(c0, c1))
         best_of(bank, b0, b1)
         choice_of(bank, b0, b1, at("Dh", 8 * b0, 8 * b1), at("Dl", 8 * b0, 8 * b1))
         for c0, c1, k in shares(b0, b1, back):
             spread("DB", "B2w", H2, c0, c1, k)
         if b0 < 4:
             share("B2w", "B2" if b0 == 0 else "Bl", H2 + 128 * b0, 128 * (min(b1, 4) - b0), None, NC, (), 128 * b0)
+    for a, e, x in PLAN["stores"]:
+        dma("y", T.q1[:, a:e], T.Qw[:, a:e], [("Qw", a, e), ("sent" + x, 0, 1)], [], 512 * (e - a))
 
-    def move2(bank, b0, b1):
-        c = at("cl", 8 * b0, 8 * b1)
-        collapses(c, bank, b0, b1)
-        for k, d in ((0, "Dh"), (1, "Dl")):
-            tt(cls("DM", k, b0, b1), c, at(d, 8 * b0, 8 * b1), A.mult)
-
-    for b in ALL:
-        mm(at("b6", 0, 128), at("ZG", 15 - b, 143 - b), at("X", 2 * (H1 + b), 2 * (H1 + V), 32, 0), b == 0)
-    tt(at("GO", 0, 128), at("b6", 0, 128), at("CO", 0, 128), A.add)
+    tables("ZB", "B2w", H2, 0, V, "b6", ["CO"])
+    ts(at("GO", 0, 16), at("b6", 0, 16), ROW, None, A.add)
     around(at("LG", 0, 16), at("GO", 0, 16), 16, float(H2 + V))
-    cp("v", at("LG", 16, 128), at("GO", 16, 128))
+    ts(at("LG", 16, 128), at("b6", 16, 128), ROW, None, A.add)
     for bank, xs, back in PLAN["test2"]:
         b0, b1 = blocks(xs)
-        test_start(bank, b0, b1, "B2w", H2)
-        for x in xs:
-            slots_of("GB", x, "B2w", *(ALL2 if x < 2 else OWN2), "L2")
-            test_sums(bank, b0, x)
-        move2(bank, b0, b1)
+        tests(bank, xs, "B2w", H2, two, "L2")
+        c = at("cl", 8 * b0, 8 * b1)
+        collapses(c, bank, b0, b1)
+        for k, d in ((0, "Dh"), (4, "Dl")):
+            tt(cls("DB", k, b0, b1), c, at(d, 8 * b0, 8 * b1), A.mult)
         for c0, c1, k in shares(b0, b1, back):
-            spread("DM", "M2w", H2, c0, c1, k)
+            spread("DB", "M2w", H2, c0, c1, k)
         if b0 == 0:
             share("M2w", "M2", H2, NB, None, NC)
 
-    for lo, hi in ((256, 1024), (1024, 1536), (1536, 2048), (0, 256)):
+    for lo, hi in PLAN["last"]:
         gather("vs", "GA", lo, hi, "M2w", H2 if lo else 0, H2 + V, "LG")
-    clear("b6", 128)
-    for b in ALL:
-        mm(at("b6", 0, 128), at("ZM", 15 - b, 143 - b), at("GA", 128 * b, 128 * b + 128), False)
+    for b in [2, 3] + [b for b in ALL if b // 2 != 1]:
+        mm(at("b6", 0, 128), at("ZM", 15 - b, 143 - b), at("GA", 128 * b, 128 * b + 128), b == 2, more=b % 2 == 0 and b != 2)
     cp("v", at("GO", 0, 128), at("b6", 0, 128))
-    dma("y", T.goal[:], T.GO[:], [("GO", 0, 128)], [], "dgo", 2000.0)
+    dma("y", T.goal[:], T.GO[:], [("GO", 0, 128)], [], 128 * 512)
 
-    issue([("y", [("dq1", 16 * len(STORES)), ("dgo", 16)]),
-           ("g", [("d%d" % i, 16) for i in range(1 + 2 * len(LOADS))] + [("l" + x, ne) for x in sent] + [("x" + x, 3 * ne) for x in sent])])
+    issue(ends)

import numpy as np
from concourse.bass import DstId, RemoteDMATransfer
from concourse.mybir import AluOpType as A, ActivationFunctionType as F

N, V, NB, NC = 4, 2048, 256, 512
H1, H2 = 3 * NB, 3 * NC
XR, XS, XB, XH, XE = H1 + NB, H1 + V, H1 + 2 * V - NB, H1 + 2 * V, 2 * (H1 + V)
PLAN = dict(
    ch=[(0, 2), (2, 4), (4, 8), (8, 12), (12, 14), (14, 16)],
    qload=[(0, 2), (2, 4), (4, 8), (8, 12), (12, 14), (14, 16)], pload=[(0, 4), (4, 8), (8, 12), (12, 16)], nbat=99, lq="ys", out="s",
    qdma=[(0, 2), (2, 4), (4, 8), (8, 12), (12, 14), (14, 16)],
    sum0=[(0, 2, "b5", ("b7",)), (2, 4, "b4", ("b6",)), (4, 8, "b5", ("b7",)), (8, 12, "b4", ("b6",)), (12, 16, "b5", ("b0", "b7"))],
    fused1={0: (0, 1, 2, 3), 1: (0, 1, 2, 3), 5: (3,)}, fused2={0: (0, 1, 2, 3), 1: (0, 1, 2, 3), 5: (3,)},
    cost1=[("b4", (1, 0), ("b6",)), ("b5", (2, 3), ("b7", "b6")), ("b0", (4, 5), ("b4", "b1"))],
    cost2=[("b4", (1, 0), ("b6",)), ("b5", (2, 3), ("b7", "b6")), ("b0", (4, 5), ("b4", "b1"))],
    test1=[("b2", (1, 0), ("b5",), "b4", False), ("b3", (2, 3), ("b6", "b7"), "b0", True), ("b2", (4, 5), ("b5", "b4"), "b7", False)],
    halo=("b5", "b6"),
    pull=[((1,), "b4", ("b4",), "b5"), ((0,), "b6", ("b6",), "b7"), ((2,), "b4", ("b4",), "b5"), ((3,), "b6", ("b6",), "b7"),
          ((4, 5), "b0", ("b4", "b0"), "b5")],
    test2=[("b2", (0,), ("b7",)), ("b3", (1, 2), ("b5", "b0")), ("b4", (3, 4), ("b1", "b7")), ("b2", (5,), ("b0",))],
    last=((256, 1024), (1024, 1536), (1536, 2048), (0, 256)), stores=[(0, 1024, "W1"), (1024, 2048, "W1")], later=(),
    grain=(2, 2, 1, 1, 2, 2), margin=1000.0, turns=4, far=2100.0, rate=150.0, once=2800.0, lrate=330.0, near=1900.0, cross=300.0,
    slow=1.0, pick=1.56, fix="s", dear=1.0, rep=("b6", "b7"), seed=0, tries=0, shake=600.0,
    flow=0, step=100.0, soon=300.0, idle=2.0, spare=1000.0, mend=26000, heat=60.0, pull_in=0.3, roam=0.3, early={}, stag=0.0,
    cases=[(1.0, dict(v=1.0, s=1.0, p=1.0, g=1.0), 1.0, 250.0, 1.0, 1.0), (1.28, dict(v=1.4, s=1.1, p=1.1, g=1.3), 1.0, 300.0, 1.1, 1.4),
           (1.17, dict(v=1.05, s=1.05, p=1.45, g=1.5), 0.85, 300.0, 1.0, 1.2), (1.22, dict(v=1.2, s=1.2, p=1.2, g=1.2), 0.8, 420.0, 1.4, 2.0)],
    opens="W", wary=1.2, turned=("ZB", "ZX"),
)
FOUND = {}
NONE = float(1 << 24)
FAR = 32768.0
R16, R8 = 1.5 * 2.0 ** 39, 1.5 * 2.0 ** 31
EPS = 2.0 ** -14
LIFT = 1024.0
HOP = 115.0

SCRATCH = {}
for _n, _w, _t in (
        ("Qw", V, "float32"), ("Pb", V, "bfloat16"), ("Cf", V, "float32"), ("Ch", H1 + V, "float16"),
        ("W", H1 + V, "bfloat16"), ("W1", H2 + V + 16, "bfloat16"), ("Bw", H1 + V, "bfloat16"), ("B2w", H2 + V + 16, "bfloat16"),
        ("M2w", H2 + V, "bfloat16"), ("X", XE, "float32"), ("L1", 512, "uint16"), ("LC", 512, "uint16"), ("L2", 512, "uint16"),
        ("LG", 128, "uint16"), ("GL", 512, "float16"), ("PL", 512, "float32"), ("PO", 128, "float32"), ("FL", 128, "float16"),
        ("NCT", 512, "bfloat16"), ("CO", 128, "bfloat16"), ("NI", 64, "int32"), ("IX", 64, "int32"),
        ("CA", 64, "int32"), ("ma", 128, "float32"), ("mb", 128, "float32"), ("GA", 8192, "bfloat16"), ("GB", 8192, "bfloat16"),
        ("GH", 8192, "float16"), ("PR", 8192, "float32"), ("PRS", V, "float32"), ("DS", V, "bfloat16"), ("DB", V, "bfloat16"),
        ("ON", 128, "bfloat16"), ("ZZ", 128, "bfloat16"), ("Id", 128, "bfloat16"), ("Idh", 128, "float16"), ("PM", 128, "bfloat16"),
        ("PMh", 128, "float16"), ("TT", 512, "float16"), ("wA", 8, "float32"), ("WC01", 64, "float32"),
        ("WC02", 64, "float32"), ("WC1", 72, "float32"), ("WC2", 72, "float32"), ("WO1", 64, "bfloat16"), ("WO2", 64, "bfloat16"),
        ("WB", 40, "bfloat16"), ("WE", 40, "bfloat16"), ("WN", 32, "bfloat16"), ("ZB", 144, "bfloat16"), ("ZX", 144, "float16"),
        ("ZM", 144, "bfloat16"), ("RZ", 240, "float16"), ("Rep", 1024, "float16"), ("RS", 256, "bfloat16"), ("ci", 8, "int32"),
        ("cf", 40, "float32"), ("EV", 128, "float32"), ("MS", 512, "float32"), ("NF", 512, "bfloat16"), ("WD", 512, "float32"),
        ("MV", 512, "float32"), ("r8", 128, "float32"), ("cl", 128, "bfloat16"), ("XD", 256, "float16"), ("XT", 768, "float16"),
        ("XF", 384, "float16"), ("GO", 128, "float32"), ("Dh", 128, "bfloat16"), ("Dl", 128, "bfloat16"), ("PMq", 128, "float16"),
        ("PMp", 128, "float16"), ("WU", 72, "float32"), ("WS0", 64, "bfloat16"), ("WS", 72, "bfloat16"), ("EG", 128, "bfloat16")):
    SCRATCH[_n] = ("sbuf", [128, _w], _t)
SCRATCH["nbi"] = ("sbuf", [128, 4, 128], "int32")
for _i in range(8):
    SCRATCH["b%d" % _i] = ("psum", [128, 512], "float32")
EX = ["C", "W", "B", "X", "W1", "Wl", "B2", "Bl", "M2"]
SEMAPHORES = ["v", "s", "p", "g"] + [k + e for k in "xl" for e in EX] + ["d%d" % i for i in range(40)]


def make(g, T):
    QO = {"v": g.vector, "s": g.scalar, "p": g.tensor, "y": g.sync, "g": g}
    calls, acc, marks = [], {}, []

    def call(ways, r, w, tok=None, late=0.0, behind=None, first=0.0, group=None, stop=None, move=0.0, picks=False):
        before = {}
        for lst, wr in ((r, False), (w, True)):
            for key, lo, hi in [x[:3] for x in lst]:
                b, part = (key.split("#") + [None])[:2]
                bank = b in SCRATCH and SCRATCH[b][0] == "psum"
                for j, p2, lo2, hi2, w2 in acc.get(b, []):
                    if bank and group and calls[j]["group"] == group:
                        continue
                    meet = (part is None or p2 is None or part == p2) and lo2 < hi and lo < hi2
                    if meet and (w2 or wr):
                        before[j] = 2
                    elif bank and (list(ways) != ["v"] or list(calls[j]["ways"]) != ["v"]):
                        before[j] = max(1, before.get(j, 0))
        i = len(calls)
        for lst, wr in ((w, True), (r, False)):
            for key, lo, hi in [x[:3] for x in lst]:
                b, part = (key.split("#") + [None])[:2]
                if wr and not group:
                    acc[b] = [a for a in acc.get(b, []) if not ((part is None or part == a[1]) and lo <= a[2] and a[3] <= hi)]
                acc.setdefault(b, []).append((i, part, lo, hi, wr))
        calls.append(dict(ways=ways, before=before, tok=tok, late=late, behind=behind, first=first, group=group, stop=stop, move=move,
                          picks=picks))
        return i

    def must_wait(a, qa, c, qc, k):
        return a["tok"] is not None or c["tok"] is not None or qa != qc or (k == 2 and qc != "p")

    def room(spans, t, ns):
        for a, e in spans:
            if t + ns <= a:
                break
            if e > t:
                t = e
        return t

    def sweep(order, links, back):
        busy = {q: [] for q in list(QO) + ["m"]}
        for i in order:
            c = calls[i]
            best = None
            for q, (fn, ns) in (c["ways"] or {None: (None, 0.0)}).items():
                t = 0.0
                for j, k in links[i]:
                    a = calls[j]
                    if must_wait(c, q, a, a["q"], k) if back else must_wait(a, a["q"], c, q, k):
                        t = max(t, a["end"] + (HOP if q == a["q"] else PLAN["cross"] if (a["q"] if back else q) else 0.0))
                    else:
                        t = max(t, a["end"])
                t += c["late"] + c["move"] if back else 0.0
                t = room(busy.get(q, []), t, ns)
                worth = t + ns * (PLAN["dear"] if q == "v" else 1.0)
                if best is None or worth < best[3]:
                    best = (t + ns, q, t, worth)
            c["q"], c["at"], c["end"] = best[1], best[2], best[0]
            if c["move"] and not back:
                t = room(busy["m"], best[2] + 0.7 * c["late"], c["move"])
                busy["m"].append((t, t + c["move"]))
                busy["m"].sort()
                c["end"] = t + c["move"] + 0.3 * c["late"]
            elif not back:
                c["end"] += c["late"]
            if best[1]:
                busy[best[1]].append((best[2], best[0]))
                busy[best[1]].sort()
        return max(c["end"] for c in calls)

    def place():
        n = len(calls)
        before = [list(c["before"].items()) + ([(c["behind"], 1)] if c["behind"] is not None else []) for c in calls]
        after = [[] for c in calls]
        way = [0.0] * n
        for i in range(n - 1, -1, -1):
            c = calls[i]
            way[i] += c["late"] + c["move"] + min([x[1] for x in c["ways"].values()] or [0.0])
            for j, k in before[i]:
                after[j].append((i, k))
                one = k == 1 and list(calls[j]["ways"]) == list(c["ways"]) or list(calls[j]["ways"]) == list(c["ways"]) == ["p"]
                way[j] = max(way[j], way[i] + (1.0 if one else HOP))
        if PLAN["flow"] and "order" not in FOUND:
            way = [-PLAN["step"] * i for i in range(n)]
            for i in range(marks[0] - 1, -1, -1):
                way[i] = max([way[j] for j, k in after[i]] or [0.0]) + PLAN["soon"]
            flow(way, before, after)
            FOUND["order"], FOUND["time"] = mend(before, after)
        if "order" not in FOUND:
            for c in calls:
                if c["move"] and "g" in c["ways"]:
                    c["late"], c["move"] = c["late"] * PLAN["wary"], c["move"] * PLAN["wary"]
            best, rng = None, np.random.default_rng(PLAN["seed"])
            for turn in range(PLAN["turns"] + PLAN["tries"]):
                if turn >= PLAN["turns"]:
                    way = list(best[2] + PLAN["shake"] * rng.random() * rng.standard_normal(n))
                order = ready(sorted(range(n), key=lambda x: (-way[x] - calls[x]["first"], x)), before)
                sweep(order, before, False)
                t = sum(replay(before, *x) / x[0] for x in PLAN["cases"])
                if best is None or t < best[0]:
                    best = (t, order, np.array(way))
                if turn < PLAN["turns"]:
                    sweep(ready(sorted(range(n), key=lambda x: (-calls[x]["end"], -x)), after), after, True)
                    way = [c["end"] for c in calls]
            sweep(best[1], before, False)
            for c in calls:
                if c["move"] and "g" in c["ways"]:
                    c["late"], c["move"] = c["late"] / PLAN["wary"], c["move"] / PLAN["wary"]
            FOUND["order"], FOUND["time"] = mend(before, after)
        for k, (i, q) in enumerate(FOUND["order"]):
            calls[i]["q"], calls[i]["at"] = q, float(k)

    def mend(before, after):
        n, names = len(calls), list(QO) + [None]
        rng = np.random.default_rng(PLAN["seed"])
        seq = sorted(range(n), key=lambda x: (calls[x]["at"], x))
        qs = [names.index(c["q"]) for c in calls]
        tok = [c["tok"] is not None for c in calls]
        pre = [[(j, tok[j] or tok[i], k == 2) for j, k in before[i]] for i in range(n)]
        late, move = [c["late"] for c in calls], [c["move"] for c in calls]
        cost = [[[c["ways"][q][1] * (1.0 if c["tok"] else slow[q]) * (picks if c["picks"] else 1.0) if q in c["ways"] else 0.0 for q in names]
                 for c in calls] for whole, slow, picks, wake, near, far in PLAN["cases"]]

        def times(seq, qs, case, a, old):
            wake, near, far = PLAN["cases"][case][3:]
            ns, a = cost[case], a // 32
            end, why, marks = list(old[1]), list(old[2]), old[3][:a + 1]
            free, last = list(marks[a][0]), list(marks[a][1])
            for k in range(32 * a, n):
                if k % 32 == 0 and k > 32 * a:
                    marks.append((list(free), list(last)))
                i = seq[k]
                q = qs[i]
                t = free[q] if q < 5 else 0.0
                w = last[q]
                for j, dma, read in pre[i]:
                    e = end[j]
                    if e + wake > t:
                        if q < 5:
                            if qs[j] != q:
                                e += wake
                            elif dma or (read and q != 2):
                                e += wake * 0.45
                        if e > t:
                            t, w = e, j
                why[i], last[q] = w, i
                free[q] = e = t + ns[i][q]
                if move[i]:
                    lag = far if q == 4 else near
                    free[6] = max(free[6], t + 0.7 * lag * late[i]) + lag * move[i]
                    end[i] = free[6] + 0.3 * lag * late[i]
                else:
                    end[i] = e + late[i]
            return max(end), end, why, marks

        def judge(seq, qs, a, old):
            xs = [times(seq, qs, k, a, old[k]) for k in range(len(cost))]
            return sum((x[0] + PLAN["pull_in"] * sum(x[1]) / n) / PLAN["cases"][k][0] for k, x in enumerate(xs)), xs

        def ahead(seq, a, b):
            i, p = seq[b], seq[a]
            need = {i}
            for x in reversed(seq[a:b + 1]):
                if x in need:
                    need.update(j for j, d, r in pre[x])
            if p in need or calls[p]["first"] > 1e8:
                return None
            mid = seq[a:b + 1]
            return seq[:a] + [x for x in mid if x in need] + [x for x in mid if x not in need] + seq[b + 1:]

        now, xs = judge(seq, qs, 0, [(0.0, [0.0] * n, [-1] * n, [([0.0] * 7, [-1] * 7)])] * len(cost))
        best = (now, seq, qs)
        for turn in range(PLAN["mend"]):
            t, end, why, marks = xs[int(rng.integers(len(xs)))]
            i, chain = end.index(t), []
            while i >= 0:
                chain.append(i)
                i = why[i]
            i = chain[int(rng.integers(len(chain)))] if rng.random() > PLAN["roam"] else int(rng.integers(n))
            s2, q2, a, p = seq, qs, seq.index(i), why[i]
            if len(calls[i]["ways"]) > 1 and rng.random() < 0.4:
                q2 = list(qs)
                q2[i] = 1 - qs[i]
                near = [k for k in range(max(0, a - 40), min(n, a + 40)) if qs[seq[k]] == q2[i] and len(calls[seq[k]]["ways"]) > 1]
                if near and rng.random() < 0.5:
                    k = near[int(rng.integers(len(near)))]
                    q2[seq[k]], a = qs[i], min(a, k)
            elif p >= 0 and qs[p] == qs[i] and all(j != p for j, d, r in pre[i]) and rng.random() < 0.8:
                while rng.random() < 0.4 and why[p] >= 0 and qs[why[p]] == qs[i]:
                    p = why[p]
                a, b = seq.index(p), a
                s2 = ahead(seq, a, b)
            else:
                nxt = [k for k in range(a + 1, min(n, a + 80)) if qs[seq[k]] == qs[i]][:8]
                s2 = ahead(seq, a, nxt[int(rng.integers(len(nxt)))]) if nxt else None
            if s2 is None:
                continue
            t2, x2 = judge(s2, q2, a, xs)
            if t2 < now + PLAN["heat"] * (1 - turn / PLAN["mend"]) * -np.log(rng.random()):
                seq, qs, now, xs = s2, q2, t2, x2
                if now < best[0]:
                    best = (now, seq, qs)
        xs = judge(best[1], best[2], 0, xs)[1]
        return [(i, names[best[2][i]]) for i in best[1]], sum(x[0] / PLAN["cases"][k][0] for k, x in enumerate(xs))

    def behind(before, after, placed):
        n = len(calls)
        way, nxt = [0.0] * n, {}
        for i in sorted(range(n), key=lambda x: (-calls[x]["at"], -x)) if placed else range(n - 1, -1, -1):
            c = calls[i]
            q = c["q"] if placed else min(c["ways"], key=lambda x: c["ways"][x][1]) if c["ways"] else None
            ns, t = c["ways"][q][1] if q else 0.0, 0.0
            for j, k in after[i]:
                d = calls[j]
                q2 = d["q"] if placed else q if q in d["ways"] else list(d["ways"] or [None])[0]
                t = max(t, way[j] + ((HOP if q == q2 else PLAN["cross"]) if q2 and must_wait(c, q, d, q2, k) else 0.0))
            way[i] = ns + max(t + c["late"] + c["move"], way[nxt[q]] if q in nxt else 0.0)
            if placed and q:
                nxt[q] = i
        return way

    def flow(way, before, after):
        left = [len(b) for b in before]
        free = {q: 0.0 for q in list(QO) + ["m"]}
        open_ = {q: {} for q in QO}

        def offer(i):
            c = calls[i]
            for q in c["ways"] or [None]:
                t = 0.0
                for j, k in before[i]:
                    a = calls[j]
                    t = max(t, a["end"] + ((HOP if q == a["q"] else PLAN["cross"]) if q and must_wait(a, a["q"], c, q, k) else 0.0))
                if q:
                    open_[q][i] = t
                else:
                    c["q"], c["at"], c["end"] = None, t, t
                    done(i)

        def done(i):
            for j, k in after[i]:
                left[j] -= 1
                if not left[j]:
                    offer(j)

        for i in [i for i, x in enumerate(left) if not x]:
            offer(i)
        while any(open_.values()):
            picks = []
            for q, o in open_.items():
                if o:
                    t0 = free[q]
                    i = max(o, key=lambda x: (way[x] + calls[x]["first"] - PLAN["idle"] * max(0.0, o[x] - t0)
                                              - (PLAN["spare"] if q == "v" and len(calls[x]["ways"]) > 1 else 0.0), -x))
                    picks.append((max(t0, o[i]) + (1.0 if q == "v" else 0.0), q, i))
            t, q, i = min(picks)
            c = calls[i]
            t = max(free[q], open_[q][i])
            for x in c["ways"]:
                del open_[x][i]
            free[q] = t + c["ways"][q][1]
            c["q"], c["at"], c["end"] = q, t, free[q] + c["late"]
            if c["move"]:
                free["m"] = max(free["m"], t + 0.7 * c["late"]) + c["move"]
                c["end"] = free["m"] + 0.3 * c["late"]
            done(i)

    def replay(before, whole, slow, picks, wake, near, far):
        free, end = {}, {}
        for i in sorted(range(len(calls)), key=lambda x: (calls[x]["at"], x)):
            c = calls[i]
            q = c["q"]
            t = t0 = free.get(q, 0.0) if q else 0.0
            for j, k in before[i]:
                hop = must_wait(calls[j], calls[j]["q"], c, q, k) and q
                t = max(t, end[j] + ((wake * 0.45 if q == calls[j]["q"] else wake) if hop else 0.0))
            ns = c["ways"][q][1] * (slow[q] if c["tok"] is None else 1.0) * (picks if c["picks"] else 1.0) if q else 0.0
            free[q] = t + ns
            if c["move"]:
                lag = far if q == "g" else near
                free["m"] = max(free.get("m", 0.0), t + 0.7 * lag * c["late"]) + lag * c["move"]
                end[i] = free["m"] + 0.3 * lag * c["late"]
            else:
                end[i] = t + ns + c["late"]
        return max(end.values())

    def ready(order, links):
        seen, out = set(), []
        for i in order:
            todo = [i]
            while todo:
                j = todo[-1]
                left = [k for k, x in links[j] if k not in seen]
                if left:
                    todo.extend(left)
                else:
                    todo.pop()
                    if j not in seen:
                        seen.add(j)
                        out.append(j)
        return out

    def issue(ends):
        place()
        last = {}
        for c in calls:
            if c["group"] and (c["group"] not in last or c["at"] > last[c["group"]]["at"]):
                last[c["group"]] = c
        for c in last.values():
            c["stop"][0] = True
        cnt = {"v": 0, "s": 0, "p": 0, "g": 0}
        known = {q: {} for q in QO}
        clk = {}
        for i in sorted(range(len(calls)), key=lambda x: (calls[x]["at"], x)):
            c = calls[i]
            q = c["q"]
            if q is None:
                c["done"] = c["tok"]
                clk[c["tok"]] = {c["tok"][0]: c["tok"][1]}
                continue
            k, todo = known[q], {}
            for j, kind in c["before"].items():
                ch, m = calls[j]["done"]
                if must_wait(calls[j], calls[j]["q"], c, q, kind) and k.get(ch, 0) < m:
                    todo[ch] = max(m, todo.get(ch, 0))
            items = sorted(todo.items())
            for ch, m in items:
                if any(c2 != ch and clk[(c2, m2)].get(ch, 0) >= m for c2, m2 in items):
                    continue
                QO[q].wait_ge(T.sem[ch], m)
                for c3, m3 in clk[(ch, m)].items():
                    k[c3] = max(m3, k.get(c3, 0))
            x = c["ways"][q][0](QO[q])
            if c["tok"] is None:
                for y in x if q == "p" else [x]:
                    cnt[q] += 1
                    y.then_inc(T.sem[q], 1)
                c["done"] = (q, cnt[q])
            else:
                c["done"] = c["tok"]
            clk[c["done"]] = dict(k)
            clk[c["done"]][c["done"][0]] = c["done"][1]
        for ch, m in list(cnt.items()) + ends:
            (g.sync if ch[0] == "d" else g).wait_ge(T.sem[ch], m)

    return call, issue, lambda: marks.append(len(calls))


def rank_program(g, core, T, topo):
    rank = T.rank_of(core)
    if rank is None:
        return
    call, issue, mark = make(g, T)
    own = V * rank
    others = [c for c in T.cores if c != core]
    R, ALL, CH = range(4), range(16), PLAN["ch"]
    CYC, PE, PICK = 0.83 * PLAN["slow"], 0.42 * PLAN["slow"], PLAN["pick"]
    ends = []

    def at(b, lo, hi, step=1, part=None, rows=128):
        return (b if part is None else "%s#%d" % (b, part), lo, hi, T[b][0:rows, lo:hi:step], b, len(range(lo, hi, step)))

    def kind(x):
        return SCRATCH[x[4]][2] if SCRATCH[x[4]][0] == "sbuf" else "psum"

    def vec(n, *xs):
        return CYC * max(64, n / 2 if all(kind(x) in ("bfloat16", "float16", "uint16") for x in xs) else n)

    def act(n):
        return CYC * (140 + n)

    def pick(ways, q):
        return {k: x for k, x in ways.items() if k in q}

    def tt(o, a, b, f):
        ns = CYC * max(64, o[5] * (1 if "psum" in (kind(a), kind(b)) else 2))
        call({"v": (lambda e: e.tensor_tensor(o[3], a[3], b[3], f), ns)}, [a, b], [o])

    def ts(o, a, s1, s2, f1, f2=None):
        rd = [a] + [x for x in (s1, s2) if isinstance(x, tuple)]
        x1 = s1[3] if isinstance(s1, tuple) else s1
        x2 = s2[3] if isinstance(s2, tuple) else s2
        if f2 is None:
            call({"v": (lambda e: e.tensor_scalar(o[3], a[3], x1, x2, f1), vec(o[5], o, a))}, rd, [o])
        else:
            call({"v": (lambda e: e.tensor_scalar(o[3], a[3], x1, x2, f1, f2), vec(o[5], o, a))}, rd, [o])

    def scan(o, a, b, f1, f2):
        call({"v": (lambda e: e.tensor_tensor_scan(o[3], a[3], b[3], 0.0, f1, f2), vec(o[5], o, a, b))}, [a, b], [o])

    def cp(q, o, a):
        call(pick({"v": (lambda e: e.tensor_copy(o[3], a[3]), vec(o[5], o, a)),
                   "s": (lambda e: e.activation(o[3], a[3], F.Copy), act(o[5]))}, q), [a], [o])

    def scaled(q, o, a, col, bias=None):
        if bias:
            ways = {"v": (lambda e: e.tensor_scalar(o[3], a[3], col[3], bias[3], A.mult, A.add), vec(o[5], o, a)),
                    "s": (lambda e: e.activation(o[3], a[3], F.Identity, bias=bias[3], scale=col[3]), act(o[5]))}
        else:
            ways = {"v": (lambda e: e.tensor_scalar(o[3], a[3], col[3], None, A.mult), vec(o[5], o, a)),
                    "s": (lambda e: e.activation(o[3], a[3], F.Identity, scale=col[3]), act(o[5]))}
        call(pick(ways, q), [a, col] + ([bias] if bias else []), [o])

    opened, run = {}, []

    def mm(o, lt, rh, start, stop=None, r=(), w=(), more=False):
        ns = PE * max(min(64, lt[5]), rh[5]) * (4 if kind(lt) == "float32" else 1)
        if start:
            opened[o[4]] = opened.get(o[4], 0) + 1
        flag = [bool(stop)]
        run.append((lambda e: e.matmul(o[3], lt[3], rh[3], start, flag[0]), ns, [lt, rh] + list(r), [o] + list(w),
                    None if start or stop is not None else (o[4], opened[o[4]]), flag))
        if not more:
            xs = list(run)
            run.clear()
            call({"p": (lambda e: [x[0](e) for x in xs], sum(x[1] for x in xs))}, sum([x[2] for x in xs], []), sum([x[3] for x in xs], []),
                 group=xs[-1][4], stop=flag)

    def fill(o, x):
        call({"v": (lambda e: e.memset(o[3], x), vec(o[5], o))}, [], [o])

    def dma(q, out, in_, r, w, size, first=0.0):
        sem = "d%d" % len([x for x in ends if x[0][0] == "d"])
        ends.append((sem, 16))
        call({q: (lambda e: e.dma_start(out, in_).then_inc(T.sem[sem], 16), 60.0)}, r, w, (sem, 16), PLAN["near"], None, first,
             move=size / PLAN["lrate"])

    def gather(q, out, lo, hi, win, w0, w1, offs):
        o, wn, of = at(out, lo, hi), at(win, w0, w1), at(offs, lo // 16, hi // 16)
        ns = CYC * PICK * (hi - lo)
        call(pick({"v": (lambda e: e.tensor_copy(o[3], wn[3].indirect(of[3])), 50 + ns),
                   "s": (lambda e: e.activation(o[3], wn[3].indirect(of[3]), F.Copy), 65 + ns)}, q), [wn, of], [o], picks=True,
             first=PLAN["stag"] * (8192 - lo) / 8192)

    def gather_times(o, wn, of, c):
        call({"v": (lambda e: e.tensor_tensor(o[3], wn[3].indirect(of[3]), c[3], A.mult), 50 + CYC * PICK * o[5])}, [wn, of, c], [o],
             picks=True)

    def g_sel(o, i, pat, c, base, cm):
        call({"g": (lambda e: e.affine_select(o[3], i[3], pat, c, 0.0, base, cm), 170 + 2 * CYC * o[5])}, [i], [o])

    def g_iota(o, pat, base, cm, late=0.0):
        call({"g": (lambda e: e.iota(o[3], pat, base, cm, allow_small_or_imprecise_dtypes=True), 130 + 2 * CYC * o[5])}, [], [o], None, late)

    def g_zero(b, lo, hi):
        for a in range(lo, hi, 256):
            g_iota(at(b, a, a + 256), [[0, 256]], 0, 0, PLAN["margin"])

    def cls(d, k, b0, b1):
        return ("%s#%d" % (d, k), 128 * b0, 128 * b1, T[d][:, 128 * b0 + k:128 * b1:16], d, 8 * (b1 - b0))

    def gcol(b, s):
        b0, b1 = [c for c in CH if c[0] <= b < c[1]][0]
        return 512 * b0 + 128 * (s * (b1 - b0) + b - b0)

    Id, Idh, E8 = at("Id", 0, 128), at("Idh", 0, 128), at("EG", 0, 128, 16)

    loads = [("Qw", T.qu, 512, x) for x in PLAN["qdma"]]
    for b0, b1 in PLAN["pload"]:
        loads.insert([i for i, x in enumerate(loads) if x[0] == "Qw" and x[3][1] > b0][0], ("Pb", T.po, 256, (b0, b1)))
    loads.insert(PLAN["nbat"], None)
    for i, x in enumerate(loads):
        q = PLAN["lq"][i % len(PLAN["lq"])]
        if x:
            a, e = 128 * x[3][0], 128 * x[3][1]
            dma(q, T[x[0]][:, a:e], x[1][:, a:e], [], [(x[0], a, e)], x[2] * (e - a), 1e9 - 1e6 * i)
        else:
            dma(q, T.nbi[:], T.nb[:], [], [("nbi", 0, 512)], 128 * 2048, 1e9 - 1e6 * i)

    msk = topo.mask(core, others[0])
    for c in others[1:]:
        msk &= topo.mask(core, c)
    ne = bin(msk).count("1")
    sent = []

    def share(b, name, lo, w, to=None, pitch=None, after=(), off=0):
        to, pitch = to or b, pitch or w
        ends.extend([("l" + name, ne), ("x" + name, 3 * ne)])
        ids = [DstId(rid=topo.addr(c)[0], pnc=topo.addr(c)[1]) for c in others]
        dst = [T[to][:, pitch * k + off:pitch * k + off + w] for k in [(rank - T.rank_of(c) - 1) % N for c in others]]
        tr = RemoteDMATransfer(dst_ids=ids, dma_engine_mask=msk, remote_sem=T.sem["x" + name], srcs=[T[b][:, lo:lo + w]], dsts=dst)
        i = call({"g": (lambda e: e.remote_dma_fused([tr], local_sem=T.sem["l" + name]), 300.0)}, [(b, lo, lo + w)] + list(after),
                 [("sent" + name, 0, 1)], ("l" + name, ne), PLAN["far"] + (0.0 if sent else PLAN["once"]), first=PLAN["early"].get(name, 0.0), move=3 * 128 * w * 2 / PLAN["rate"])
        sent.append(name)
        call({}, [], [(to, pitch * k + off, pitch * k + off + w) for k in range(3)], ("x" + name, 3 * ne), 0.0, i)

    def ci(k):
        return at("ci", k, k + 1)

    def cf(k):
        return at("cf", k, k + 1)

    ROW, LOW, UP, W6, WCOST, CODE1, CODE2, NCODE1, NCODE2, RA, RX, RQ, BEST, NBEST, STEP, NUM, ENUM, GOAL, SW, SB, RB, SINK, ALONE = [cf(k) for k in range(23)]
    fill(at("ON", 0, 128), 1.0)
    call({"g": (lambda e: e.iota(ci(0)[3], [[0, 1]], 0, 1), 130.0)}, [], [ci(0)])
    g_sel(Id, at("ON", 0, 128), [[-1, 128]], A.is_equal, 0, 1)
    g_sel(at("EG", 0, 128), at("ON", 0, 128), [[-16, 8], [0, 16]], A.is_ge, 0, 1)
    g_sel(at("EG", 0, 128), at("EG", 0, 128), [[16, 8], [0, 16]], A.is_ge, 15, -1)
    for b in ("WC01", "WC02", "WC1", "WC2", "WO1", "WO2", "WB", "WE", "ZB", "ZX", "ZM", "RZ", "RS"):
        fill(at(b, 0, T[b].shape[1]), 0.0)
    fill(at("RS", 0, 256, 4), 1e9)
    fill(at("NF", 0, 512, 4, 0), 0.0)
    fill(at("XT", 0, 128), 0.0)
    ts(ci(1), ci(0), 15, None, A.bitwise_and)
    ts(ci(2), ci(1), 2, None, A.logical_shift_right)
    ts(ci(3), ci(1), 3, None, A.bitwise_and)
    cp("v", ROW, ci(1))
    tt(LOW, ci(3), ci(2), A.is_lt)
    tt(cf(24), ci(3), ci(2), A.is_gt)
    tt(cf(25), ci(3), ci(2), A.is_equal)
    ts(UP, LOW, -1.0, 1.0, A.mult, A.add)
    ts(cf(26), ci(3), 0.0, LOW, A.is_equal, A.mult)
    ts(W6, cf(24), 2.0, cf(25), A.mult, A.add)
    tt(WCOST, W6, cf(26), A.add)
    tt(CODE1, LOW, cf(26), A.subtract)
    ts(cf(27), ROW, 14.0, 3.0, A.is_equal, A.mult)
    tt(CODE2, CODE1, cf(27), A.add)
    ts(NCODE1, CODE1, -1.0, None, A.mult)
    ts(NCODE2, CODE2, -1.0, None, A.mult)
    ts(cf(28), ROW, 8.0, None, A.is_equal)
    ts(cf(34), ROW, 12.0, None, A.is_equal)
    ts(RA, ROW, 4.0, cf(34), A.is_equal, A.subtract)
    tt(RB, RA, RA, A.mult)
    ts(RX, cf(28), FAR / LIFT, RA, A.mult, A.add)
    ts(cf(36), UP, cf(28), 3 * LIFT, A.add, A.mult)
    ts(SINK, RB, -4 * LIFT, cf(36), A.mult, A.subtract)
    ts(RQ, SINK, 0.0, 4 * LIFT, A.is_lt, A.mult)
    ts(ALONE, RB, 60 * LIFT, -64 * LIFT, A.mult, A.add)
    ts(cf(35), cf(28), -1.0, None, A.mult)
    ts(cf(29), ROW, 12.0, None, A.is_lt)
    ts(BEST, ci(3), 0.0, cf(29), A.is_equal, A.mult)
    ts(NBEST, BEST, -1.0, None, A.mult)
    ts(cf(30), ROW, 2.0, None, A.is_equal)
    ts(STEP, ROW, 12.0, cf(30), A.is_equal, A.add)
    ts(NUM, ci(3), 2.0, cf(30), A.is_equal, A.subtract)
    ts(ENUM, NUM, EPS, None, A.mult)
    tt(cf(31), BEST, cf(28), A.subtract)
    tt(GOAL, cf(31), NUM, A.add)
    ts(SW, ROW, 4.0, NONE, A.is_equal, A.mult)
    ts(SB, ROW, 0.0, NONE, A.is_equal, A.mult)
    cp("vs", at("wA", 0, 8), E8)
    cp("vs", Idh, Id)
    for o, col in ((at("WC01", 0, 64, 8, 0), WCOST), (at("WC01", 1, 64, 8, 1), CODE1), (at("WC1", 6, 70, 8, 0), WCOST),
                   (at("WC1", 7, 71, 8, 1), CODE1), (at("WC1", 5, 69, 8, 2), NCODE1), (at("WO1", 7, 64, 8), NCODE1),
                   (at("WC02", 0, 64, 8, 0), WCOST), (at("WC02", 1, 64, 8, 1), CODE2), (at("WC2", 6, 70, 8, 0), WCOST),
                   (at("WC2", 7, 71, 8, 1), CODE2), (at("WC2", 5, 69, 8, 2), NCODE2), (at("WO2", 7, 64, 8), NCODE2),
                   (at("WB", 3, 35, 4), BEST), (at("WE", 3, 35, 4), ENUM), (at("ZB", 15, 143, 16), STEP), (at("ZX", 15, 143, 16), RX),
                   (at("ZM", 15, 143, 16), GOAL), (at("RZ", 112, 128, 2, 0), RQ), (at("RZ", 113, 128, 2, 1), RA)):
        scaled("vs", o, E8, col)
    scaled("vs", at("PM", 0, 128), Id, UP)
    g_iota(at("GO", 0, 128), [[1, 128]], 0, -1)
    tt(cf(32), ci(3), ci(2), A.subtract)
    ts(cf(33), cf(32), 3.0, None, A.mult)
    ts(at("r8", 0, 128), at("GO", 0, 128), cf(33), cf(24), A.is_equal, A.mult)
    tt(at("PMh", 0, 128), at("PM", 0, 128), at("r8", 0, 128), A.add)
    cp("vs", at("PMq", 0, 128), at("PM", 0, 128))
    scaled("vs", at("PMp", 0, 128), at("EG", 0, 128), cf(35))
    tt(at("PMp", 0, 128), at("PMp", 0, 128), at("PMh", 0, 128), A.add)
    if PLAN["fix"] == "p":
        for b in ("WU", "WS0", "WS"):
            fill(at(b, 0, T[b].shape[1]), 0.0)
        for o, col in ((at("WU", 6, 70, 8), W6), (at("WS0", 0, 64, 8, 0), cf(26)), (at("WS0", 1, 64, 8, 1), CODE2), (at("WS", 6, 70, 8, 0), cf(26)),
                       (at("WS", 7, 71, 8, 1), CODE2), (at("WS", 5, 69, 8, 2), NCODE2)):
            scaled("vs", o, E8, col)
    for k in range(8):
        mm(at(PLAN["rep"][k // 4], 128 * (k % 4), 128 * (k % 4) + 128), at("RZ", 112 - 16 * k, 240 - 16 * k), Idh, True, True, more=k % 4 < 3)
    for k in (0, 1):
        cp("vs", at("Rep", 512 * k, 512 * k + 512), at(PLAN["rep"][k], 0, 512))
    scaled("vs", at("WN", 0, 32), at("EG", 0, 128, 4), NBEST)
    scaled("vs", at("W1", H2 + V, H2 + V + 16), at("ON", 0, 16), SW)
    scaled("vs", at("B2w", H2 + V, H2 + V + 16), at("ON", 0, 16), SB)
    g_iota(at("EV", 0, 128), [[128, 16], [0, 8]], own, 1)
    ts(at("EV", 0, 128), at("EV", 0, 128), EPS, None, A.mult)
    for d, ks, r in (("DS", (9, 13, 14), NC), ("DB", (6, 10, 14), V)):
        if d == "DS":
            fill(at(d, 0, V), 0.0)
        else:
            for a in range(0, V, 512):
                o, x = at(d, a, a + 512), at("Pb", a, a + 512)
                call({"v": (lambda e, o=o: e.memset(o[3], 0.0), vec(512, o)),
                      "s": (lambda e, o=o, x=x: e.activation(o[3], x[3], F.Copy, scale=0.0), act(512))}, [x], [o])
        g_iota(cls(d, ks[0], 0, 16), [[0, 128]], 0, 1)
        g_iota(cls(d, ks[1], 0, 16), [[128, 16], [0, 8]], 0, 0)
        g_iota(cls(d, ks[2], 0, 16), [[0, 128]], r * rank, 0)
    for (b0, b1), (c0, c1) in zip(CH[::2], CH[1::2]):
        g_iota(at("NCT", 32 * b0, 32 * c1), [[-128 * (b1 - b0), 2], [0, 4], [-16, 8 * (b1 - b0)]], -128 * b0, 0)
    g_iota(at("CO", 0, 128), [[16, 128]], 0, 0)

    def slots(b0, b1):
        return ("nbi", 0, 512, T.nbi[:, :, 8 * b0:8 * b1], "nbi", 32 * (b1 - b0))

    ts(at("NI", 0, 64), slots(0, 2), float(V * (3 - rank)), None, A.add)
    for b0, b1 in CH[1:]:
        ts(at("GL", 32 * b0, 32 * b1), slots(b0, b1), float(-own), None, A.add)
    ix, ca = at("IX", 0, 64), at("CA", 0, 64)
    ts(ix, at("NI", 0, 64), 11, 3, A.logical_shift_right, A.bitwise_and)
    ts(ca, at("NI", 0, 64), V - 1, None, A.bitwise_and)
    ts(at("ma", 0, 64), ix, 256.0, None, A.mult)
    ts(at("ma", 64, 128), ix, 512.0, 512.0, A.mult, A.add)
    ts(at("mb", 64, 128), ix, float(3 - rank), float(-V), A.is_ge, A.mult)
    tt(at("PL", 0, 64), at("ma", 0, 64), ca, A.add)
    tt(at("ma", 64, 128), at("ma", 64, 128), at("mb", 64, 128), A.add)
    cp("v", at("L1", 0, 64), at("PL", 0, 64))
    cp("v", at("L1", 64, 128), at("GL", 64, 128))
    ts(at("L1", 128, 512), at("GL", 128, 512), float(-NB), None, A.add)
    tt(at("GL", 0, 64), at("ma", 64, 128), ca, A.add)
    cp("vs", at("PL", 64, 512), at("L1", 64, 512))
    ts(at("FL", 0, 64), ca, float(NB), float(V), A.is_ge, A.mult)
    ts(at("FL", 64, 128), at("GL", 64, 128), float(NB), float(V), A.is_ge, A.mult)
    ts(at("mb", 0, 64), ix, 3.0, float(XH - XB + H1), A.is_lt, A.mult)
    ts(at("PO", 0, 128), at("FL", 0, 128), -1.0, float(XB - H1), A.mult, A.add)
    tt(at("PO", 0, 64), at("PO", 0, 64), at("mb", 0, 64), A.add)

    def s_sum(bank, b0, b1):
        for b in range(b0, b1):
            mm(at(bank, 8 * b, 8 * b + 8), at("PRS", 128 * b, 128 * b + 128), at("wA", 0, 8), True, True, more=b % 2 == 0)

    def pieces(d, ks, src, b0, b1):
        hi, mid, lo = [cls(d, k, b0, b1) for k in ks]
        r8 = at("r8", 8 * b0, 8 * b1)
        ts(r8, src, R8, -R8, A.add, A.add)
        cp("vs" if kind(src) != "psum" else "v", hi, src)
        tt(lo, src, r8, A.subtract)
        tt(mid, r8, hi, A.subtract)

    def spread(d, win, base, b0, b1, bank, with_p=False):
        if with_p:
            mm(at(bank, 0, 128 * (b1 - b0)), at("PM", 0, 128), at("Pb", 128 * b0, 128 * b1), True, False)
        for b in range(b0, b1):
            mm(at(bank, 128 * (b - b0), 128 * (b - b0) + 128), at(d, 128 * b, 128 * b + 128), Id, not with_p, None if with_p else True,
               more=b < b1 - 1)
        cp("vs", at(win, base + 128 * b0, base + 128 * b1), at(bank, 0, 128 * (b1 - b0)))

    def c_bank(b0, b1):
        return at("b%d" % (b0 // 4), 128 * (b0 % 4), 128 * (b0 % 4 + b1 - b0))

    def blocks(xs):
        return min(CH[x][0] for x in xs), max(CH[x][1] for x in xs)

    def shares(b0, b1, banks):
        n = -(-(b1 - b0) // len(banks))
        return [(b0 + n * i, min(b1, b0 + n * i + n), bank) for i, bank in enumerate(banks)]

    def by_bank(b0, b1):
        return [(max(b0, k), min(b1, k + 4)) for k in range(0, 16, 4) if max(b0, k) < min(b1, k + 4)]

    def plain(fused, b0, b1):
        return any(c0 < b1 and b0 < c1 and len(fused.get(x, ())) < 4 for x, (c0, c1) in enumerate(CH))

    SK = [4, 8, 12]
    mark()
    for b0, b1 in PLAN["pload"]:
        for c0, c1 in by_bank(b0, b1):
            mm(c_bank(c0, c1), Id, at("Pb", 128 * c0, 128 * c1), True, True)
    for b0, b1 in PLAN["qload"]:
        a, e = 128 * b0, 128 * b1
        tt(at("PRS", a, e), at("Qw", a, e), c_bank(b0, b1), A.mult)
        scaled("s", at("Ch", H1 + a, H1 + e), at("Qw", a, e), UP, LOW)
        if b0 == 0 and PLAN["opens"] == "C":
            share("Ch", "C", H1, NB)
    for b0, b1, bank, back in PLAN["sum0"]:
        s_sum(bank, b0, b1)
        pieces("DS", SK, at(bank, 8 * b0, 8 * b1), b0, b1)
        for c0, c1, k in shares(b0, b1, back):
            spread("DS", "W", H1, c0, c1, k, True)
        if b0 == 0:
            share("W", "W", H1, NB)
    for b0, b1 in PLAN["qload"]:
        if plain(PLAN["fused1"], b0, b1):
            mm(c_bank(b0, b1), Idh, at("Ch", H1 + 128 * b0, H1 + 128 * b1), True, True)
    if PLAN["opens"] == "W":
        share("Ch", "C", H1, NB, after=[("Qw", 0, V), ("Pb", 0, V), ("sentW", 0, 1)])

    def costs(bank, xs, win, base, window, offs, fused, c, cb, k):
        b0, b1 = blocks(xs)
        for b in range(b0, b1):
            mm(at(bank, 64 * (b - b0), 64 * (b - b0) + 64), at(win, base + 128 * b, base + 128 * b + 128), at("WO" + k, 0, 64), b == b0,
               more=b % 4 < 3 and b0 < b < b1 - 1)
        for x in xs:
            c0, c1 = CH[x]
            for s in R:
                lo, n = gcol(c0, s), 128 * (c1 - c0)
                if s in fused.get(x, ()):
                    gather_times(at("PR", lo, lo + n), at(win, *window(x)), at(offs, lo // 16, (lo + n) // 16), at(c, cb + 128 * c0, cb + 128 * c1))
                else:
                    gather("s", "GA", lo, lo + n, win, *window(x), offs)
                    tt(at("PR", lo, lo + n), at("GA", lo, lo + n), c_bank(c0, c1), A.mult)
            for s in R:
                w = at("WC0" + k, 0, 64) if s == 0 else at("WC" + k, 6 - 2 * s, 70 - 2 * s)
                apart = k == "2" and PLAN["fix"] == "p" and s not in fused.get(x, ())
                for src, w in ((("PR", at("WU", 6 - 2 * s, 70 - 2 * s)), ("GA", at("WS", 6 - 2 * s, 70 - 2 * s) if s else at("WS0", 0, 64)))
                               if apart else (("PR", w),)):
                    for b in range(c0, c1):
                        mm(at(bank, 64 * (b - b0), 64 * (b - b0) + 64), at(src, gcol(b, s), gcol(b, s) + 128), w, False, more=b < c1 - 1)

    def slots_of(out, x, win, w0, w1, offs):
        n, k = 128 * (CH[x][1] - CH[x][0]), PLAN["grain"][x]
        for s in range(0, 4, k):
            gather("vs", out, gcol(CH[x][0], s), gcol(CH[x][0], s) + k * n, win, w0, w1, offs)

    def best_of(bank, b0, b1):
        n = b1 - b0
        scan(at("MS", 32 * b0, 32 * b1), at("RS", 0, 32 * n), at(bank, 0, 64 * n, 2), A.add, A.min)
        pieces("DB", [0, 4, 8], at("MS", 32 * b0 + 3, 32 * b1, 4), b0, b1)

    def choice_of(bank, b0, b1, hi, lo):
        n = b1 - b0
        for s in (1, 2, 3):
            tt(at("NF", 32 * b0 + s, 32 * b1, 4, s), at(bank, 2 * s, 64 * n, 8), at("MS", 32 * b0 + s - 1, 32 * b1, 4), A.is_ge)
        scan(at("WD", 32 * b0, 32 * b1), at("NF", 32 * b0, 32 * b1), at(bank, 1, 64 * n, 2), A.mult, A.add)
        dd = at("WD", 32 * b0 + 3, 32 * b1, 4)
        cp("vs", hi, dd)
        tt(lo, dd, hi, A.subtract)

    def tests(bank, xs, win, base, window, offs):
        b0, b1 = blocks(xs)
        for b in range(b0, b1):
            mm(at(bank, 32 * (b - b0), 32 * (b - b0) + 32), at(win, base + 128 * b, base + 128 * b + 128), at("WN", 0, 32), b == b0,
               w=[("less", b, b + 1)], more=b % 4 < 3 and b0 < b < b1 - 1)
        for x in xs:
            slots_of("GB", x, win, *window(x), offs)
            for s in R:
                for w in ("WB", "WE"):
                    for b in range(*CH[x]):
                        mm(at(bank, 32 * (b - b0), 32 * (b - b0) + 32), at("GB", gcol(b, s), gcol(b, s) + 128), at(w, 3 - s, 35 - s), False,
                           r=[("less", b, b + 1)], more=w == "WB" or b < CH[x][1] - 1)

    def collapses(o, bank, b0, b1):
        n = b1 - b0
        scan(at("MV", 32 * b0, 32 * b1), at("RS", 0, 32 * n), at(bank, 0, 32 * n), A.add, A.min)
        tt(o, at("MV", 32 * b0 + 3, 32 * b1, 4), at("EV", 8 * b0, 8 * b1), A.is_gt)

    def tables(z, src, first, lo, hi, bank, firsts):
        o = at(bank, lo // 16, hi // 16)
        if z in PLAN["turned"] and (hi - lo) % 2048 == 0:
            for a in range(lo, hi, 2048):
                t, x = at(bank, a // 16, a // 16 + 128), at("TT", a // 16, a // 16 + 128)
                for b in ALL:
                    mm(at(bank, a // 16 + b, a // 16 + 128, 16), at(src, first + a + b, first + a + 2048, 16), at(z, 15, 143, 16), True, True,
                       more=b % 8 < 7)
                cp("vs", x, t)
            for i, c in enumerate(firsts):
                c = at(c, lo // 16, hi // 16)
                mm(o, Idh if kind(c) == "float16" else Id, c, i == 0)
            for a in range(lo, hi, 2048):
                mm(at(bank, a // 16, a // 16 + 128), at("TT", a // 16, a // 16 + 128), Idh, False)
            return
        for i, c in enumerate(firsts):
            c = at(c, lo // 16, hi // 16)
            mm(o, Idh if kind(c) == "float16" else Id, c, i == 0)
        for a in range(lo, hi, 1024):
            for b in ALL:
                mm(at(bank, a // 16, a // 16 + 64), at(z, 15 - b, 143 - b), at(src, first + a + b, first + a + 1024, 16), False, more=b % 8 < 7)

    def one(x):
        return ((0, H1, H1 + NB)[min(x, 2)], H1 + V)

    def two(x):
        return (0 if x < 2 else H2, H2 + V + 16)

    for bank, xs, back in PLAN["cost1"]:
        b0, b1 = blocks(xs)
        costs(bank, xs, "W", H1, one, "L1", PLAN["fused1"], "Ch", H1, "1")
        best_of(bank, b0, b1)
        choice_of(bank, b0, b1, cls("DB", 12, b0, b1), cls("DB", 2, b0, b1))
        cp("vs", at("XD", 16 * b0 + 1, 16 * b1, 2, 1), at("WD", 32 * b0 + 3, 32 * b1, 4))
        for c0, c1, k in shares(b0, b1, back):
            spread("DB", "Bw", H1, c0, c1, k)
        if b0 == 0:
            share("Bw", "B", H1, NB)
            if PLAN["opens"] == "B":
                share("Ch", "C", H1, NB, after=[("sentB", 0, 1)])

    def planes(srcs, c0, p1, bank, rows=False):
        n = 128 * len(srcs)
        bank, second = bank if isinstance(bank, tuple) else (bank, None)
        for j in (bank, second) if second else (bank,):
            if j == bank:
                mm(at(j, 0, n), at("PMq", 0, 128), at("Ch", c0, c0 + n), True)
            for i, (b, lo, k, r) in enumerate(srcs):
                mm(at(j, 128 * i, 128 * i + 128), at("Rep", 128 * k, 128 * k + 128, 1, None, r), at(b, lo, lo + 128, 1, None, r),
                   j != bank, None if j == bank else True, more=i < len(srcs) - 1)
        for a, e, p in p1:
            over(at("X", p, p + e - a), at(bank, a, e), SINK)
        if rows:
            g_zero("X", c0, c0 + n)
            dma("y", T.X[4::8, c0:c0 + n], T.X[4::8, p1[0][2]:p1[0][2] + n], [("X", p1[0][2], p1[0][2] + n)], [("X", c0, c0 + n)], 64 * n)
        else:
            over(at("X", c0, c0 + n), at(second or bank, 0, n), ALONE)

    def over(o, a, col):
        call({"v": (lambda e: e.tensor_scalar(o[3], a[3], col[3], 0.0, A.add, A.max), vec(o[5], o, a)),
              "s": (lambda e: e.activation(o[3], a[3], F.Relu, bias=col[3]), act(o[5]))}, [a, col], [o])

    for k, (bank, xs, back, lists, rows) in enumerate(PLAN["test1"]):
        b0, b1 = blocks(xs)
        tests(bank, xs, "Bw", H1, one, "L1")
        c, n = at("XD", 16 * b0, 16 * b1, 2, 0), 16 * (b1 - b0)
        collapses(c, bank, b0, b1)
        mm(at(bank, 0, 128, 1, None, n), at("XD", 16 * b0, 16 * b1), Idh, True, True)
        cp("vs", at("XT", 128 * k, 128 * k + 128, 1, None, n), at(bank, 0, 128, 1, None, n))
        if b0 == 0:
            share("XT", "X", 128 * k, 128, "XF")
        for c0, c1, j in shares(b0, b1, back):
            p1 = [(0, NB, XB), (NB, 128 * c1, XS)] if c0 == 0 else [(0, 128 * (c1 - c0), XS + 128 * c0 - NB)]
            planes([("XT", 128 * k, b - b0, n) for b in range(c0, c1)], H1 + 128 * c0, [p for p in p1 if p[0] < p[1]], j, rows)
        for kk in (12, 2):
            tt(cls("DB", kk, b0, b1), cls("DB", kk, b0, b1), c, A.mult)
        tables("ZB", "GB", 0, 512 * b0, 512 * b1, lists, ["GL", "NCT"])
        for a, e in ((32 * b0, min(128, 32 * b1)), (max(128, 32 * b0), 32 * b1)):
            if a < e:
                t = at(lists, a, e)
                if a < 128:
                    ts(t, t, ROW, None, A.is_equal)
                    tt(t, t, at("PO", a, e), A.mult)
                else:
                    ts(t, t, ROW, float(XS - XR), A.is_equal, A.mult)
                tt(at("LC", a, e), t, at("PL", a, e), A.add)
    planes([("XF", 128 * (i // 2), i % 2, 32) for i in range(4)], 0, [(0, 512, XH)], PLAN["halo"][0])
    planes([("XF", 256, i, 32) for i in range(2)], 512, [(0, 256, XH + 512)], PLAN["halo"][1])

    def around(o, x, n, cap):
        ts(at("ma", 0, n), x, float(NC), float(V), A.is_lt, A.mult)
        tt(at("mb", 0, n), x, at("ma", 0, n), A.add)
        ts(o, at("mb", 0, n), float(-NC), cap, A.add, A.min)

    for xs, sums, back, lists in PLAN["pull"]:
        b0, b1 = blocks(xs)
        for c0, c1 in by_bank(b0, b1):
            mm(c_bank(c0, c1), at("PMh", 0, 128), at("Ch", H1 + 128 * c0, H1 + 128 * c1), True)
        for x in xs:
            slots_of("GH", x, "X", *((0, XE), (H1, XH), (XR, XB))[min(x, 2)], "LC")
            for s in R:
                lo = gcol(CH[x][0], s)
                mm(c_bank(*CH[x]), at("PMp", 0, 128), at("GH", lo, lo + 128 * (CH[x][1] - CH[x][0])), False)
        for c0, c1 in by_bank(b0, b1):
            tt(at("PRS", 128 * c0, 128 * c1), at("Pb", 128 * c0, 128 * c1), c_bank(c0, c1), A.mult)
        s_sum(sums, b0, b1)
        for x in xs:
            if PLAN["fused2"].get(x):
                scaled("s", at("Cf", 128 * CH[x][0], 128 * CH[x][1]), c_bank(*CH[x]), UP, LOW)
        for c0, c1 in by_bank(b0, b1):
            if c0 // 4 not in PLAN["later"]:
                cp(PLAN["out"], at("Qw", 128 * c0, 128 * c1), c_bank(c0, c1))
            if plain(PLAN["fused2"], c0, c1) and PLAN["fix"] != "p":
                scaled(PLAN["fix"], c_bank(c0, c1), c_bank(c0, c1), UP, LOW)
        pieces("DS", SK, at(sums, 8 * b0, 8 * b1), b0, b1)
        for c0, c1, k in shares(b0, b1, back):
            spread("DS", "W1", H2, c0, c1, k, True)
        if b0 >= 4:
            tables("ZX", "GH", 0, 512 * b0, 512 * b1, lists, ["GL"])
            ts(at("L2", 32 * b0, 32 * b1), at(lists, 32 * b0, 32 * b1), float(V), None, A.min)
        else:
            share("W1", "W1" if b0 == 0 else "Wl", H2 + 128 * b0, 128 * (b1 - b0), None, NC, (), 128 * b0)
            tables("ZX", "GH", 0, 512 * b0, 512 * b1, lists, ["GL", "FL"])
            around(at("L2", 32 * b0, 32 * b1), at(lists, 32 * b0, 32 * b1), 32 * (b1 - b0), float(H2 + V))

    for bank, xs, back in PLAN["cost2"]:
        b0, b1 = blocks(xs)
        costs(bank, xs, "W1", H2, two, "L2", PLAN["fused2"], "Cf", 0, "2")
        for c0, c1 in by_bank(b0, b1):
            if c0 // 4 in PLAN["later"]:
                cp(PLAN["out"], at("Qw", 128 * c0, 128 * c1), c_bank(c0, c1))
        best_of(bank, b0, b1)
        choice_of(bank, b0, b1, at("Dh", 8 * b0, 8 * b1), at("Dl", 8 * b0, 8 * b1))
        for c0, c1, k in shares(b0, b1, back):
            spread("DB", "B2w", H2, c0, c1, k)
        if b0 < 4:
            share("B2w", "B2" if b0 == 0 else "Bl", H2 + 128 * b0, 128 * (min(b1, 4) - b0), None, NC, (), 128 * b0)
    for a, e, x in PLAN["stores"]:
        dma("y", T.q1[:, a:e], T.Qw[:, a:e], [("Qw", a, e), ("sent" + x, 0, 1)], [], 512 * (e - a))

    tables("ZB", "B2w", H2, 0, V, "b6", ["CO"])
    ts(at("GO", 0, 16), at("b6", 0, 16), ROW, None, A.add)
    around(at("LG", 0, 16), at("GO", 0, 16), 16, float(H2 + V))
    ts(at("LG", 16, 128), at("b6", 16, 128), ROW, None, A.add)
    for bank, xs, back in PLAN["test2"]:
        b0, b1 = blocks(xs)
        tests(bank, xs, "B2w", H2, two, "L2")
        c = at("cl", 8 * b0, 8 * b1)
        collapses(c, bank, b0, b1)
        for k, d in ((0, "Dh"), (4, "Dl")):
            tt(cls("DB", k, b0, b1), c, at(d, 8 * b0, 8 * b1), A.mult)
        for c0, c1, k in shares(b0, b1, back):
            spread("DB", "M2w", H2, c0, c1, k)
        if b0 == 0:
            share("M2w", "M2", H2, NB, None, NC)

    for lo, hi in PLAN["last"]:
        gather("vs", "GA", lo, hi, "M2w", H2 if lo else 0, H2 + V, "LG")
    for b in [2, 3] + [b for b in ALL if b // 2 != 1]:
        mm(at("b6", 0, 128), at("ZM", 15 - b, 143 - b), at("GA", 128 * b, 128 * b + 128), b == 2, more=b % 2 == 0 and b != 2)
    cp("v", at("GO", 0, 128), at("b6", 0, 128))
    dma("y", T.goal[:], T.GO[:], [("GO", 0, 128)], [], 128 * 512)

    issue(ends)
